import numpy as np, ml_dtypes
CORES = [13,21,141,149]
N = 4
BF = ml_dtypes.bfloat16
H, P, B, T, S = 2048, 1280, 256, 3, 32
BOUND = P + B * (np.arange(T * B) // B)
def parts(rng):
    G = P + T * B
    fe = (256 * (0.6 * rng.random((N, 8, 16, G)) + 0.4 * rng.random((N, 8, 1, G)))).astype(np.int64)
    no = (256 * (0.6 * rng.random((N, 8, 16, H)) + 0.4 * rng.random((N, 8, 1, H)))).astype(np.int64)
    no = np.minimum(no + rng.integers(0, 64, (N, 8, 1, 1)), 255)
    co = rng.integers(0, BOUND, (N, 8, 16, T * B))
    pool = np.argsort(rng.random((N, 8, H)), axis=-1)[..., :256]; ix = (256 * rng.random((N, 8, P)) ** 3).astype(np.int64)
    hv = np.where(rng.random((N, 8, P)) < 0.3, rng.integers(0, H, (N, 8, P)), np.take_along_axis(pool, ix, 2))
    return fe, no, co, hv
def pack(fe, no, co, hv):
    return {"lim": np.ascontiguousarray(no.reshape(N, 128, H)).astype(np.float32).astype(BF), "feat": np.ascontiguousarray(fe.reshape(N, 128, P + T * B)).astype(np.float32).astype(BF),
            "comp": np.ascontiguousarray(co.reshape(N, 128, T * B)).astype(np.int32), "hd": np.ascontiguousarray(hv).astype(np.int32)}
def setup_inputs(rng):
    return pack(*parts(rng))
def setup_inputs_ties(rng):
    fe, no, co, hv = parts(rng)
    d = rng.permutation(np.array([1, 2, S - 1, S, S + 1, S, 1, S + 1])).reshape(1, 8, 1, 1)
    fe = 100 + d * (rng.random(fe.shape) < 0.8).astype(np.int64); no = 100 + d * (rng.random(no.shape) < 0.35).astype(np.int64)
    fe[..., 1::2] = fe[..., 0::2].copy()
    co[:, :, 8:, ::3] = co[:, :, :8, ::3].copy()
    return pack(fe, no, co, hv)
def setup_inputs_alike(rng):
    fe, no, co, hv = parts(rng)
    hv[:, ::2] = rng.choice(np.array([0, H - 1, H // 2, 37]), (N, 4, P)); hv[..., 0] = H - 1; hv[..., P - 1] = 0
    no[:, :4] = rng.integers(200, 256, (N, 4, 16, H))
    co[:, 1] = co[:, 1, :1].copy()
    co[:, 3] = np.where(rng.random((N, 16, T * B)) < 0.5, 0, BOUND - 1)
    co[:, 5] = rng.integers(BOUND - B, BOUND, (N, 16, T * B))
    co[:, 7, 2:] = np.where(rng.random((N, 14, T * B)) < 0.5, co[:, 7, :1], co[:, 7, 1:2])
    return pack(fe, no, co, hv)
def setup_inputs_ends(rng):
    fe, no, co, hv = parts(rng); M = T * B; k = np.arange(16)[:, None]
    for g in range(5): hv[:, g] = rng.permutation(H)[:P]
    no[:, :5] = 255
    o = np.argsort(rng.random((N, 16, M)), axis=1); s = rng.integers(0, P // 2, (N, 1, M))
    fe[:, 0] = 255; fe[:, 0, :, 1:P:2] = 0
    co[:, 0] = np.where(o < 2, 2 * rng.integers(0, P // 2, (N, 1, M)) + 1, 2 * ((s + o) % (P // 2)))
    fe[:, 1, :, :P] = rng.integers(200, 256, (N, 16, P)); fe[:, 1, :, P:] = 255
    lo = np.argsort(rng.random((N, 3, T, B)), axis=-1)
    lo[:, 1:] = 0; lo[:, 2, :, 1:-1] = 1 + np.argsort(rng.random((N, T, B - 1)), axis=-1)[..., :B - 2]
    w = B + rng.integers(0, P - B, (N, 3, 1, M))
    co[:, 2:5] = np.where(k == rng.integers(0, 16, (N, 3, 1, M)), lo.reshape(N, 3, 1, M), w)
    fe[:, 2:5, :, P:] = rng.integers(0, 160, (N, 3, 16, M)); fe[:, 4, :, P::B] = 255
    for g, b in ((5, 254), (6, 0)):
        fe[:, g] = b + (rng.random((N, 16, P + M)) < 0.8).astype(np.int64); no[:, g] = b + (rng.random((N, 16, H)) < 0.3).astype(np.int64)
    return pack(fe, no, co, hv)
def setup_inputs_still(rng):
    fe, no, co, hv = parts(rng); fe = np.maximum(fe, 1)
    z = rng.integers(0, 3, (N, 8, 1, 1)); z[:, 0] = 0; z[:, 1] = 1; z[:, 2] = 2
    return pack(fe, np.where(z == 0, 255, np.where(z == 1, 0, no)), co, hv)
def setup_inputs_spread(rng):
    fe, no, co, hv = parts(rng)
    fe = (np.exp2(8 * rng.random((N, 8, 1, P + T * B))) * rng.random(fe.shape)).astype(np.int64)
    no = (np.exp2(8 * rng.random((N, 8, 1, H))) * rng.random(no.shape)).astype(np.int64)
    hv = (H * rng.random((N, 8, P)) ** 4).astype(np.int64)
    return pack(fe, no, co, hv)
def check_inputs(d):
    bad = []
    for k in ("lim", "feat"):
        x = np.asarray(d[k]).astype(np.float32)
        if not np.all((x >= 0) & (x <= 255) & (x == np.floor(x))): bad.append("whole numbers of " + k)
    if np.min(d["hd"]) < 0 or np.max(d["hd"]) > H - 1: bad.append("range of hd")
    if np.min(d["comp"]) < 0 or not np.all(np.asarray(d["comp"]) < BOUND): bad.append("range of comp")
    return bad
def reference(lim, feat, comp, hd):
    fe = feat.astype(np.float32).astype(np.int16).reshape(N, 8, 16, P + T * B); no = lim.astype(np.float32).astype(np.int16).reshape(N, 8, 16, H)
    co = comp.astype(np.int64).reshape(N, 8, 16, T * B)
    h = np.zeros((N, 8, P + T * B), np.int64); h[:, :, :P] = hd
    kappa = np.zeros(N, np.int64); ranks = np.arange(N)
    for t in range(T):
        fv = fe[..., P + t * B:P + (t + 1) * B]
        ix = co[..., t * B:(t + 1) * B].reshape(N, 8, 16 * B)
        c = np.take_along_axis(h, ix, 2)
        fc = np.take_along_axis(fe, ix[:, :, None, :], 3).reshape(N, 8, 16, 16, B)
        share = np.add.reduce(np.minimum(fv[:, :, :, None, :], fc), axis=2, dtype=np.int64)
        for a in range(N):
            q = (ranks + a) % N
            x = np.take_along_axis(no[q], c[:, :, None, :], 3).reshape(N, 8, 16, 16, B)
            n = np.add.reduce(fv[:, :, :, None, :] > x, axis=2, dtype=np.int64).reshape(N, 8, 16 * B)
            c = np.where(n >= 9, ((c * c >> 5) + c + 613 * n + kappa[q][:, None, None]) & (H - 1), c)
        c = c.reshape(N, 8, 16, B)
        m = np.add.reduce(c[:, :, :, None, :] == c[:, :, None, :, :], axis=3, dtype=np.int64)
        key = 4096 * m + share
        won = np.take_along_axis(c, np.argmax(key, axis=2)[:, :, None, :], 2)[:, :, 0]
        lost = np.take_along_axis(c, np.argmin(key, axis=2)[:, :, None, :], 2)[:, :, 0]
        h[:, :, P + t * B:P + (t + 1) * B] = won
        for r in range(N):
            for g in range(8):
                e, first = np.unique(lost[r, g], return_index=True)
                old = no[r, g][:, e]
                no[r, g][:, e] = old + np.clip(fv[r, g][:, first] - old, -S, S)
        kappa = np.add.reduce(won, axis=(1, 2)) & 255
    return {"yh": h[:, :, P:].astype(np.float32), "yl": no.reshape(N, 128, H).astype(np.float32).astype(BF)}

@@ -1,0 +1,691 @@
+from concourse.bass import DstId, RemoteDMATransfer
+from concourse.mybir import AluOpType as A, ActivationFunctionType as AF, AxisListType
+
+N, H, P0, B, NT = 4, 2048, 1280, 256, 3
+NB, W = 4, 64
+VB = (0, 1)
+HV = (1, 3)
+RV = ()
+PIECE = 512
+CY, PCY, WAKE = 1.04, 0.52, 110.0
+GV, GS = 1.8, 1.56
+TUNE = (1000.0, 400.0, 4000.0, 562833, 1.0)
+
+SCRATCH = {}
+POOL = {}
+_FILL = {}
+_BYTES = {"float32": 4, "int32": 4, "bfloat16": 2, "float16": 2, "uint16": 2}
+
+
+def sb(names, shape, dtype):
+    for n in names.split():
+        SCRATCH[n] = ("sbuf", shape, dtype)
+
+
+def al(names, width, dtype):
+    unit = 32 // _BYTES[dtype]
+    for n in names.split():
+        p = "p_" + dtype
+        POOL[n] = (p, _FILL.get(p, 0), width)
+        _FILL[p] = _FILL.get(p, 0) + -(-width // unit) * unit
+        SCRATCH[p] = ("sbuf", [128, _FILL[p]], dtype)
+
+
+for _s in range(N):
+    sb("lm%d" % _s, [128, H + B], "bfloat16")
+    al("kc%d" % _s, 1, "float32")
+    al("kq%d" % _s, 128, "float16")
+sb("ft", [128, 2048], "bfloat16")
+sb("fv3", [128, 48, 16], "bfloat16")
+sb("ci", [128, 768], "int32")
+sb("hdi", [128, P0], "int32")
+sb("htab", [128, 2048], "float32")
+sb("hl", [128, 2 * PIECE], "bfloat16")
+al("xf", 768, "float16")
+al("cl", 768, "uint16")
+for _t in range(NT):
+    sb("fa%d fb%d" % (_t, _t), [128, 8, 256], "bfloat16")
+    sb("fr%d" % _t, [128, 2048], "bfloat16")
+    sb("new%d" % _t, [128, B], "bfloat16")
+    sb("off%d" % _t, [128, 32], "uint16")
+    sb("hlb%d" % _t, [128, 4, 8], "float16")
+    al("lf%d" % _t, 16, "float32")
+    al("lu%d" % _t, 16, "uint16")
+    for _b in range(NB):
+        al("ss%d_%d" % (_t, _b), 128, "float32")
+for _t in range(NT - 1):
+    for _s in range(1, N):
+        sb("rn%d_%d" % (_s, _t), [128, B], "bfloat16")
+        sb("ro%d_%d" % (_s, _t), [128, 32], "uint16")
+    sb("hn%d" % _t, [128, B], "bfloat16")
+    sb("ho%d" % _t, [128, 32], "uint16")
+for _b in range(NB):
+    al("hx%d" % _b, 1024, "float16")
+    al("cm%d xg%d mn%d mx%d" % (_b, _b, _b, _b), 1024, "bfloat16")
+    al("ul%d" % _b, W, "uint16")
+    al("sq%d tb%d tc%d tr%d de%d" % (_b, _b, _b, _b, _b), W, "float32")
+    al("mi%d mj%d" % (_b, _b), W, "int32")
+    al("cf%d" % _b, 80, "float16")
+    sb("eb%d" % _b, [128, 32, 16], "bfloat16")
+    al("rr%d nr%d yy%d" % (_b, _b, _b), 128, "float32")
+sb("ind", [128, 16, 272], "bfloat16")
+al("lbs lbm", 256, "float16")
+al("dup du1 du2 dumm", 16, "float32")
+al("old dif clp", B, "bfloat16")
+al("ks pf p16 gf rf b16 d2048 isr0 par npar", 1, "float32")
+al("ki kj pi gi ri pa", 1, "int32")
+al("io km", 256, "int32")
+al("iof", 160, "float32")
+al("kf", 256, "float32")
+al("idw r32 bwn bws bwp bwm", 160, "float16")
+al("nid id32 i613 i612 pm0 pm1 sw0 sw1 ones", 128, "float16")
+al("wi onb", 128, "bfloat16")
+al("c256 ta maskc", W, "float16")
+al("tbn", W, "float32")
+al("rsa rst", 128, "float32")
+al("ub", 2048, "bfloat16")
+for _b in range(NB):
+    SCRATCH["pb%d" % _b] = ("psum", [128, 16, 32], "float32")
+for _n in ("pe", "pd0", "pd1", "pm"):
+    SCRATCH[_n] = ("psum", [128, 512], "float32")
+
+DMASEMS = ["l_comp", "l_ci2", "l_hd", "l_ft", "l_fv", "l_lim", "st_h", "st_l"] + ["f_%d" % t for t in range(NT)]
+SEMAPHORES = (["qv", "qs", "qt", "qg"] + DMASEMS + ["lm_1", "lm_2", "lm_3", "bulk0", "bulk1", "ha0", "ha1", "hls"]
+              + ["%s%d" % (n, t) for t in range(NT - 1) for n in ("upo", "upn", "lo", "ln")]
+              + ["uq%d_%d" % (s, t) for t in range(NT - 1) for s in (1, 3)])
+
+
+def helpers(T, topo, core):
+    r = T.cores.index(core)
+    before, after = T.cores[(r - 1) % N], T.cores[(r + 1) % N]
+    cand = [c for c in topo.cores_of(core) if c not in T.cores and topo.may_write(c, before) and topo.may_write(c, after)]
+    near = [c for c in cand if topo.die(c) == topo.die(core)]
+    far = [c for c in cand if topo.die(c) != topo.die(core)]
+    return (near[0], far[0]), (near[1], far[1])
+
+
+def helper_program(g, core, T, topo):
+    S = T.sem
+    for rank in T.cores:
+        if core not in topo.cores_of(rank):
+            continue
+        r = T.cores.index(rank)
+        for hs, dst, slot in zip(helpers(T, topo, rank), (T.cores[(r - 1) % N], T.cores[(r + 1) % N]), (1, 3)):
+            if core not in hs:
+                continue
+            half = hs.index(core)
+            rid, pid = topo.addr(dst, core)
+            mask = topo.mask(core, dst)
+            ne = len(topo.engines(core, dst))
+            ls = 0
+            for p in range(2):
+                g.wait_ge(S["ha%d" % p], len(topo.engines(rank, core)) // 2)
+                c0 = half * 2 * PIECE + p * PIECE
+                g.remote_dma(T["lm%d" % slot][:, c0:c0 + PIECE], T.hl[:, p * PIECE:(p + 1) * PIECE], S["lm_%d" % slot], S.hls, pid, rid, mask)
+                ls += ne
+            if half == 0:
+                up = len(topo.engines(rank, T.cores[(r + 2) % N]))
+                for t in range(NT - 1):
+                    for sem, n, h in (("upo", "ro", "ho"), ("upn", "rn", "hn")):
+                        g.wait_ge(S["%s%d" % (sem, t)], up)
+                        g.remote_dma(T["%s%d_%d" % (n, slot, t)][:, :], T["%s%d" % (h, t)][:, :], S["uq%d_%d" % (slot, t)], S.hls, pid, rid, mask)
+                        ls += ne
+            g.wait_ge(S.hls, ls)
+
+
+def rank_program(g, core, T, topo):
+    if T.rank_of(core) is None:
+        helper_program(g, core, T, topo)
+        return
+    r = T.rank_of(core)
+    S = T.sem
+    V, C, M, Y = g.vector, g.scalar, g.tensor, g.sync
+    ops, hist = [], {}
+    psum = {n for n in SCRATCH if SCRATCH[n][0] == "psum"}
+
+    def X(n, lo=0, hi=None, st=1):
+        if n in POOL:
+            p, o, w = POOL[n]
+            t = T[p]
+        else:
+            t = T[n]
+            o, w = 0, t.shape[1]
+        if hi is None:
+            hi = w
+        return (t[:, o + lo:o + hi:st] if st != 1 else t[:, o + lo:o + hi], n, lo, hi)
+
+    def X3(n, a, b, lo=0, hi=None):
+        w = T[n].shape[2]
+        return (T[n][:, a:b, lo:w if hi is None else hi], n, a * w, b * w)
+
+    def XI(n, a, b, i):
+        w = T[n].shape[2]
+        return (T[n][:, a:b, i], n, a * w, b * w)
+
+    def HL(n, b, lo, hi):
+        return (T[n][:, b, lo:hi], n, 8 * b + lo, 8 * b + hi)
+
+    def PB(b, a, z):
+        return X3("pb%d" % b, a, z)
+
+    def IND(win, off):
+        return (win[0].indirect(off[0]), win, off)
+
+    def split(a):
+        return [a[1], a[2]] if len(a) == 3 else [a]
+
+    def size(a):
+        k = 1
+        for d in a[0].shape[1:]:
+            k *= d
+        return k
+
+    def add(q, busy, fire, reads, writes, sem=None, cnt=0, lat=0.0, extra=()):
+        i = len(ops)
+        deps = set(extra)
+        acc = [(x, 0) for x in reads] + [(x, 1) for x in writes]
+        for (ap, n, lo, hi), w in acc:
+            past = hist.get(n, ([], []))
+            for (j, jw, jlo, jhi, jq) in (past[0] + past[1] if w or n in psum else past[1]):
+                if n in psum and jq != q or jhi > lo and jlo < hi and (w or jw):
+                    deps.add(j)
+        for (ap, n, lo, hi), w in acc:
+            hist.setdefault(n, ([], []))[w].append((i, w, lo, hi, q))
+        ops.append({"q": q, "busy": busy, "fire": fire, "deps": deps - {i}, "sem": sem, "cnt": cnt, "lat": lat})
+        return i
+
+    def vc(n, f):
+        return max(64.0, n * f) * CY
+
+    def tt(out, a, b, op):
+        if len(a) == 3:
+            return add("v", 50 + vc(size(b), GV), lambda: V.tensor_tensor(out[0], a[0], b[0], op), split(a) + [b], [out])
+        return add("v", vc(size(out), 1 if (a[1] in psum or b[1] in psum) else 2), lambda: V.tensor_tensor(out[0], a[0], b[0], op), [a, b], [out])
+
+    def ts(out, a, s1, s2, o1, o2=None, fast=False):
+        rd = [a] + [s for s in (s1, s2) if isinstance(s, tuple)]
+        v1 = s1[0] if isinstance(s1, tuple) else s1
+        v2 = s2[0] if isinstance(s2, tuple) else s2
+        if o2 is None:
+            fn = lambda: V.tensor_scalar(out[0], a[0], v1, None, o1)
+        else:
+            fn = lambda: V.tensor_scalar(out[0], a[0], v1, v2, o1, o2)
+        return add("v", vc(size(out), 0.5 if fast else 1), fn, rd, [out])
+
+    def cp(out, a):
+        if len(a) == 3:
+            return add("v", 50 + vc(size(out), GS), lambda: V.tensor_copy(out[0], a[0]), split(a), [out])
+        if len(out) == 3:
+            return add("v", 50 + vc(size(a), 3.5), lambda: V.tensor_copy(out[0], a[0]), [a, out[2]], [out[1]])
+        return add("v", vc(size(out), 1), lambda: V.tensor_copy(out[0], a[0]), [a], [out])
+
+    def ms(out, c):
+        return add("v", vc(size(out), 1), lambda: V.memset(out[0], c), [], [out])
+
+    def act(out, a, func, bias=0.0, scale=1.0, acc=None):
+        cost = 65 + vc(size(out), GS) if len(a) == 3 else 60 + vc(size(out), 1)
+        if acc:
+            fn = lambda: C.activation(out[0], a[0], func, bias=bias, scale=scale, accum_out=acc[0])
+        else:
+            fn = lambda: C.activation(out[0], a[0], func, bias=bias, scale=scale)
+        return add("s", cost, fn, split(a), [out] + ([acc] if acc else []))
+
+    def mm(lst):
+        rd, wr = {}, {}
+        for o, l, x, s0, s1 in lst:
+            rd[l[1:]], rd[x[1:]], wr[o[1:]] = l, x, o
+
+        def fire():
+            for o, l, x, s0, s1 in lst:
+                ins = M.matmul(o[0], l[0], x[0], s0, s1)
+            return ins
+        return add("t", sum(max(64.0, size(x[2])) for x in lst) * PCY, fire, list(rd.values()), list(wr.values()))
+
+    def dma(q, out, in_, sem, lat):
+        e = {"y": Y, "s": C}[q]
+        rd = [in_] if isinstance(in_, tuple) else []
+        wr = [out] if isinstance(out, tuple) else []
+        src, dst_ = (in_[0] if rd else in_), (out[0] if wr else out)
+        return add(q, 60, lambda: e.dma_start(dst_, src), rd, wr, sem=sem, cnt=16, lat=lat)
+
+    ha, hb = helpers(T, topo, core)
+    opp = T.cores[(r + 2) % N]
+    mo = topo.mask(core, opp)
+    no = len(topo.engines(core, opp))
+
+    def dst(c):
+        rid, pid = topo.addr(c, core)
+        return DstId(rid=rid, pnc=pid)
+
+    def pair(hs, p):
+        tr = []
+        for h in range(2):
+            es = topo.engines(core, hs[h])
+            k = len(es) // 2
+            c0 = (2 * h + p) * PIECE
+            tr.append(RemoteDMATransfer(dst_ids=[dst(hs[h])], dma_engine_mask=sum(1 << e for e in es[h * k:(h + 1) * k]), remote_sem=S["ha%d" % p],
+                                        srcs=[T.lm0[:, c0:c0 + PIECE]], dsts=[T.hl[:, p * PIECE:(p + 1) * PIECE]]))
+        return lambda: g.remote_dma_fused(tr, local_sem=S.bulk0)
+
+    dma("y", X("ci", 0, 256), T.comp[:, 0:256], "l_comp", 2000)
+    dma("s", X("lm0", 0, H), T.lim[:, :], "l_lim", 3500)
+    dma("y", X("ft"), T.feat[:, :], "l_ft", 3500)
+    ms(X("hdi"), 0)
+    add("y", 60, lambda: Y.dma_start(T.hdi[0:128:16, :], T.hd[:, :]), [], [X("hdi")], sem="l_hd", cnt=16, lat=2000)
+    dma("y", X3("fv3", 0, 48), T.feat[:, P0:2048], "l_fv", 2300)
+    dma("s", X("ci", 256, 768), T.comp[:, 256:768], "l_ci2", 2500)
+    add("g", 560, lambda: g.iota(X("io")[0], [[1, 256]], 0, 0), [], [X("io")])
+    add("g", 140, lambda: g.iota(X("pi")[0], [[0, 1]], 0, 1), [], [X("pi")])
+
+    cp(X("pf"), X("pi"))
+    ts(X("ri"), X("pi"), 15, None, A.bitwise_and)
+    ts(X("gi"), X("pi"), 4, None, A.logical_shift_right)
+    ts(X("pa"), X("pi"), 4, 1, A.logical_shift_right, A.bitwise_and)
+    cp(X("iof"), X("io", 0, 160))
+    cp(X("rf"), X("ri"))
+    cp(X("gf"), X("gi"))
+    cp(X("par"), X("pa"))
+    ts(X("npar"), X("par"), -1.0, 1.0, A.mult, A.add)
+    ts(X("p16"), X("pf"), 16.0, None, A.add)
+    ts(X("b16"), X("gf"), 16.0, 16.0, A.mult, A.add)
+    ts(X("isr0"), X("rf"), 0.0, None, A.is_equal)
+    ts(X("idw"), X("iof"), X("p16"), None, A.is_equal)
+    ID = X("idw", 16, 144)
+
+    def SL(n, s):
+        return X(n, s, s + 128)
+    ts(X("pm0"), ID, X("npar"), None, A.mult, fast=True)
+    ts(X("pm1"), ID, X("par"), None, A.mult, fast=True)
+    ts(X("sw0"), SL("idw", 0), X("npar"), None, A.mult, fast=True)
+    ts(X("sw1"), SL("idw", 32), X("par"), None, A.mult, fast=True)
+    ts(X("r32"), X("idw"), X("isr0"), 32.0, A.mult, A.mult, fast=True)
+    for n, w in (("bwn", 19616.0), ("bws", 9808.0), ("bwp", 16.0), ("bwm", -16.0)):
+        ts(X(n), X("iof"), X("b16"), w, A.is_equal, A.mult)
+    for n, w in (("nid", -1.0), ("id32", 32.0), ("i613", 613.0), ("i612", 612.0), ("wi", 65536.0)):
+        act(X(n), ID, AF.Copy, scale=w)
+
+    def lists(t, b):
+        c0 = t * 256 + b * W
+        if b == 0:
+            cp(X("xf", t * 256, t * 256 + 256), X("ci", t * 256, t * 256 + 256))
+        run = []
+        for j in range(4):
+            o = X("pm", b * W + 16 * j, b * W + 16 * j + 16)
+            k = c0 // 16 + j
+            me, ot = X("xf", 16 * k, 16 * k + 16), X("xf", 16 * (k ^ 1), 16 * (k ^ 1) + 16)
+            run += [(o, X("pm%d" % (k & 1)), me, True, False), (o, X("sw%d" % (k & 1)), ot, False, True)]
+        mm(run)
+        tr, y = X("tr%d" % b), X("pm", b * W, b * W + W)
+        add("v", vc(W, 1), lambda: V.transpose(tr[0], y[0]), [y], [tr])
+        cp(X("cl", c0, c0 + W), tr)
+
+    lists(0, 0)
+    cp(X("htab", 0, P0), X("hdi"))
+    for b in range(1, NB):
+        lists(0, b)
+
+    def fr(t, eng):
+        for half, n in ((0, "fa%d" % t), (1, "fb%d" % t)):
+            a = 16 * t + 8 * half
+            for k in range(16):
+                o, i = T[n][:, :, 16 * k:16 * k + 16], T.fv3[:, a:a + 8, :]
+                q, cost, fn = {"v": ("v", vc(128, 0.5), lambda o=o, i=i: V.tensor_copy(o, i)),
+                               "s": ("s", 60 + vc(128, 1), lambda o=o, i=i: C.activation(o, i, AF.Copy)),
+                               "g": ("g", 170 + 256 * CY, lambda o=o, i=i: g.affine_select(o, i, [[0, 8], [0, 16]], A.is_gt, 0.0, 1, 0))}[eng[half]]
+                add(q, cost, fn, [X3("fv3", a, a + 8)], [(o, n, 128 * k, 128 * k + 128)])
+            if half == 0:
+                dma("y", X("fr%d" % t), X3(n, 0, 8), "f_%d" % t, 3500)
+
+    fr(0, "vs")
+    ts(X("km"), X("io"), 15, None, A.bitwise_and)
+    cp(X("kf"), X("km"))
+    ts(X("c256"), X("kf", 0, W), 0.0, 256.0, A.mult, A.add)
+    ts(X("ones"), X("iof", 0, 128), 0.0, 1.0, A.mult, A.add)
+    ts(X("ta"), X("kf", 0, W), -1.0, 15.0, A.mult, A.add)
+    ts(X("tbn"), X("kf", 0, W), -2.0, 15.0, A.mult, A.add)
+    for t in range(NT):
+        ms(X("off%d" % t), 0)
+
+    RL = X("lm0", 0, H)
+    nb = len(topo.engines(core, ha[0]))
+    rid, pid = topo.addr(opp, core)
+    for p in range(2):
+        add("g", 1200, pair(ha, p), [RL], [], sem="bulk0", cnt=nb, lat=3000)
+    add("g", 1200, lambda: g.remote_dma(T.lm2[:, 0:H], T.lm0[:, 0:H], S.lm_2, S.bulk1, pid, rid, mo), [RL], [], sem="bulk1", cnt=no, lat=6000)
+    for p in range(2):
+        add("g", 1200, pair(hb, p), [RL], [], sem="bulk0", cnt=nb, lat=3000)
+    for s, at in ((1, 14000), (2, 16000), (3, 20000)):
+        src = T.cores[(r + s) % N]
+        if s == 2:
+            cnt = len(topo.engines(src, core))
+        else:
+            cnt = sum(2 * len(topo.engines(h, core)) for h in helpers(T, topo, src)[0 if s == 1 else 1])
+        add("x", 0, None, [], [X("lm%d" % s, 0, H)], sem="lm_%d" % s, cnt=cnt, lat=at)
+    for t in (1, 2):
+        fr(t, "gg")
+
+    def late():
+        onb = X("onb")
+        ms(onb, 1.0)
+        ts(X("rsa"), X("kf", 0, 128), 0.0, -2.0e9, A.is_equal, A.mult)
+        ts(X("rst"), X("rsa"), 1.0e9, None, A.add)
+        ts(X("maskc"), X("kf", 0, W), X("rf"), 4096.0, A.is_ge, A.mult)
+        for b in range(NB):
+            ts(X("cf%d" % b, 0, 8), X("iof", 0, 8), 0.0, None, A.mult)
+        ts(X("d2048"), X("rf"), 2048.0, None, A.add)
+        ts(X("dumm"), X("iof", 0, 16), 16.0, X("d2048"), A.mult, A.add)
+        for j in range(16):
+            o = X("ub", 128 * j, 128 * j + 128)
+            add("g", 170 + 256 * CY, lambda o=o, j=j: g.affine_select(o[0], onb[0], [[-16, 8], [0, 16]], A.is_equal, 0.0, -j, 1), [onb], [o])
+
+    rot = [0]
+
+    def diff(t, b, xg, out, func, bias):
+        for h in range(2):
+            d = X("pd%d" % rot[0])
+            rot[0] ^= 1
+            a = (b % 2) * 4 + 2 * h
+            n = ("fa%d" if b < 2 else "fb%d") % t
+            mm([(d, ID, (T[n][:, a:a + 2, :], n, 0, 2048), True, False), (d, X("nid"), X(xg, 512 * h, 512 * h + 512), False, True)])
+            act(X(out, 512 * h, 512 * h + 512), d, func, bias=bias)
+
+    def col(n, j):
+        return X(n, j, 1024, 16)
+
+    def halves(n, c0=0):
+        return [(X(n, c0 + 32 * z, c0 + 32 * z + 32), 512 * z, 512 * z + 512) for z in range(2)]
+
+    def shares(t, b):
+        mn, win = "mn%d" % b, X("ft", 0, P0 + B * t)
+        o = X("pm", 256 + W * b, 320 + W * b)
+        vp = b in VB
+        for cl, lo, hi in halves("cl", t * 256 + b * W):
+            if vp:
+                tt(X(mn, lo, hi), IND(win, cl), X("fr%d" % t, 1024 * b + lo, 1024 * b + hi), A.min)
+            else:
+                act(X("mx%d" % b, lo, hi), IND(win, cl), AF.Copy)
+        if not vp:
+            diff(t, b, "mx%d" % b, mn, AF.Relu, 0.0)
+        mm([(o, ID, X("ta"), True, False)] + [(o, SL("bwp" if vp else "bwm", 16 - j), col(mn, j), False, j == 15) for j in range(16)])
+        ss = "ss%d_%d" % (t, b)
+        act(X(ss, 0, W), o, AF.Copy)
+        tt(X(ss, W, 2 * W), X("tbn"), o, A.subtract)
+
+    def heads(t, b):
+        win, cl = X("htab", 0, P0 + B * t), X("cl", t * 256 + b * W, t * 256 + b * W + W)
+        if b in HV:
+            cp(X("hx%d" % b), IND(win, cl))
+        else:
+            act(X("hx%d" % b), IND(win, cl), AF.Copy)
+        mm([(PB(b, 0, 2), SL("r32", 16 - j), col("hx%d" % b, j), j == 0, j == 15) for j in range(16)])
+        ts(X("ul%d" % b), PB(b, 0, 2), 1.0 / 32, None, A.mult)
+        act(X("sq%d" % b), PB(b, 0, 2), AF.Square, bias=16.0, scale=1.0 / 32)
+
+    def visit(t, b, a):
+        lm, cm = X("lm%d" % a, 0, H), "cm%d" % b
+        run = [(X("kq%d" % a), X("ones", 0, W))] if t else []
+        if b in VB:
+            for ul, lo, hi in halves("ul%d" % b):
+                tt(X(cm, lo, hi), IND(lm, ul), X("fr%d" % t, 1024 * b + lo, 1024 * b + hi), A.is_lt)
+            bw = "bwn"
+            if not t:
+                run.append((X("nid"), X("c256")))
+        else:
+            for ul, lo, hi in halves("ul%d" % b):
+                act(X("xg%d" % b, lo, hi), IND(lm, ul), AF.Copy)
+            diff(t, b, "xg%d" % b, cm, AF.Sign, -0.5)
+            bw = "bws"
+            run.append((X("i613" if t else "i612"), X("c256")))
+        run += [(SL(bw, 16 - j), col(cm, j)) for j in range(16)]
+        mm([(PB(b, 2, 4), l, x, i == 0, i == len(run) - 1) for i, (l, x) in enumerate(run)])
+        ts(X("tc%d" % b), PB(b, 2, 4), 170000.0, 16777216.0, A.is_ge, A.mult)
+        tt(PB(b, 4, 6), X("sq%d" % b), PB(b, 2, 4), A.add)
+        tt(X("tb%d" % b), X("tc%d" % b), PB(b, 0, 2), A.add)
+        tt(X("mi%d" % b), X("tb%d" % b), PB(b, 4, 6), A.min)
+        ts(X("mj%d" % b), X("mi%d" % b), 5, 2047, A.arith_shift_right, A.bitwise_and)
+        if a < N - 1:
+            cp(X("ul%d" % b), X("mj%d" % b))
+        cp(X("cf%d" % b, 8, 72), X("mj%d" % b))
+        if a < N - 1:
+            mm([(PB(b, 0, 2), X("id32"), X("cf%d" % b, 8, 72), True, True)])
+            act(X("sq%d" % b), PB(b, 0, 2), AF.Square, bias=16.0, scale=1.0 / 32)
+
+    def elect(t, b):
+        cf, eb, pb = "cf%d" % b, "eb%d" % b, "pb%d" % b
+        c, pm, de = X(cf, 8, 72), X3(pb, 10, 14, 0, 16), X("de%d" % b)
+        mm([(X3(pb, 6, 10, 0, 16), ID, c, True, True), (X3(pb, 6, 10, 16, 32), ID, c, True, True)])
+        for d in range(1, 9):
+            tt(X3(eb, 4 * d - 4, 4 * d), c, X3(pb, 6, 10, d, d + 16), A.is_equal)
+        tt(de, X(cf, 7, 71), c, A.subtract)
+        run = []
+        for d in range(1, 9):
+            run.append((pm, X3(eb, 4 * d - 4, 4 * d)))
+            if d < 8:
+                run.append((X3(pb, 10, 14, d, 16), X3(eb, 4 * d - 4, 4 * d, 0, 16 - d)))
+                run.append((X3(pb, 10, 14, 0, d), X3(eb, 4 * d - 4, 4 * d, 16 - d, 16)))
+        mm([(o, X("wi"), x, i == 0, i == len(run) - 1) for i, (o, x) in enumerate(run)])
+        ss = "ss%d_%d" % (t, b)
+        kk, rr, nr, rst = X("pe", 128 * b, 128 * b + 128), X("rr%d" % b), X("nr%d" % b), X("rst")
+        tt(X("pe", 128 * b, 128 * b + W), X(ss, 0, W), pm, A.add)
+        tt(X("pe", 128 * b + W, 128 * b + 2 * W), X(ss, W, 2 * W), pm, A.subtract)
+        add("v", vc(128, 1), lambda: V.tensor_tensor_scan(rr[0], rst[0], kk[0], 0.0, A.min, A.max), [rst, kk], [rr])
+        tt(nr, rr, kk, A.not_equal)
+        for h in range(2):
+            n, y = X("nr%d" % b, W * h, W * h + W), X("yy%d" % b, W * h, W * h + W)
+            add("v", vc(W, 1), lambda n=n, y=y: V.tensor_tensor_scan(y[0], de[0], n[0], 0.0, A.add, A.mult), [de, n], [y])
+        c15, hl = X(cf, 23, 72, 16), "hlb%d" % t
+        tt(HL(hl, b, 0, 4), X("yy%d" % b, 15, 64, 16), c15, A.add)
+        tt(HL(hl, b, 4, 8), X("yy%d" % b, 79, 128, 16), c15, A.add)
+        tt(X("lf%d" % t, 4 * b, 4 * b + 4), X("yy%d" % b, 79, 128, 16), c15, A.add)
+        mm([(XI(pb, 0, 8, j), X("ub", 128 * j, 128 * j + 128), HL(hl, b, 0, 8), True, True) for j in range(16)])
+        c0 = P0 + B * t + W * b
+        act(X("htab", c0, c0 + W), X3(pb, 0, 4, 0, 16), AF.Copy)
+
+    def compare(t, b):
+        lf, pl = "lf%d" % t, X3("pb%d" % b, 4, 8, 0, 16)
+        cp(X("lu%d" % t, 4 * b, 4 * b + 4), X(lf, 4 * b, 4 * b + 4))
+        tt(X("lbm", W * b, W * b + W), X("maskc"), pl, A.add)
+        act(X("lbs", W * b, W * b + W), pl, AF.Copy)
+        for j in range(4 * b, 4 * b + 4):
+            def o(lo, hi):
+                return (T.ind[:, j, lo:hi], "ind", 272 * j + lo, 272 * j + hi)
+            if j:
+                ts(o(256 - 16 * j, 256), X("lbs", 0, 16 * j), X(lf, j, j + 1), 4096.0, A.is_equal, A.mult, fast=True)
+            ts(o(256, 272), X("lbm", 16 * j, 16 * j + 16), X(lf, j, j + 1), 4096.0, A.is_equal, A.mult, fast=True)
+            i, d = o(256 - 16 * j, 272), X("dup", j, j + 1)
+            if j in RV:
+                add("v", vc(16 * j + 16, 1), lambda i=i, d=d: V.tensor_reduce(d[0], i[0], AxisListType.X, A.add), [i], [d])
+            else:
+                act(i, i, AF.Copy, acc=d)
+
+    def kappa(t):
+        o, ks = (T.pb0[:, 0, 0:16], "pb0", 0, 32), X("ks")
+        mm([(o, X("ones"), (T["hlb%d" % t][:, :, 0:4], "hlb%d" % t, 0, 32), True, True)])
+        add("v", vc(16, 1), lambda: V.tensor_reduce(ks[0], o[0], AxisListType.X, A.add), [o], [ks])
+        cp(X("ki"), ks)
+        ts(X("kj"), X("ki"), 255, None, A.bitwise_and)
+        cp(X("off%d" % t, 16, 17), X("kj"))
+        ts(X("kc0"), X("kj"), 32.0, -256.0, A.mult, A.add)
+        ts(X("kq0"), ID, X("kc0"), None, A.mult, fast=True)
+
+    def scat(a, new, off):
+        cp(IND(X("lm%d" % a, 0, H + B), off), new)
+
+    def losers(t):
+        lf = "lf%d" % t
+        act(X("old"), IND(X("lm0", 0, H), X("lu%d" % t)), AF.Copy)
+        tt(X("dif"), X("ft", P0 + B * t, P0 + B * t + B), X("old"), A.subtract)
+        ts(X("clp"), X("dif"), -32.0, 32.0, A.max, A.min, fast=True)
+        tt(X("new%d" % t), X("old"), X("clp"), A.add)
+        tt(X("du1"), X("dup"), X("dumm"), A.min)
+        tt(X("du2"), X("du1"), X(lf), A.max)
+        cp(X("off%d" % t, 0, 16), X("du2"))
+        scat(0, X("new%d" % t), X("off%d" % t, 0, 16))
+
+    def send(t):
+        ids = [dst(c) for c in (opp, ha[0], hb[0])]
+
+        def call(src, bufs, sem, ls):
+            tr = [RemoteDMATransfer(dst_ids=ids, dma_engine_mask=mo, remote_sem=S[sem], srcs=[T[src][:, :]], dsts=[T[n][:, :] for n in bufs])]
+            return lambda: g.remote_dma_fused(tr, local_sem=S[ls])
+        sent = []
+        ne = len(topo.engines(opp, core))
+        for src, got, h, up, ls in (("off", "ro2", "ho", "upo", "lo"), ("new", "rn2", "hn", "upn", "ln")):
+            n = "%s%d" % (src, t)
+            fn = call(n, ["%s_%d" % (got, t)] + ["%s%d" % (h, t)] * 2, "%s%d" % (up, t), "%s%d" % (ls, t))
+            sent.append(add("g", 1500, fn, [X(n)], [], sem="%s%d" % (ls, t), cnt=no, lat=2500))
+            add("x", 0, None, [], [X("%s_%d" % (got, t))], sem="%s%d" % (up, t), cnt=ne, lat=2500, extra=(sent[-1],))
+        for s in (1, 3):
+            h = helpers(T, topo, T.cores[(r + s) % N])[0 if s == 1 else 1][0]
+            add("x", 0, None, [], [X("ro%d_%d" % (s, t)), X("rn%d_%d" % (s, t))], sem="uq%d_%d" % (s, t), cnt=2 * len(topo.engines(h, core)), lat=6000, extra=sent)
+
+    def receive(t, s):
+        ts(X("kc%d" % s), X("ro%d_%d" % (s, t), 16, 17), 32.0, -256.0, A.mult, A.add)
+        ts(X("kq%d" % s), ID, X("kc%d" % s), None, A.mult, fast=True)
+        scat(s, X("rn%d_%d" % (s, t)), X("ro%d_%d" % (s, t), 0, 16))
+
+    for t in range(NT):
+        for b in range(NB):
+            heads(t, b)
+        for a in range(N):
+            if t and a:
+                receive(t - 1, a)
+            for b in range(NB):
+                visit(t, b, a)
+            if t == 0 and a == 0:
+                late()
+            if t == 0 and a == 1:
+                for b in range(NB):
+                    shares(0, b)
+        for b in range(NB):
+            elect(t, b)
+        for b in range(NB):
+            compare(t, b)
+        if t == 0:
+            for tn in (1, 2):
+                for b in range(NB):
+                    lists(tn, b)
+        if t < NT - 1:
+            kappa(t)
+        losers(t)
+        if t < NT - 1:
+            send(t)
+            for b in range(NB):
+                shares(t + 1, b)
+    add("y", 60, lambda: Y.dma_start(T.yh[:, :], T.htab[0:128:16, P0:2048]), [X("htab", P0, 2048)], [], sem="st_h", cnt=16, lat=2000)
+    dma("y", T.yl[:, :], X("lm0", 0, H), "st_l", 3500)
+    emit(g, T, ops)
+
+
+def schedule(ops):
+    n = len(ops)
+    look, fit, theta, rnd, amp = TUNE
+    succ = [[] for _ in range(n)]
+    need = [len(o["deps"]) for o in ops]
+    for i, o in enumerate(ops):
+        for j in o["deps"]:
+            succ[j].append(i)
+    prio = [0.0] * n
+    for i in range(n - 1, -1, -1):
+        o = ops[i]
+        m = max([prio[j] for j in succ[i]], default=-WAKE - o["lat"]) + o["lat"] + WAKE
+        rnd = (rnd * 1103515245 + 12345) % 2147483648
+        prio[i] = o["busy"] * (1.0 + amp * (rnd / 2147483648.0 - 0.5)) + m
+    free, ready, avail, queues = {}, [0.0] * n, {}, {}
+    for i in range(n):
+        if need[i] == 0:
+            avail.setdefault(ops[i]["q"], []).append(i)
+    end = 0.0
+    for _ in range(n):
+        best = None
+        for q, lst in avail.items():
+            if lst:
+                e = max(free.get(q, 0.0), min(ready[i] for i in lst))
+                if best is None or e < best[0]:
+                    best = (e, q)
+        e, q = best
+        lst = avail[q]
+        now = [i for i in lst if ready[i] <= e + 1e-6]
+        pick = max(now, key=lambda i: (prio[i], -i))
+        if q in "vs":
+            soon = [i for i in lst if e + 1e-6 < ready[i] <= e + look and prio[i] > prio[pick] + theta]
+            if soon:
+                p = max(soon, key=lambda i: (prio[i], -i))
+                if e + ops[pick]["busy"] > ready[p] + fit:
+                    ok = [i for i in now if e + ops[i]["busy"] <= ready[p] + fit]
+                    pick = max(ok, key=lambda i: (prio[i], -i)) if ok else p
+        lst.remove(pick)
+        o = ops[pick]
+        e = max(e, ready[pick])
+        fin = e + o["busy"]
+        if q != "x":
+            free[q] = fin
+        o["t0"], o["t1"] = e, fin
+        queues.setdefault(q, []).append(pick)
+        comp = fin + o["lat"]
+        end = max(end, comp)
+        for j in succ[pick]:
+            ready[j] = max(ready[j], comp + WAKE)
+            need[j] -= 1
+            if need[j] == 0:
+                avail.setdefault(ops[j]["q"], []).append(j)
+    return queues, end
+
+
+def emit(g, T, ops):
+    queues, end = schedule(ops)
+    S = T.sem
+    eng = {"v": g.vector, "s": g.scalar, "t": g.tensor, "g": g, "y": g.sync}
+    qsem = {"v": "qv", "s": "qs", "t": "qt", "g": "qg"}
+    wanted = set()
+    for o in ops:
+        wanted |= o["deps"]
+    total = {}
+    for q, lst in queues.items():
+        for i in lst:
+            o = ops[i]
+            if o["sem"]:
+                s, c = o["sem"], o["cnt"]
+            elif i in wanted:
+                s, c = qsem[q], 1
+            else:
+                continue
+            total[s] = total.get(s, 0) + c
+            o["tok"] = (s, total[s])
+    for o in ops:
+        if o["sem"]:
+            o["tok"] = (o["sem"], total[o["sem"]])
+    known = {q: {} for q in queues}
+    nxt = {q: 0 for q in queues}
+    done = set()
+    while len(done) < len(ops):
+        for q, lst in queues.items():
+            kn = known[q]
+            while nxt[q] < len(lst):
+                i = lst[nxt[q]]
+                o = ops[i]
+                if not o["deps"] <= done:
+                    break
+                if q == "x":
+                    o["clk"] = {o["tok"][0]: o["tok"][1]}
+                else:
+                    for j in sorted(o["deps"], key=lambda j: -ops[j]["t1"]):
+                        s, v = ops[j]["tok"]
+                        if kn.get(s, 0) < v:
+                            eng[q].wait_ge(S[s], v)
+                            for s2, v2 in ops[j]["clk"].items():
+                                kn[s2] = max(kn.get(s2, 0), v2)
+                            kn[s] = max(kn.get(s, 0), v)
+                    ins = o["fire"]()
+                    o["clk"] = dict(kn)
+                    if o["sem"] in DMASEMS:
+                        ins.then_inc(S[o["sem"]], 16)
+                    elif not o["sem"] and i in wanted:
+                        ins.then_inc(S[o["tok"][0]], 1)
+                    if "tok" in o:
+                        o["clk"][o["tok"][0]] = max(kn.get(o["tok"][0], 0), o["tok"][1])
+                done.add(i)
+                nxt[q] += 1
+    for s, v in total.items():
+        if known["g"].get(s, 0) < v:
+            g.wait_ge(S[s], v)

@@ -2,14 +2,20 @@ from concourse.bass import DstId, RemoteDMATransfer
 from concourse.mybir import AluOpType as A, ActivationFunctionType as AF, AxisListType
 
 N, H, P0, B, NT = 4, 2048, 1280, 256, 3
-NB, W = 4, 64
-VB = (0, 1)
-HV = (1, 3)
-RV = ()
-PIECE = 512
-CY, PCY, WAKE = 1.04, 0.52, 110.0
-GV, GS = 1.8, 1.56
-TUNE = (1000.0, 400.0, 4000.0, 562833, 1.0)
+NB, W, E = 2, 128, 2048
+NS = 768
+VCH = 416
+SSH = (0,)
+HV = 0
+Q4 = H // 4
+UP = 280
+BIG = 68 * 65536
+CY, PCY, WAKE = 1.04, 0.52, 170.0
+GA, SC = 1.56, 3.8
+HCH = 512
+LOOK = 900.0
+FIT = 250.0
+THETA = 0.0
 
 SCRATCH = {}
 POOL = {}
@@ -32,105 +38,97 @@ def al(names, width, dtype):
 
 
 for _s in range(N):
-    sb("lm%d" % _s, [128, H + B], "bfloat16")
+    sb("lm%d" % _s, [128, H + 2 * B], "bfloat16")
     al("kc%d" % _s, 1, "float32")
-    al("kq%d" % _s, 128, "float16")
+    al("kq%d" % _s, 128, "bfloat16")
+    al("ou%d" % _s, 16, "uint16")
 sb("ft", [128, 2048], "bfloat16")
-sb("fv3", [128, 48, 16], "bfloat16")
 sb("ci", [128, 768], "int32")
-sb("hdi", [128, P0], "int32")
+sb("hdi", [128, 80], "int32")
 sb("htab", [128, 2048], "float32")
-sb("hl", [128, 2 * PIECE], "bfloat16")
-al("xf", 768, "float16")
+sb("hl", [128, Q4], "bfloat16")
+al("hdf", 80, "float16")
 al("cl", 768, "uint16")
 for _t in range(NT):
-    sb("fa%d fb%d" % (_t, _t), [128, 8, 256], "bfloat16")
-    sb("fr%d" % _t, [128, 2048], "bfloat16")
-    sb("new%d" % _t, [128, B], "bfloat16")
-    sb("off%d" % _t, [128, 32], "uint16")
-    sb("hlb%d" % _t, [128, 4, 8], "float16")
-    al("lf%d" % _t, 16, "float32")
-    al("lu%d" % _t, 16, "uint16")
-    for _b in range(NB):
-        al("ss%d_%d" % (_t, _b), 128, "float32")
+    sb("fr%d" % _t, [128, NB * E], "bfloat16")
+    sb("up%d" % _t, [128, UP], "float16")
 for _t in range(NT - 1):
-    for _s in range(1, N):
-        sb("rn%d_%d" % (_s, _t), [128, B], "bfloat16")
-        sb("ro%d_%d" % (_s, _t), [128, 32], "uint16")
-    sb("hn%d" % _t, [128, B], "bfloat16")
-    sb("ho%d" % _t, [128, 32], "uint16")
+    sb("ru1_%d ru2_%d ru3_%d hu%d" % (_t, _t, _t, _t), [128, UP], "float16")
 for _b in range(NB):
-    al("hx%d" % _b, 1024, "float16")
-    al("cm%d xg%d mn%d mx%d" % (_b, _b, _b, _b), 1024, "bfloat16")
+    sb("hx%d" % _b, [128, E], "float16")
+    sb("cm%d mn0_%d mn1_%d mn2_%d" % (_b, _b, _b, _b), [128, E], "bfloat16")
+    al("xg%d" % _b, NS, "bfloat16")
     al("ul%d" % _b, W, "uint16")
-    al("sq%d tb%d tc%d tr%d de%d" % (_b, _b, _b, _b, _b), W, "float32")
+    al("sq%d" % _b, W, "float32")
     al("mi%d mj%d" % (_b, _b), W, "int32")
-    al("cf%d" % _b, 80, "float16")
-    sb("eb%d" % _b, [128, 32, 16], "bfloat16")
-    al("rr%d nr%d yy%d" % (_b, _b, _b), 128, "float32")
-sb("ind", [128, 16, 272], "bfloat16")
-al("lbs lbm", 256, "float16")
-al("dup du1 du2 dumm", 16, "float32")
-al("old dif clp", B, "bfloat16")
-al("ks pf p16 gf rf b16 d2048 isr0 par npar", 1, "float32")
-al("ki kj pi gi ri pa", 1, "int32")
-al("io km", 256, "int32")
-al("iof", 160, "float32")
-al("kf", 256, "float32")
-al("idw r32 bwn bws bwp bwm", 160, "float16")
-al("nid id32 i613 i612 pm0 pm1 sw0 sw1 ones", 128, "float16")
-al("wi onb", 128, "bfloat16")
-al("c256 ta maskc", W, "float16")
-al("tbn", W, "float32")
-al("rsa rst", 128, "float32")
-al("ub", 2048, "bfloat16")
+    al("ch%d lz%d dz%d" % (_b, _b, _b), W + 16, "float16")
+    al("wz%d lr%d de%d" % (_b, _b, _b), W, "float16")
+    al("rr%d" % _b, 2 * W, "float32")
+    al("nr%d yy%d" % (_b, _b), 2 * W, "float16")
+    al("dmy%d" % _b, 1, "float32")
+    sb("eb%d" % _b, [128, 64, 16], "bfloat16")
+sb("mx", [128, 1024], "bfloat16")
+sb("ind", [128, 24 * W], "bfloat16")
+al("lbs", B, "float16")
+al("lf", 16, "float32")
+al("lu", 16, "uint16")
+al("old clp", B, "bfloat16")
+al("ks pf gf cst ca thr", 1, "float32")
+al("ki kj pi gi", 1, "int32")
+al("io", 144, "int32")
+al("km", W, "int32")
+al("iof", 144, "float32")
+al("kf idf rsa rsb st", W, "float32")
+al("idw", 144, "float16")
+al("nid idq on32 keep", W, "float16")
+al("wi ones p0m rwa rwb hf", W, "bfloat16")
+al("w1 wh", 8, "float16")
+al("w2 wp wm wu", 8, "bfloat16")
+al("e0", 2, "bfloat16")
 for _b in range(NB):
-    SCRATCH["pb%d" % _b] = ("psum", [128, 16, 32], "float32")
-for _n in ("pe", "pd0", "pd1", "pm"):
-    SCRATCH[_n] = ("psum", [128, 512], "float32")
+    SCRATCH["px%d" % _b] = ("psum", [128, 16, 32], "float32")
+    SCRATCH["pk%d" % _b] = ("psum", [128, 32, 16], "float32")
+for _n in range(4):
+    SCRATCH["pd%d" % _n] = ("psum", [128, 512], "float32")
 
-DMASEMS = ["l_comp", "l_ci2", "l_hd", "l_ft", "l_fv", "l_lim", "st_h", "st_l"] + ["f_%d" % t for t in range(NT)]
-SEMAPHORES = (["qv", "qs", "qt", "qg"] + DMASEMS + ["lm_1", "lm_2", "lm_3", "bulk0", "bulk1", "ha0", "ha1", "hls"]
-              + ["%s%d" % (n, t) for t in range(NT - 1) for n in ("upo", "upn", "lo", "ln")]
-              + ["uq%d_%d" % (s, t) for t in range(NT - 1) for s in (1, 3)])
+DMASEMS = ["l_comp", "l_ci2", "l_hd", "l_fa", "l_fb", "l_fc", "l_lim", "st_h", "st_l"]
+SEMAPHORES = (["qv", "qs", "qt", "qg"] + DMASEMS + ["lm_1", "lm_2", "lm_3", "bulk", "ha", "hls"]
+              + ["%s%d" % (n, t) for t in range(NT - 1) for n in ("hu", "lo", "uq1_", "uq2_", "uq3_")])
 
 
 def helpers(T, topo, core):
-    r = T.cores.index(core)
-    before, after = T.cores[(r - 1) % N], T.cores[(r + 1) % N]
-    cand = [c for c in topo.cores_of(core) if c not in T.cores and topo.may_write(c, before) and topo.may_write(c, after)]
-    near = [c for c in cand if topo.die(c) == topo.die(core)]
-    far = [c for c in cand if topo.die(c) != topo.die(core)]
-    return (near[0], far[0]), (near[1], far[1])
+    cand = [c for c in topo.cores_of(core) if c not in T.cores and all(topo.may_write(c, d) for d in T.cores)]
+    return [c for c in cand if topo.die(c) == topo.die(core)] + [c for c in cand if topo.die(c) != topo.die(core)]
+
+
+def share(es, i, n):
+    k = len(es) // n
+    return sum(1 << e for e in es[i * k:(i + 1) * k])
 
 
 def helper_program(g, core, T, topo):
     S = T.sem
-    for rank in T.cores:
-        if core not in topo.cores_of(rank):
+    for r, rank in enumerate(T.cores):
+        hs = helpers(T, topo, rank)
+        if core not in hs:
             continue
-        r = T.cores.index(rank)
-        for hs, dst, slot in zip(helpers(T, topo, rank), (T.cores[(r - 1) % N], T.cores[(r + 1) % N]), (1, 3)):
-            if core not in hs:
-                continue
-            half = hs.index(core)
+        i = hs.index(core)
+        ls = [0]
+
+        def hand(s, out, src, sem):
+            dst = T.cores[(r - s) % N]
             rid, pid = topo.addr(dst, core)
-            mask = topo.mask(core, dst)
-            ne = len(topo.engines(core, dst))
-            ls = 0
-            for p in range(2):
-                g.wait_ge(S["ha%d" % p], len(topo.engines(rank, core)) // 2)
-                c0 = half * 2 * PIECE + p * PIECE
-                g.remote_dma(T["lm%d" % slot][:, c0:c0 + PIECE], T.hl[:, p * PIECE:(p + 1) * PIECE], S["lm_%d" % slot], S.hls, pid, rid, mask)
-                ls += ne
-            if half == 0:
-                up = len(topo.engines(rank, T.cores[(r + 2) % N]))
-                for t in range(NT - 1):
-                    for sem, n, h in (("upo", "ro", "ho"), ("upn", "rn", "hn")):
-                        g.wait_ge(S["%s%d" % (sem, t)], up)
-                        g.remote_dma(T["%s%d_%d" % (n, slot, t)][:, :], T["%s%d" % (h, t)][:, :], S["uq%d_%d" % (slot, t)], S.hls, pid, rid, mask)
-                        ls += ne
-            g.wait_ge(S.hls, ls)
+            g.remote_dma(out, src, S[sem], S.hls, pid, rid, topo.mask(core, dst))
+            ls[0] += len(topo.engines(core, dst))
+        g.wait_ge(S.ha, len(topo.engines(rank, core)) // len(hs))
+        for s in range(1, N):
+            hand(s, T["lm%d" % s][:, i * Q4:(i + 1) * Q4], T.hl[:, :], "lm_%d" % s)
+        if i < 2:
+            s = (1, 3)[i]
+            for t in range(NT - 1):
+                g.wait_ge(S["hu%d" % t], len(topo.engines(rank, core)) // 4)
+                hand(s, T["ru%d_%d" % (s, t)][:, :], T["hu%d" % t][:, :], "uq%d_%d" % (s, t))
+        g.wait_ge(S.hls, ls[0])
 
 
 def rank_program(g, core, T, topo):
@@ -152,6 +150,8 @@ def rank_program(g, core, T, topo):
             o, w = 0, t.shape[1]
         if hi is None:
             hi = w
+        if st == -1:
+            return (t[:, o + hi - 1:(o + lo - 1 if o + lo else None):-1], n, lo, hi)
         return (t[:, o + lo:o + hi:st] if st != 1 else t[:, o + lo:o + hi], n, lo, hi)
 
     def X3(n, a, b, lo=0, hi=None):
@@ -162,11 +162,9 @@ def rank_program(g, core, T, topo):
         w = T[n].shape[2]
         return (T[n][:, a:b, i], n, a * w, b * w)
 
-    def HL(n, b, lo, hi):
-        return (T[n][:, b, lo:hi], n, 8 * b + lo, 8 * b + hi)
-
-    def PB(b, a, z):
-        return X3("pb%d" % b, a, z)
+    def XR(n, a, lo, hi):
+        w = T[n].shape[2]
+        return (T[n][:, a, lo:hi], n, a * w + lo, a * w + hi)
 
     def IND(win, off):
         return (win[0].indirect(off[0]), win, off)
@@ -180,18 +178,25 @@ def rank_program(g, core, T, topo):
             k *= d
         return k
 
-    def add(q, busy, fire, reads, writes, sem=None, cnt=0, lat=0.0, extra=()):
+    def short(*aps):
+        return all(_BYTES[SCRATCH[POOL[a[1]][0] if a[1] in POOL else a[1]][2]] == 2 for a in aps)
+
+    def add(q, busy, fire, reads, writes, sem=None, cnt=0, lat=0.0, extra=(), team=None):
         i = len(ops)
-        deps = set(extra)
+        deps, after = set(extra), set()
         acc = [(x, 0) for x in reads] + [(x, 1) for x in writes]
         for (ap, n, lo, hi), w in acc:
             past = hist.get(n, ([], []))
             for (j, jw, jlo, jhi, jq) in (past[0] + past[1] if w or n in psum else past[1]):
-                if n in psum and jq != q or jhi > lo and jlo < hi and (w or jw):
+                if n in psum and jq == q == "t":
+                    after.add(j)
+                elif team and ops[j]["team"] == team:
+                    continue
+                elif n in psum and jq != q or jhi > lo and jlo < hi and (w or jw):
                     deps.add(j)
         for (ap, n, lo, hi), w in acc:
             hist.setdefault(n, ([], []))[w].append((i, w, lo, hi, q))
-        ops.append({"q": q, "busy": busy, "fire": fire, "deps": deps - {i}, "sem": sem, "cnt": cnt, "lat": lat})
+        ops.append({"q": q, "busy": busy, "fire": fire, "deps": deps - {i}, "after": after - deps - {i}, "sem": sem, "cnt": cnt, "lat": lat, "team": team})
         return i
 
     def vc(n, f):
@@ -199,10 +204,10 @@ def rank_program(g, core, T, topo):
 
     def tt(out, a, b, op):
         if len(a) == 3:
-            return add("v", 50 + vc(size(b), GV), lambda: V.tensor_tensor(out[0], a[0], b[0], op), split(a) + [b], [out])
+            return add("v", 50 + vc(size(b), GA), lambda: V.tensor_tensor(out[0], a[0], b[0], op), split(a) + [b], [out])
         return add("v", vc(size(out), 1 if (a[1] in psum or b[1] in psum) else 2), lambda: V.tensor_tensor(out[0], a[0], b[0], op), [a, b], [out])
 
-    def ts(out, a, s1, s2, o1, o2=None, fast=False):
+    def ts(out, a, s1, s2, o1, o2=None):
         rd = [a] + [s for s in (s1, s2) if isinstance(s, tuple)]
         v1 = s1[0] if isinstance(s1, tuple) else s1
         v2 = s2[0] if isinstance(s2, tuple) else s2
@@ -210,36 +215,39 @@ def rank_program(g, core, T, topo):
             fn = lambda: V.tensor_scalar(out[0], a[0], v1, None, o1)
         else:
             fn = lambda: V.tensor_scalar(out[0], a[0], v1, v2, o1, o2)
-        return add("v", vc(size(out), 0.5 if fast else 1), fn, rd, [out])
+        return add("v", vc(size(out), 0.5 if short(out, a) else 1), fn, rd, [out])
 
     def cp(out, a):
         if len(a) == 3:
-            return add("v", 50 + vc(size(out), GS), lambda: V.tensor_copy(out[0], a[0]), split(a), [out])
+            return add("v", 50 + vc(size(out), GA), lambda: V.tensor_copy(out[0], a[0]), split(a), [out])
         if len(out) == 3:
-            return add("v", 50 + vc(size(a), 3.5), lambda: V.tensor_copy(out[0], a[0]), [a, out[2]], [out[1]])
-        return add("v", vc(size(out), 1), lambda: V.tensor_copy(out[0], a[0]), [a], [out])
+            return add("v", 50 + vc(size(a), SC), lambda: V.tensor_copy(out[0], a[0]), [a, out[2]], [out[1]])
+        return add("v", vc(size(out), 0.5 if short(out, a) else 1), lambda: V.tensor_copy(out[0], a[0]), [a], [out])
 
     def ms(out, c):
-        return add("v", vc(size(out), 1), lambda: V.memset(out[0], c), [], [out])
+        return add("v", vc(size(out), 0.5 if short(out) else 1), lambda: V.memset(out[0], c), [], [out])
 
-    def act(out, a, func, bias=0.0, scale=1.0, acc=None):
-        cost = 65 + vc(size(out), GS) if len(a) == 3 else 60 + vc(size(out), 1)
-        if acc:
-            fn = lambda: C.activation(out[0], a[0], func, bias=bias, scale=scale, accum_out=acc[0])
-        else:
-            fn = lambda: C.activation(out[0], a[0], func, bias=bias, scale=scale)
-        return add("s", cost, fn, split(a), [out] + ([acc] if acc else []))
+    def scan(out, a, b, init, o1, o2):
+        return add("v", vc(size(out), 0.5 if short(out, a, b) else 1), lambda: V.tensor_tensor_scan(out[0], a[0], b[0], init, o1, o2), [a, b], [out])
 
-    def mm(lst):
+    def act(out, a, func=AF.Copy, bias=0.0, scale=1.0):
+        cost = 65 + vc(size(out), GA) if len(a) == 3 else 60 + vc(size(out), 1)
+        cols = [s for s in (bias, scale) if isinstance(s, tuple)]
+        bv = bias[0] if isinstance(bias, tuple) else bias
+        sv = scale[0] if isinstance(scale, tuple) else scale
+        return add("s", cost, lambda: C.activation(out[0], a[0], func, bias=bv, scale=sv), split(a) + cols, [out])
+
+    def mm(lst, first=True, last=True, apart=False):
         rd, wr = {}, {}
-        for o, l, x, s0, s1 in lst:
+        for o, l, x in lst:
             rd[l[1:]], rd[x[1:]], wr[o[1:]] = l, x, o
 
         def fire():
-            for o, l, x, s0, s1 in lst:
-                ins = M.matmul(o[0], l[0], x[0], s0, s1)
+            for i, (o, l, x) in enumerate(lst):
+                ins = M.matmul(o[0], l[0], x[0], apart or first and i == 0, apart or last and i == len(lst) - 1)
             return ins
-        return add("t", sum(max(64.0, size(x[2])) for x in lst) * PCY, fire, list(rd.values()), list(wr.values()))
+        cost = sum(max(64.0, size(x)) * (1 if short(x) else 4) for o, l, x in lst) * PCY
+        return add("t", cost, fire, list(rd.values()), list(wr.values()))
 
     def dma(q, out, in_, sem, lat):
         e = {"y": Y, "s": C}[q]
@@ -248,330 +256,293 @@ def rank_program(g, core, T, topo):
         src, dst_ = (in_[0] if rd else in_), (out[0] if wr else out)
         return add(q, 60, lambda: e.dma_start(dst_, src), rd, wr, sem=sem, cnt=16, lat=lat)
 
-    ha, hb = helpers(T, topo, core)
+    hs = helpers(T, topo, core)
     opp = T.cores[(r + 2) % N]
-    mo = topo.mask(core, opp)
-    no = len(topo.engines(core, opp))
+    near = topo.engines(core, hs[0])
+    far = topo.engines(core, opp)
 
     def dst(c):
         rid, pid = topo.addr(c, core)
         return DstId(rid=rid, pnc=pid)
 
-    def pair(hs, p):
-        tr = []
-        for h in range(2):
-            es = topo.engines(core, hs[h])
-            k = len(es) // 2
-            c0 = (2 * h + p) * PIECE
-            tr.append(RemoteDMATransfer(dst_ids=[dst(hs[h])], dma_engine_mask=sum(1 << e for e in es[h * k:(h + 1) * k]), remote_sem=S["ha%d" % p],
-                                        srcs=[T.lm0[:, c0:c0 + PIECE]], dsts=[T.hl[:, p * PIECE:(p + 1) * PIECE]]))
-        return lambda: g.remote_dma_fused(tr, local_sem=S.bulk0)
-
-    dma("y", X("ci", 0, 256), T.comp[:, 0:256], "l_comp", 2000)
-    dma("s", X("lm0", 0, H), T.lim[:, :], "l_lim", 3500)
-    dma("y", X("ft"), T.feat[:, :], "l_ft", 3500)
-    ms(X("hdi"), 0)
-    add("y", 60, lambda: Y.dma_start(T.hdi[0:128:16, :], T.hd[:, :]), [], [X("hdi")], sem="l_hd", cnt=16, lat=2000)
-    dma("y", X3("fv3", 0, 48), T.feat[:, P0:2048], "l_fv", 2300)
-    dma("s", X("ci", 256, 768), T.comp[:, 256:768], "l_ci2", 2500)
-    add("g", 560, lambda: g.iota(X("io")[0], [[1, 256]], 0, 0), [], [X("io")])
-    add("g", 140, lambda: g.iota(X("pi")[0], [[0, 1]], 0, 1), [], [X("pi")])
+    F0, F1 = P0 + B, 2048
+    dma("y", X("hdi"), T.hd[:, :], "l_hd", 1900)
+    dma("s", X("ci", 0, B), T.comp[:, 0:B], "l_comp", 2300)
+    dma("y", X("ft", P0, F0), T.feat[:, P0:F0], "l_fa", 2600)
+    dma("s", X("lm0", 0, H), T.lim[:, :], "l_lim", 4500)
+    dma("y", X("ft", 0, P0), T.feat[:, 0:P0], "l_fb", 6000)
+    dma("s", X("ci", B, 768), T.comp[:, B:768], "l_ci2", 7500)
+    dma("y", X("ft", F0, F1), T.feat[:, F0:F1], "l_fc", 8000)
+    add("g", 430, lambda: g.iota(X("io")[0], [[1, 144]], 0, 0), [], [X("io")])
+    add("g", 200, lambda: g.iota(X("pi")[0], [[0, 1]], 0, 1), [], [X("pi")])
 
     cp(X("pf"), X("pi"))
-    ts(X("ri"), X("pi"), 15, None, A.bitwise_and)
+    cp(X("iof"), X("io"))
+    ts(X("idw"), X("iof"), X("pf"), None, A.is_equal)
+    ID, J, J8 = X("idw", 0, W), X("iof", 0, W), X("iof", 0, 8)
+    cp(X("hdf"), X("hdi"))
+    for z, (u0, u1) in enumerate(((0, 6), (6, 12), (12, 16))):
+        pd = "pd%d" % z
+        mm([(X(pd, 80 * (u - u0), 80 * (u - u0) + 80), X("idw", u, u + W), X("hdf")) for u in range(u0, u1)], apart=True)
+        act(X("htab", 80 * u0, 80 * u1), X(pd, 0, 80 * (u1 - u0)))
+    cp(X("cl", 0, B), X("ci", 0, B))
     ts(X("gi"), X("pi"), 4, None, A.logical_shift_right)
-    ts(X("pa"), X("pi"), 4, 1, A.logical_shift_right, A.bitwise_and)
-    cp(X("iof"), X("io", 0, 160))
-    cp(X("rf"), X("ri"))
     cp(X("gf"), X("gi"))
-    cp(X("par"), X("pa"))
-    ts(X("npar"), X("par"), -1.0, 1.0, A.mult, A.add)
-    ts(X("p16"), X("pf"), 16.0, None, A.add)
-    ts(X("b16"), X("gf"), 16.0, 16.0, A.mult, A.add)
-    ts(X("isr0"), X("rf"), 0.0, None, A.is_equal)
-    ts(X("idw"), X("iof"), X("p16"), None, A.is_equal)
-    ID = X("idw", 16, 144)
-
-    def SL(n, s):
-        return X(n, s, s + 128)
-    ts(X("pm0"), ID, X("npar"), None, A.mult, fast=True)
-    ts(X("pm1"), ID, X("par"), None, A.mult, fast=True)
-    ts(X("sw0"), SL("idw", 0), X("npar"), None, A.mult, fast=True)
-    ts(X("sw1"), SL("idw", 32), X("par"), None, A.mult, fast=True)
-    ts(X("r32"), X("idw"), X("isr0"), 32.0, A.mult, A.mult, fast=True)
-    for n, w in (("bwn", 19616.0), ("bws", 9808.0), ("bwp", 16.0), ("bwm", -16.0)):
-        ts(X(n), X("iof"), X("b16"), w, A.is_equal, A.mult)
-    for n, w in (("nid", -1.0), ("id32", 32.0), ("i613", 613.0), ("i612", 612.0), ("wi", 65536.0)):
-        act(X(n), ID, AF.Copy, scale=w)
-
-    def lists(t, b):
-        c0 = t * 256 + b * W
-        if b == 0:
-            cp(X("xf", t * 256, t * 256 + 256), X("ci", t * 256, t * 256 + 256))
-        run = []
-        for j in range(4):
-            o = X("pm", b * W + 16 * j, b * W + 16 * j + 16)
-            k = c0 // 16 + j
-            me, ot = X("xf", 16 * k, 16 * k + 16), X("xf", 16 * (k ^ 1), 16 * (k ^ 1) + 16)
-            run += [(o, X("pm%d" % (k & 1)), me, True, False), (o, X("sw%d" % (k & 1)), ot, False, True)]
-        mm(run)
-        tr, y = X("tr%d" % b), X("pm", b * W, b * W + W)
-        add("v", vc(W, 1), lambda: V.transpose(tr[0], y[0]), [y], [tr])
-        cp(X("cl", c0, c0 + W), tr)
-
-    lists(0, 0)
-    cp(X("htab", 0, P0), X("hdi"))
-    for b in range(1, NB):
-        lists(0, b)
+    ts(X("wh"), X("iof", 0, W, 16), X("pf"), 32.0, A.is_equal, A.mult)
+    for n, w in (("idq", 1.0 / 32), ("nid", -1.0), ("idf", 1.0), ("wi", 4096.0)):
+        ts(X(n), ID, w, None, A.mult)
+    for n, w in (("w1", 32.0 * 613), ("w2", float(BIG)), ("wp", 1.0), ("wm", -1.0)):
+        ts(X(n), J8, X("gf"), w, A.is_equal, A.mult)
+    ms(X("ones"), 1.0)
+    ts(X("cst"), X("idw", 1, 2), -9.0 * BIG, None, A.mult)
+    ts(X("ca"), X("idw", 2, 3), -256.0, X("cst"), A.mult, A.add)
+    ts(X("kq0"), X("ones"), X("ca"), None, A.mult)
+    for b in range(NB):
+        ms(X("ch%d" % b, W, W + 16), 0.0)
 
     def fr(t, eng):
-        for half, n in ((0, "fa%d" % t), (1, "fb%d" % t)):
-            a = 16 * t + 8 * half
+        n = "fr%d" % t
+        step = W if eng == "v" else B
+        for m0 in range(0, B, step):
+            i = X("ft", P0 + B * t + m0, P0 + B * t + m0 + step)
             for k in range(16):
-                o, i = T[n][:, :, 16 * k:16 * k + 16], T.fv3[:, a:a + 8, :]
-                q, cost, fn = {"v": ("v", vc(128, 0.5), lambda o=o, i=i: V.tensor_copy(o, i)),
-                               "s": ("s", 60 + vc(128, 1), lambda o=o, i=i: C.activation(o, i, AF.Copy)),
-                               "g": ("g", 170 + 256 * CY, lambda o=o, i=i: g.affine_select(o, i, [[0, 8], [0, 16]], A.is_gt, 0.0, 1, 0))}[eng[half]]
-                add(q, cost, fn, [X3("fv3", a, a + 8)], [(o, n, 128 * k, 128 * k + 128)])
-            if half == 0:
-                dma("y", X("fr%d" % t), X3(n, 0, 8), "f_%d" % t, 3500)
+                o = X(n, 16 * m0 + k, 16 * (m0 + step), 16)
+                if eng == "v":
+                    add("v", vc(step, 0.5), lambda o=o, i=i: V.tensor_copy(o[0], i[0]), [i], [o], team=n)
+                else:
+                    add("g", 170 + 2 * step * CY, lambda o=o, i=i: g.affine_select(o[0], i[0], [[0, step]], A.is_gt, 0.0, 1, 0), [i], [o], team=n)
 
-    fr(0, "vs")
-    ts(X("km"), X("io"), 15, None, A.bitwise_and)
-    cp(X("kf"), X("km"))
-    ts(X("c256"), X("kf", 0, W), 0.0, 256.0, A.mult, A.add)
-    ts(X("ones"), X("iof", 0, 128), 0.0, 1.0, A.mult, A.add)
-    ts(X("ta"), X("kf", 0, W), -1.0, 15.0, A.mult, A.add)
-    ts(X("tbn"), X("kf", 0, W), -2.0, 15.0, A.mult, A.add)
-    for t in range(NT):
-        ms(X("off%d" % t), 0)
+    fr(0, "v")
 
-    RL = X("lm0", 0, H)
-    nb = len(topo.engines(core, ha[0]))
-    rid, pid = topo.addr(opp, core)
-    for p in range(2):
-        add("g", 1200, pair(ha, p), [RL], [], sem="bulk0", cnt=nb, lat=3000)
-    add("g", 1200, lambda: g.remote_dma(T.lm2[:, 0:H], T.lm0[:, 0:H], S.lm_2, S.bulk1, pid, rid, mo), [RL], [], sem="bulk1", cnt=no, lat=6000)
-    for p in range(2):
-        add("g", 1200, pair(hb, p), [RL], [], sem="bulk0", cnt=nb, lat=3000)
-    for s, at in ((1, 14000), (2, 16000), (3, 20000)):
-        src = T.cores[(r + s) % N]
-        if s == 2:
-            cnt = len(topo.engines(src, core))
-        else:
-            cnt = sum(2 * len(topo.engines(h, core)) for h in helpers(T, topo, src)[0 if s == 1 else 1])
+    tr = [RemoteDMATransfer(dst_ids=[dst(h)], dma_engine_mask=share(near, i, len(hs)), remote_sem=S.ha,
+                            srcs=[T.lm0[:, i * Q4:(i + 1) * Q4]], dsts=[T.hl[:, :]]) for i, h in enumerate(hs)]
+    add("g", 2500, lambda: g.remote_dma_fused(tr, local_sem=S.bulk), [X("lm0", 0, H)], [], sem="bulk", cnt=len(near), lat=3000)
+    for s, at in ((1, 15000), (2, 19000), (3, 23000)):
+        cnt = sum(len(topo.engines(h, core)) for h in helpers(T, topo, T.cores[(r + s) % N]))
         add("x", 0, None, [], [X("lm%d" % s, 0, H)], sem="lm_%d" % s, cnt=cnt, lat=at)
-    for t in (1, 2):
-        fr(t, "gg")
+    fr(1, "g")
+    fr(2, "g")
 
     def late():
-        onb = X("onb")
-        ms(onb, 1.0)
-        ts(X("rsa"), X("kf", 0, 128), 0.0, -2.0e9, A.is_equal, A.mult)
-        ts(X("rst"), X("rsa"), 1.0e9, None, A.add)
-        ts(X("maskc"), X("kf", 0, W), X("rf"), 4096.0, A.is_ge, A.mult)
+        cp(X("cl", B, 768), X("ci", B, 768))
+        ts(X("km"), X("io", 0, W), 15, None, A.bitwise_and)
+        cp(X("kf"), X("km"))
+        act(X("keep"), X("kf"), AF.Sigmoid, bias=-128.0, scale=256.0)
+        ts(X("rsa"), X("keep"), 2.0e9, -1.0e9, A.mult, A.add)
+        ts(X("rsb"), X("keep"), -2.0e9, 1.0e9, A.mult, A.add)
+        ts(X("on32"), X("ones"), 1.0 / 32, None, A.mult)
+        ts(X("p0m"), X("ones"), X("idw", 0, 1), 32.0, A.mult, A.mult)
         for b in range(NB):
-            ts(X("cf%d" % b, 0, 8), X("iof", 0, 8), 0.0, None, A.mult)
-        ts(X("d2048"), X("rf"), 2048.0, None, A.add)
-        ts(X("dumm"), X("iof", 0, 16), 16.0, X("d2048"), A.mult, A.add)
-        for j in range(16):
-            o = X("ub", 128 * j, 128 * j + 128)
-            add("g", 170 + 256 * CY, lambda o=o, j=j: g.affine_select(o[0], onb[0], [[-16, 8], [0, 16]], A.is_equal, 0.0, -j, 1), [onb], [o])
+            ms(X("lz%d" % b), 0.0)
+            ms(X("dz%d" % b), 0.0)
+            ms(X("wz%d" % b), 0.0)
+            ts(X("dmy%d" % b), X("pf"), 2.0, float(H + 2 * W * b), A.mult, A.add)
+        for t in range(NT):
+            ms(X("up%d" % t, B + 16, UP), 0.0)
+        ts(X("hf"), X("keep"), 0.5, None, A.mult)
+        ts(X("st"), X("keep"), -1.0, 1.0, A.mult, A.add)
+        scan(X("rwa"), X("hf"), X("st"), 0.0, A.mult, A.add)
+        ts(X("hf"), X("ones"), 0.5, None, A.mult)
+        ts(X("st"), X("keep"), 0.0, None, A.mult)
+        scan(X("rwb"), X("hf"), X("st"), 2.0 ** 57, A.mult, A.add)
+        ts(X("e0", 0, 1), X("idw", 0, 1), 1.0, None, A.mult)
+        ts(X("e0", 1, 2), X("idw", 0, 1), 2.5, None, A.mult)
+        mm([(XR("pk0", 0, 0, 1), X("rwa"), X("e0", 0, 1))])
+        mm([(XR("pk0", 0, 1, 2), X("rwb"), X("e0", 1, 2))])
+        ts(X("wu"), X("wp"), XR("pk0", 0, 0, 1), None, A.mult)
+        cp(X("thr"), XR("pk0", 0, 1, 2))
 
     rot = [0]
 
-    def diff(t, b, xg, out, func, bias):
-        for h in range(2):
-            d = X("pd%d" % rot[0])
-            rot[0] ^= 1
-            a = (b % 2) * 4 + 2 * h
-            n = ("fa%d" if b < 2 else "fb%d") % t
-            mm([(d, ID, (T[n][:, a:a + 2, :], n, 0, 2048), True, False), (d, X("nid"), X(xg, 512 * h, 512 * h + 512), False, True)])
-            act(X(out, 512 * h, 512 * h + 512), d, func, bias=bias)
+    def parts(lo, hi, most):
+        n = -(-(hi - lo) // most)
+        step = -(-(hi - lo) // (32 * n)) * 32
+        return [(a, min(a + step, hi)) for a in range(lo, hi, step)]
 
-    def col(n, j):
-        return X(n, j, 1024, 16)
+    def col(n, k):
+        return X(n, k, E, 16)
 
-    def halves(n, c0=0):
-        return [(X(n, c0 + 32 * z, c0 + 32 * z + 32), 512 * z, 512 * z + 512) for z in range(2)]
+    def offs(n, c0, lo, hi):
+        return X(n, c0 + lo // 16, c0 + hi // 16)
 
     def shares(t, b):
-        mn, win = "mn%d" % b, X("ft", 0, P0 + B * t)
-        o = X("pm", 256 + W * b, 320 + W * b)
-        vp = b in VB
-        for cl, lo, hi in halves("cl", t * 256 + b * W):
-            if vp:
-                tt(X(mn, lo, hi), IND(win, cl), X("fr%d" % t, 1024 * b + lo, 1024 * b + hi), A.min)
-            else:
-                act(X("mx%d" % b, lo, hi), IND(win, cl), AF.Copy)
-        if not vp:
-            diff(t, b, "mx%d" % b, mn, AF.Relu, 0.0)
-        mm([(o, ID, X("ta"), True, False)] + [(o, SL("bwp" if vp else "bwm", 16 - j), col(mn, j), False, j == 15) for j in range(16)])
-        ss = "ss%d_%d" % (t, b)
-        act(X(ss, 0, W), o, AF.Copy)
-        tt(X(ss, W, 2 * W), X("tbn"), o, A.subtract)
+        mn, win, c0 = "mn%d_%d" % (t, b), X("ft", 0, P0 + B * t), B * t + W * b
+        if b not in SSH:
+            for lo, hi in parts(0, E, VCH):
+                tt(X(mn, lo, hi), IND(win, offs("cl", c0, lo, hi)), X("fr%d" % t, E * b + lo, E * b + hi), A.min)
+            return
+        for i, (lo, hi) in enumerate(parts(0, E, 512)):
+            x, d = X("mx", 512 * (i % 2), 512 * (i % 2) + 512), X("pd3")
+            act(x, IND(win, offs("cl", c0, lo, hi)))
+            mm([(d, ID, X("fr%d" % t, E * b + lo, E * b + hi)), (d, X("nid"), x)])
+            act(X(mn, lo, hi), d, AF.Relu)
+
+    def to_list(b):
+        px = "px%d" % b
+        mm([(X3(px, 0, 8, 16, 32), X("ch%d" % b, 0, W), X("idq"))])
+        cp(X("ul%d" % b), X3(px, 0, 8, 16, 32))
 
     def heads(t, b):
-        win, cl = X("htab", 0, P0 + B * t), X("cl", t * 256 + b * W, t * 256 + b * W + W)
-        if b in HV:
-            cp(X("hx%d" % b), IND(win, cl))
-        else:
-            act(X("hx%d" % b), IND(win, cl), AF.Copy)
-        mm([(PB(b, 0, 2), SL("r32", 16 - j), col("hx%d" % b, j), j == 0, j == 15) for j in range(16)])
-        ts(X("ul%d" % b), PB(b, 0, 2), 1.0 / 32, None, A.mult)
-        act(X("sq%d" % b), PB(b, 0, 2), AF.Square, bias=16.0, scale=1.0 / 32)
+        win, hx, px, c0 = X("htab", 0, P0 + B * t), "hx%d" % b, "px%d" % b, B * t + W * b
+        hv = HV if b == 0 else 0
+        for lo, hi in parts(0, hv, VCH) if hv else []:
+            cp(X(hx, lo, hi), IND(win, offs("cl", c0, lo, hi)))
+        for lo, hi in parts(hv, E, HCH):
+            act(X(hx, lo, hi), IND(win, offs("cl", c0, lo, hi)))
+        mm([(XI(px, 0, 8, k), col(hx, k), X("wh")) for k in range(16)], apart=True)
+        cp(X("ch%d" % b, 0, W), X3(px, 0, 8, 0, 16))
+        to_list(b)
 
     def visit(t, b, a):
-        lm, cm = X("lm%d" % a, 0, H), "cm%d" % b
-        run = [(X("kq%d" % a), X("ones", 0, W))] if t else []
-        if b in VB:
-            for ul, lo, hi in halves("ul%d" % b):
-                tt(X(cm, lo, hi), IND(lm, ul), X("fr%d" % t, 1024 * b + lo, 1024 * b + hi), A.is_lt)
-            bw = "bwn"
-            if not t:
-                run.append((X("nid"), X("c256")))
-        else:
-            for ul, lo, hi in halves("ul%d" % b):
-                act(X("xg%d" % b, lo, hi), IND(lm, ul), AF.Copy)
-            diff(t, b, "xg%d" % b, cm, AF.Sign, -0.5)
-            bw = "bws"
-            run.append((X("i613" if t else "i612"), X("c256")))
-        run += [(SL(bw, 16 - j), col(cm, j)) for j in range(16)]
-        mm([(PB(b, 2, 4), l, x, i == 0, i == len(run) - 1) for i, (l, x) in enumerate(run)])
-        ts(X("tc%d" % b), PB(b, 2, 4), 170000.0, 16777216.0, A.is_ge, A.mult)
-        tt(PB(b, 4, 6), X("sq%d" % b), PB(b, 2, 4), A.add)
-        tt(X("tb%d" % b), X("tc%d" % b), PB(b, 0, 2), A.add)
-        tt(X("mi%d" % b), X("tb%d" % b), PB(b, 4, 6), A.min)
-        ts(X("mj%d" % b), X("mi%d" % b), 5, 2047, A.arith_shift_right, A.bitwise_and)
+        lm, cm, px, fr_ = X("lm%d" % a, 0, H), "cm%d" % b, "px%d" % b, "fr%d" % t
+        x, ch = X3(px, 0, 8, 0, 16), X("ch%d" % b, 0, W)
+        act(X("sq%d" % b), ch, AF.Square, bias=16.0, scale=1.0 / 32)
+        mm([(x, X("idf"), X("sq%d" % b)), (x, X("kq%d" % (a if t else 0)), X("ones"))], last=False)
+        todo = []
+        for lo, hi in parts(E - NS, E, 512):
+            xg, d = X("xg%d" % b, lo - E + NS, hi - E + NS), bank(hi - lo)
+            act(xg, IND(lm, offs("ul%d" % b, 0, lo, hi)))
+            mm([(d, ID, X(fr_, E * b + lo, E * b + hi)), (d, X("nid"), xg)])
+            todo.append((X(cm, lo, hi), d))
+        for o, d in todo:
+            act(o, d, AF.Sigmoid, bias=-128.0, scale=256.0)
+        for lo, hi in parts(0, E - NS, VCH):
+            tt(X(cm, lo, hi), IND(lm, offs("ul%d" % b, 0, lo, hi)), X(fr_, E * b + lo, E * b + hi), A.is_lt)
+        mm([(XI(px, 0, 8, k), col(cm, k), X(w)) for k in range(16) for w in ("w1", "w2")], first=False)
+        tt(X("mi%d" % b), x, ch, A.max)
+        ts(X("mj%d" % b), X("mi%d" % b), 32 * (H - 1), None, A.bitwise_and)
+        cp(ch, X("mj%d" % b))
         if a < N - 1:
-            cp(X("ul%d" % b), X("mj%d" % b))
-        cp(X("cf%d" % b, 8, 72), X("mj%d" % b))
-        if a < N - 1:
-            mm([(PB(b, 0, 2), X("id32"), X("cf%d" % b, 8, 72), True, True)])
-            act(X("sq%d" % b), PB(b, 0, 2), AF.Square, bias=16.0, scale=1.0 / 32)
+            to_list(b)
+
+    def lists(out, pad, idn):
+        mm([(out, X(pad, 15 - u, 15 - u + W), X(idn, u, W, 16)) for u in range(16)])
+
+    def sums(t, b):
+        pk = "pk%d" % b
+        mm([(X3(pk, 0, 8), X("wi"), X("ones"))] + [(XI(pk, 0, 8, k), col("mn%d_%d" % (t, b), k), X("wm" if b in SSH else "wp")) for k in range(16)], last=False)
+
+    def bank(n):
+        rot[0] = (rot[0] + 1) % 3
+        return X("pd%d" % rot[0], 0, n)
 
     def elect(t, b):
-        cf, eb, pb = "cf%d" % b, "eb%d" % b, "pb%d" % b
-        c, pm, de = X(cf, 8, 72), X3(pb, 10, 14, 0, 16), X("de%d" % b)
-        mm([(X3(pb, 6, 10, 0, 16), ID, c, True, True), (X3(pb, 6, 10, 16, 32), ID, c, True, True)])
+        px, pk, eb, ch = "px%d" % b, "pk%d" % b, "eb%d" % b, X("ch%d" % b, 0, W)
+        key, de = X3(pk, 0, 8), bank(W)
+        mm([(X3(px, 8, 16, 0, 16), ID, ch), (X3(px, 8, 16, 16, 32), ID, ch)], apart=True)
+        mm([(de, ID, X("ch%d" % b, 1, W + 1)), (de, X("nid"), ch)])
+        act(X("de%d" % b), de)
         for d in range(1, 9):
-            tt(X3(eb, 4 * d - 4, 4 * d), c, X3(pb, 6, 10, d, d + 16), A.is_equal)
-        tt(de, X(cf, 7, 71), c, A.subtract)
-        run = []
-        for d in range(1, 9):
-            run.append((pm, X3(eb, 4 * d - 4, 4 * d)))
-            if d < 8:
-                run.append((X3(pb, 10, 14, d, 16), X3(eb, 4 * d - 4, 4 * d, 0, 16 - d)))
-                run.append((X3(pb, 10, 14, 0, d), X3(eb, 4 * d - 4, 4 * d, 16 - d, 16)))
-        mm([(o, X("wi"), x, i == 0, i == len(run) - 1) for i, (o, x) in enumerate(run)])
-        ss = "ss%d_%d" % (t, b)
-        kk, rr, nr, rst = X("pe", 128 * b, 128 * b + 128), X("rr%d" % b), X("nr%d" % b), X("rst")
-        tt(X("pe", 128 * b, 128 * b + W), X(ss, 0, W), pm, A.add)
-        tt(X("pe", 128 * b + W, 128 * b + 2 * W), X(ss, W, 2 * W), pm, A.subtract)
-        add("v", vc(128, 1), lambda: V.tensor_tensor_scan(rr[0], rst[0], kk[0], 0.0, A.min, A.max), [rst, kk], [rr])
-        tt(nr, rr, kk, A.not_equal)
-        for h in range(2):
-            n, y = X("nr%d" % b, W * h, W * h + W), X("yy%d" % b, W * h, W * h + W)
-            add("v", vc(W, 1), lambda n=n, y=y: V.tensor_tensor_scan(y[0], de[0], n[0], 0.0, A.add, A.mult), [de, n], [y])
-        c15, hl = X(cf, 23, 72, 16), "hlb%d" % t
-        tt(HL(hl, b, 0, 4), X("yy%d" % b, 15, 64, 16), c15, A.add)
-        tt(HL(hl, b, 4, 8), X("yy%d" % b, 79, 128, 16), c15, A.add)
-        tt(X("lf%d" % t, 4 * b, 4 * b + 4), X("yy%d" % b, 79, 128, 16), c15, A.add)
-        mm([(XI(pb, 0, 8, j), X("ub", 128 * j, 128 * j + 128), HL(hl, b, 0, 8), True, True) for j in range(16)])
-        c0 = P0 + B * t + W * b
-        act(X("htab", c0, c0 + W), X3(pb, 0, 4, 0, 16), AF.Copy)
+            e = X3(eb, 8 * d - 8, 8 * d)
+            tt(e, ch, X3(px, 8, 16, d, d + 16), A.is_equal)
+        for ds in ((1, 2), (3, 4), (5, 6), (7,), (8,)):
+            run = []
+            for d in ds:
+                run.append((key, X("wi"), X3(eb, 8 * d - 8, 8 * d)))
+                if d < 8:
+                    run.append((X3(pk, 0, 8, d, 16), X("wi"), X3(eb, 8 * d - 8, 8 * d, 0, 16 - d)))
+                    run.append((X3(pk, 0, 8, 0, d), X("wi"), X3(eb, 8 * d - 8, 8 * d, 16 - d, 16)))
+            mm(run, first=False, last=8 in ds)
+        act(X("sq%d" % b), key)
+        back = X("sq%d" % b, 0, W, -1)
+        for h, (rs, o1, o2) in enumerate((("rsa", A.min, A.max), ("rsb", A.max, A.min))):
+            lo, hi = W * h, W * h + W
+            scan(X("rr%d" % b, lo, hi, -1), X(rs), back, 0.0, o1, o2)
+            tt(X("nr%d" % b, lo, hi), X("rr%d" % b, lo, hi), key, A.not_equal)
+            scan(X("yy%d" % b, lo, hi, -1), X("de%d" % b, 0, W, -1), X("nr%d" % b, lo, hi, -1), 0.0, A.add, A.mult)
+            out = X("lz%d" % b, 15, 15 + W, 16) if h else X("wz%d" % b, 0, W, 16)
+            tt(out, X("yy%d" % b, lo, hi, 16), X("ch%d" % b, 0, W, 16), A.add)
+            if h == 0:
+                c0 = P0 + B * t + W * b
+                mm([(X3(px, 0, 8, 0, 16), X("wz%d" % b), X("idq"))])
+                act(X("htab", c0, c0 + W), X3(px, 0, 8, 0, 16))
+        scan(X("lr%d" % b), X("keep"), X("lz%d" % b, 15, 15 + W), 0.0, A.mult, A.add)
+        mm([(X3(px, 0, 8, 16, 32), X("lr%d" % b), X("idq"))])
+        cp(X("lbs", W * b, W * b + W), X3(px, 0, 8, 16, 32))
+        lists(XR(pk, 16, 0, 8), "lz%d" % b, "idq")
+        cp(X("lf", 8 * b, 8 * b + 8), XR(pk, 16, 0, 8))
 
-    def compare(t, b):
-        lf, pl = "lf%d" % t, X3("pb%d" % b, 4, 8, 0, 16)
-        cp(X("lu%d" % t, 4 * b, 4 * b + 4), X(lf, 4 * b, 4 * b + 4))
-        tt(X("lbm", W * b, W * b + W), X("maskc"), pl, A.add)
-        act(X("lbs", W * b, W * b + W), pl, AF.Copy)
-        for j in range(4 * b, 4 * b + 4):
-            def o(lo, hi):
-                return (T.ind[:, j, lo:hi], "ind", 272 * j + lo, 272 * j + hi)
-            if j:
-                ts(o(256 - 16 * j, 256), X("lbs", 0, 16 * j), X(lf, j, j + 1), 4096.0, A.is_equal, A.mult, fast=True)
-            ts(o(256, 272), X("lbm", 16 * j, 16 * j + 16), X(lf, j, j + 1), 4096.0, A.is_equal, A.mult, fast=True)
-            i, d = o(256 - 16 * j, 272), X("dup", j, j + 1)
-            if j in RV:
-                add("v", vc(16 * j + 16, 1), lambda i=i, d=d: V.tensor_reduce(d[0], i[0], AxisListType.X, A.add), [i], [d])
-            else:
-                act(i, i, AF.Copy, acc=d)
+    def compare(b):
+        row, pk = X("lbs", W * b, W * b + W), "pk%d" % b
+        o, run = XR(pk, 17, 0, 8), []
+        for a in range(8 * b + 8):
+            i = X("ind", W * (8 * b + a), W * (8 * b + a + 1))
+            ts(i, row, X("lf", a, a + 1), 2.0 ** (56 - 16 * (a - 8 * b)) if a >= 8 * b else 2.0 ** 80, A.is_equal, A.mult)
+            run.append((o, i, X("wu")))
+        mm(run)
+        ts(X("dz%d" % b, 15, 15 + W, 16), o, X("thr"), X("dmy%d" % b), A.is_ge, A.mult)
+        lists(XR("pk0", 1, 8 * b, 8 * b + 8), "dz%d" % b, "idw")
+
+    def kq(s, k):
+        act(X("kc%d" % s), k)
+        act(X("kq%d" % s), X("p0m"), AF.Identity, bias=X("ca"), scale=X("kc%d" % s))
 
     def kappa(t):
-        o, ks = (T.pb0[:, 0, 0:16], "pb0", 0, 32), X("ks")
-        mm([(o, X("ones"), (T["hlb%d" % t][:, :, 0:4], "hlb%d" % t, 0, 32), True, True)])
-        add("v", vc(16, 1), lambda: V.tensor_reduce(ks[0], o[0], AxisListType.X, A.add), [o], [ks])
+        o, ks, k = XR("pk0", 19, 0, 8), X("ks"), X("up%d" % t, B + 16, B + 17)
+        mm([(o, X("on32"), X("wz%d" % b, 0, W, 16)) for b in range(NB)])
+        add("v", vc(8, 1), lambda: V.tensor_reduce(ks[0], o[0], AxisListType.X, A.add), [o], [ks])
         cp(X("ki"), ks)
         ts(X("kj"), X("ki"), 255, None, A.bitwise_and)
-        cp(X("off%d" % t, 16, 17), X("kj"))
-        ts(X("kc0"), X("kj"), 32.0, -256.0, A.mult, A.add)
-        ts(X("kq0"), ID, X("kc0"), None, A.mult, fast=True)
+        cp(k, X("kj"))
+        kq(0, k)
 
-    def scat(a, new, off):
-        cp(IND(X("lm%d" % a, 0, H + B), off), new)
+    def scat(s, up):
+        cp(X("ou%d" % s), X(up, B, B + 16))
+        cp(IND(X("lm%d" % s), X("ou%d" % s)), X(up, 0, B))
 
-    def losers(t):
-        lf = "lf%d" % t
-        act(X("old"), IND(X("lm0", 0, H), X("lu%d" % t)), AF.Copy)
-        tt(X("dif"), X("ft", P0 + B * t, P0 + B * t + B), X("old"), A.subtract)
-        ts(X("clp"), X("dif"), -32.0, 32.0, A.max, A.min, fast=True)
-        tt(X("new%d" % t), X("old"), X("clp"), A.add)
-        tt(X("du1"), X("dup"), X("dumm"), A.min)
-        tt(X("du2"), X("du1"), X(lf), A.max)
-        cp(X("off%d" % t, 0, 16), X("du2"))
-        scat(0, X("new%d" % t), X("off%d" % t, 0, 16))
+    def changes(t):
+        up, old, dif, new = "up%d" % t, X("old"), bank(B), bank(B)
+        cp(X("lu"), X("lf"))
+        act(old, IND(X("lm0", 0, H), X("lu")))
+        mm([(dif, ID, X("ft", P0 + B * t, P0 + B * t + B)), (dif, X("nid"), old)])
+        ts(X("clp"), dif, -32.0, 32.0, A.max, A.min)
+        mm([(new, ID, old), (new, ID, X("clp"))])
+        act(X(up, 0, B), new)
 
     def send(t):
-        ids = [dst(c) for c in (opp, ha[0], hb[0])]
-
-        def call(src, bufs, sem, ls):
-            tr = [RemoteDMATransfer(dst_ids=ids, dma_engine_mask=mo, remote_sem=S[sem], srcs=[T[src][:, :]], dsts=[T[n][:, :] for n in bufs])]
-            return lambda: g.remote_dma_fused(tr, local_sem=S[ls])
-        sent = []
-        ne = len(topo.engines(opp, core))
-        for src, got, h, up, ls in (("off", "ro2", "ho", "upo", "lo"), ("new", "rn2", "hn", "upn", "ln")):
-            n = "%s%d" % (src, t)
-            fn = call(n, ["%s_%d" % (got, t)] + ["%s%d" % (h, t)] * 2, "%s%d" % (up, t), "%s%d" % (ls, t))
-            sent.append(add("g", 1500, fn, [X(n)], [], sem="%s%d" % (ls, t), cnt=no, lat=2500))
-            add("x", 0, None, [], [X("%s_%d" % (got, t))], sem="%s%d" % (up, t), cnt=ne, lat=2500, extra=(sent[-1],))
-        for s in (1, 3):
-            h = helpers(T, topo, T.cores[(r + s) % N])[0 if s == 1 else 1][0]
-            add("x", 0, None, [], [X("ro%d_%d" % (s, t)), X("rn%d_%d" % (s, t))], sem="uq%d_%d" % (s, t), cnt=2 * len(topo.engines(h, core)), lat=6000, extra=sent)
+        up = "up%d" % t
+        rest = [e for e in near if e not in far]
+        tr = [RemoteDMATransfer(dst_ids=[dst(hs[i])], dma_engine_mask=share(rest, i, 2), remote_sem=S["hu%d" % t], srcs=[T[up][:, :]], dsts=[T["hu%d" % t][:, :]])
+              for i in range(2)]
+        tr.append(RemoteDMATransfer(dst_ids=[dst(opp)], dma_engine_mask=topo.mask(core, opp), remote_sem=S["uq2_%d" % t], srcs=[T[up][:, :]],
+                                    dsts=[T["ru2_%d" % t][:, :]]))
+        sent = add("g", 1200, lambda: g.remote_dma_fused(tr, local_sem=S["lo%d" % t]), [X(up)], [], sem="lo%d" % t, cnt=len(near), lat=2500)
+        for s in range(1, N):
+            src = T.cores[(r + s) % N]
+            if s != 2:
+                src = helpers(T, topo, src)[s // 2]
+            add("x", 0, None, [], [X("ru%d_%d" % (s, t))], sem="uq%d_%d" % (s, t), cnt=len(topo.engines(src, core)), lat=3000 if s == 2 else 7000, extra=(sent,))
 
     def receive(t, s):
-        ts(X("kc%d" % s), X("ro%d_%d" % (s, t), 16, 17), 32.0, -256.0, A.mult, A.add)
-        ts(X("kq%d" % s), ID, X("kc%d" % s), None, A.mult, fast=True)
-        scat(s, X("rn%d_%d" % (s, t)), X("ro%d_%d" % (s, t), 0, 16))
+        n = "ru%d_%d" % (s, t)
+        kq(s, X(n, B + 16, B + 17))
+        scat(s, n)
 
     for t in range(NT):
         for b in range(NB):
             heads(t, b)
+        if t == 0:
+            late()
         for a in range(N):
+            if a == N - 1:
+                for b in range(NB):
+                    shares(t, b)
+                    sums(t, b)
             if t and a:
                 receive(t - 1, a)
             for b in range(NB):
                 visit(t, b, a)
-            if t == 0 and a == 0:
-                late()
-            if t == 0 and a == 1:
-                for b in range(NB):
-                    shares(0, b)
-        for b in range(NB):
-            elect(t, b)
-        for b in range(NB):
-            compare(t, b)
-        if t == 0:
-            for tn in (1, 2):
-                for b in range(NB):
-                    lists(tn, b)
+        elect(t, 0)
+        compare(0)
+        elect(t, 1)
         if t < NT - 1:
             kappa(t)
-        losers(t)
+        changes(t)
+        compare(1)
+        tt(X("up%d" % t, B, B + 16), XR("pk0", 1, 0, 16), X("lf"), A.max)
         if t < NT - 1:
             send(t)
-            for b in range(NB):
-                shares(t + 1, b)
+        scat(0, "up%d" % t)
     add("y", 60, lambda: Y.dma_start(T.yh[:, :], T.htab[0:128:16, P0:2048]), [X("htab", P0, 2048)], [], sem="st_h", cnt=16, lat=2000)
     dma("y", T.yl[:, :], X("lm0", 0, H), "st_l", 3500)
     emit(g, T, ops)
@@ -579,23 +550,20 @@ def rank_program(g, core, T, topo):
 
 def schedule(ops):
     n = len(ops)
-    look, fit, theta, rnd, amp = TUNE
     succ = [[] for _ in range(n)]
-    need = [len(o["deps"]) for o in ops]
+    need = [len(o["deps"]) + len(o["after"]) for o in ops]
     for i, o in enumerate(ops):
         for j in o["deps"]:
-            succ[j].append(i)
+            succ[j].append((i, ops[j]["lat"] + WAKE))
+        for j in o["after"]:
+            succ[j].append((i, 0.0))
     prio = [0.0] * n
     for i in range(n - 1, -1, -1):
-        o = ops[i]
-        m = max([prio[j] for j in succ[i]], default=-WAKE - o["lat"]) + o["lat"] + WAKE
-        rnd = (rnd * 1103515245 + 12345) % 2147483648
-        prio[i] = o["busy"] * (1.0 + amp * (rnd / 2147483648.0 - 0.5)) + m
+        prio[i] = -10.0 * i
     free, ready, avail, queues = {}, [0.0] * n, {}, {}
     for i in range(n):
         if need[i] == 0:
             avail.setdefault(ops[i]["q"], []).append(i)
-    end = 0.0
     for _ in range(n):
         best = None
         for q, lst in avail.items():
@@ -607,33 +575,30 @@ def schedule(ops):
         lst = avail[q]
         now = [i for i in lst if ready[i] <= e + 1e-6]
         pick = max(now, key=lambda i: (prio[i], -i))
-        if q in "vs":
-            soon = [i for i in lst if e + 1e-6 < ready[i] <= e + look and prio[i] > prio[pick] + theta]
-            if soon:
-                p = max(soon, key=lambda i: (prio[i], -i))
-                if e + ops[pick]["busy"] > ready[p] + fit:
-                    ok = [i for i in now if e + ops[i]["busy"] <= ready[p] + fit]
-                    pick = max(ok, key=lambda i: (prio[i], -i)) if ok else p
+        soon = [i for i in lst if e + 1e-6 < ready[i] <= e + LOOK and prio[i] > prio[pick] + THETA]
+        if soon and q != "x":
+            p = max(soon, key=lambda i: (prio[i], -i))
+            if e + ops[pick]["busy"] > ready[p] + FIT:
+                ok = [i for i in now if e + ops[i]["busy"] <= ready[p] + FIT]
+                pick = max(ok, key=lambda i: (prio[i], -i)) if ok else p
         lst.remove(pick)
         o = ops[pick]
         e = max(e, ready[pick])
         fin = e + o["busy"]
         if q != "x":
             free[q] = fin
-        o["t0"], o["t1"] = e, fin
+        o["t1"] = fin
         queues.setdefault(q, []).append(pick)
-        comp = fin + o["lat"]
-        end = max(end, comp)
-        for j in succ[pick]:
-            ready[j] = max(ready[j], comp + WAKE)
+        for j, w in succ[pick]:
+            ready[j] = max(ready[j], fin + w)
             need[j] -= 1
             if need[j] == 0:
                 avail.setdefault(ops[j]["q"], []).append(j)
-    return queues, end
+    return queues
 
 
 def emit(g, T, ops):
-    queues, end = schedule(ops)
+    queues = schedule(ops)
     S = T.sem
     eng = {"v": g.vector, "s": g.scalar, "t": g.tensor, "g": g, "y": g.sync}
     qsem = {"v": "qv", "s": "qs", "t": "qt", "g": "qg"}

@@ -3,18 +3,39 @@ from concourse.mybir import AluOpType as A, ActivationFunctionType as AF, AxisLi
 
 N, H, P0, B, NT = 4, 2048, 1280, 256, 3
 NB, W, E = 2, 128, 2048
-NS = 768
-VCH = 416
+NS = 704
+NS0 = 256
+NS1 = 768
+NS2 = 768
+MO = (W, 0)
+VCH = 256
 SSH = (0,)
-HV = 0
-Q4 = H // 4
-UP = 280
+HV = 1024
+PC = (128, 384)
+WB = 0
+WC = 1
+HV1 = 0
+UP = 144
+AT1 = 19000
+ATU = 5500
+TA = (0, 1)
 BIG = 68 * 65536
-CY, PCY, WAKE = 1.04, 0.52, 170.0
+CY = 0.9
+PCY = 0.45
+WAKE = 130.0
 GA, SC = 1.56, 3.8
+DS = ((1, 2), (3, 4), (5, 6), (7,), (8,))
+BONUS = 0.0
+PASSES = 4
+BOTH = ()
+GST = 128
+SHORT = 130.0
+NS3 = 768
+OFF = ""
 HCH = 512
+SCH = 512
 LOOK = 900.0
-FIT = 250.0
+FIT = 300.0
 THETA = 0.0
 
 SCRATCH = {}
@@ -38,50 +59,54 @@ def al(names, width, dtype):
 
 
 for _s in range(N):
-    sb("lm%d" % _s, [128, H + 2 * B], "bfloat16")
+    sb("lm%d" % _s, [128, H + B], "bfloat16")
     al("kc%d" % _s, 1, "float32")
     al("kq%d" % _s, 128, "bfloat16")
-    al("ou%d" % _s, 16, "uint16")
+    al("ou%d" % _s, 32, "uint16")
 sb("ft", [128, 2048], "bfloat16")
 sb("ci", [128, 768], "int32")
 sb("hdi", [128, 80], "int32")
 sb("htab", [128, 2048], "float32")
-sb("hl", [128, Q4], "bfloat16")
+sb("tab", [128, P0 + 2 * B], "float32")
+sb("hl", [128, H // 4], "bfloat16")
 al("hdf", 80, "float16")
 al("cl", 768, "uint16")
 for _t in range(NT):
     sb("fr%d" % _t, [128, NB * E], "bfloat16")
-    sb("up%d" % _t, [128, UP], "float16")
+    sb("up%d" % _t, [128, NB * UP], "float16")
+    sb("mn%d_0" % _t, [128, E], "bfloat16")
 for _t in range(NT - 1):
-    sb("ru1_%d ru2_%d ru3_%d hu%d" % (_t, _t, _t, _t), [128, UP], "float16")
+    sb("ru1_%d ru2_%d ru3_%d hu%d" % (_t, _t, _t, _t), [128, NB * UP], "float16")
 for _b in range(NB):
     sb("hx%d" % _b, [128, E], "float16")
-    sb("cm%d mn0_%d mn1_%d mn2_%d" % (_b, _b, _b, _b), [128, E], "bfloat16")
-    al("xg%d" % _b, NS, "bfloat16")
+    sb("cm%d" % _b, [128, E], "bfloat16")
+    al("xg%d" % _b, 1536, "bfloat16")
     al("ul%d" % _b, W, "uint16")
     al("sq%d" % _b, W, "float32")
     al("mi%d mj%d" % (_b, _b), W, "int32")
     al("ch%d lz%d dz%d" % (_b, _b, _b), W + 16, "float16")
-    al("wz%d lr%d de%d" % (_b, _b, _b), W, "float16")
+    al("wz%d lr%d de%d lbs%d" % (_b, _b, _b, _b), W, "float16")
     al("rr%d" % _b, 2 * W, "float32")
     al("nr%d yy%d" % (_b, _b), 2 * W, "float16")
-    al("dmy%d" % _b, 1, "float32")
+    al("lf%d" % _b, 8, "float32")
+    al("lu%d" % _b, 8, "uint16")
+    al("old%d clp%d" % (_b, _b), W, "bfloat16")
     sb("eb%d" % _b, [128, 64, 16], "bfloat16")
+    sb("ind%d" % _b, [128, 8 * W], "bfloat16")
+sb("mn0_1 mn1_1 mn2_1", [128, E], "bfloat16")
+sb("mf", [128, E], "float32")
 sb("mx", [128, 1024], "bfloat16")
-sb("ind", [128, 24 * W], "bfloat16")
-al("lbs", B, "float16")
-al("lf", 16, "float32")
-al("lu", 16, "uint16")
-al("old clp", B, "bfloat16")
-al("ks pf gf cst ca thr", 1, "float32")
-al("ki kj pi gi", 1, "int32")
+al("ks pf gf cst ca thr dmy r0 n0", 1, "float32")
+al("ki kj pi gi ri", 1, "int32")
 al("io", 144, "int32")
 al("km", W, "int32")
 al("iof", 144, "float32")
-al("kf idf rsa rsb st", W, "float32")
+al("kf idf rsa rsb st ef v0 v1", W, "float32")
+al("wf", 16, "float32")
 al("idw", 144, "float16")
-al("nid idq on32 keep", W, "float16")
-al("wi ones p0m rwa rwb hf", W, "bfloat16")
+al("nid idq on32 keep id8 idm8 d1", W, "float16")
+al("wi p0m rwa rwb hf sel0", W, "bfloat16")
+al("ones", 2 * W, "bfloat16")
 al("w1 wh", 8, "float16")
 al("w2 wp wm wu", 8, "bfloat16")
 al("e0", 2, "bfloat16")
@@ -91,9 +116,9 @@ for _b in range(NB):
 for _n in range(4):
     SCRATCH["pd%d" % _n] = ("psum", [128, 512], "float32")
 
-DMASEMS = ["l_comp", "l_ci2", "l_hd", "l_fa", "l_fb", "l_fc", "l_lim", "st_h", "st_l"]
-SEMAPHORES = (["qv", "qs", "qt", "qg"] + DMASEMS + ["lm_1", "lm_2", "lm_3", "bulk", "ha", "hls"]
-              + ["%s%d" % (n, t) for t in range(NT - 1) for n in ("hu", "lo", "uq1_", "uq2_", "uq3_")])
+DMASEMS = ["l_comp", "l_ci2", "l_ci3", "l_hd", "l_fa", "l_fb", "l_fc", "l_lim0", "l_lim1", "st_h", "st_l"]
+SEMAPHORES = (["qv", "qs", "qt", "qg"] + DMASEMS + ["lm_1", "lm_2", "lm_3", "bulk0", "bulk1", "ha0", "ha1", "hls"]
+              + ["%s%d%d" % (n, t, b) for t in range(NT - 1) for b in range(NB) for n in ("hu", "lo", "uq1_", "uq2_", "uq3_")])
 
 
 def helpers(T, topo, core):
@@ -101,9 +126,13 @@ def helpers(T, topo, core):
     return [c for c in cand if topo.die(c) == topo.die(core)] + [c for c in cand if topo.die(c) != topo.die(core)]
 
 
-def share(es, i, n):
-    k = len(es) // n
-    return sum(1 << e for e in es[i * k:(i + 1) * k])
+def bits(es):
+    return sum(1 << e for e in es)
+
+
+def message_engines(T, topo, core):
+    far = topo.engines(core, T.cores[(T.cores.index(core) + 2) % N])
+    return [e for e in topo.engines(core, helpers(T, topo, core)[0]) if e not in far], far[0::2], far[1::2]
 
 
 def helper_program(g, core, T, topo):
@@ -120,14 +149,18 @@ def helper_program(g, core, T, topo):
             rid, pid = topo.addr(dst, core)
             g.remote_dma(out, src, S[sem], S.hls, pid, rid, topo.mask(core, dst))
             ls[0] += len(topo.engines(core, dst))
-        g.wait_ge(S.ha, len(topo.engines(rank, core)) // len(hs))
         for s in range(1, N):
-            hand(s, T["lm%d" % s][:, i * Q4:(i + 1) * Q4], T.hl[:, :], "lm_%d" % s)
+            for p in range(2):
+                if s == 1:
+                    g.wait_ge(S["ha%d" % p], len(topo.engines(rank, core)) // len(hs))
+                c0, h0 = p * len(hs) * PC[0] + i * PC[p], p * PC[0]
+                hand(s, T["lm%d" % s][:, c0:c0 + PC[p]], T.hl[:, h0:h0 + PC[p]], "lm_%d" % s)
         if i < 2:
             s = (1, 3)[i]
             for t in range(NT - 1):
-                g.wait_ge(S["hu%d" % t], len(topo.engines(rank, core)) // 4)
-                hand(s, T["ru%d_%d" % (s, t)][:, :], T["hu%d" % t][:, :], "uq%d_%d" % (s, t))
+                for b in range(NB):
+                    g.wait_ge(S["hu%d%d" % (t, b)], len(message_engines(T, topo, rank)[s - 1]))
+                    hand(s, T["ru%d_%d" % (s, t)][:, b * UP:(b + 1) * UP], T["hu%d" % t][:, b * UP:(b + 1) * UP], "uq%d_%d%d" % (s, t, b))
         g.wait_ge(S.hls, ls[0])
 
 
@@ -249,30 +282,42 @@ def rank_program(g, core, T, topo):
         cost = sum(max(64.0, size(x)) * (1 if short(x) else 4) for o, l, x in lst) * PCY
         return add("t", cost, fire, list(rd.values()), list(wr.values()))
 
-    def dma(q, out, in_, sem, lat):
+    def dma(q, out, in_, sem, lat, extra=()):
         e = {"y": Y, "s": C}[q]
         rd = [in_] if isinstance(in_, tuple) else []
         wr = [out] if isinstance(out, tuple) else []
         src, dst_ = (in_[0] if rd else in_), (out[0] if wr else out)
-        return add(q, 60, lambda: e.dma_start(dst_, src), rd, wr, sem=sem, cnt=16, lat=lat)
+        return add(q, 60, lambda: e.dma_start(dst_, src), rd, wr, sem=sem, cnt=16, lat=lat, extra=extra)
 
     hs = helpers(T, topo, core)
     opp = T.cores[(r + 2) % N]
     near = topo.engines(core, hs[0])
-    far = topo.engines(core, opp)
 
     def dst(c):
         rid, pid = topo.addr(c, core)
         return DstId(rid=rid, pnc=pid)
 
     F0, F1 = P0 + B, 2048
-    dma("y", X("hdi"), T.hd[:, :], "l_hd", 1900)
-    dma("s", X("ci", 0, B), T.comp[:, 0:B], "l_comp", 2300)
-    dma("y", X("ft", P0, F0), T.feat[:, P0:F0], "l_fa", 2600)
-    dma("s", X("lm0", 0, H), T.lim[:, :], "l_lim", 4500)
-    dma("y", X("ft", 0, P0), T.feat[:, 0:P0], "l_fb", 6000)
-    dma("s", X("ci", B, 768), T.comp[:, B:768], "l_ci2", 7500)
-    dma("y", X("ft", F0, F1), T.feat[:, F0:F1], "l_fc", 8000)
+    cut, back = len(hs) * PC[0], [()]
+    dma("s", X("lm0", 0, cut), T.lim[:, 0:cut], "l_lim0", 2300)
+    dma("y", X("hdi"), T.hd[:, :], "l_hd", 2600)
+    dma("s", X("ci", 0, B), T.comp[:, 0:B], "l_comp", 3500)
+    dma("y", X("ft", P0, F0), T.feat[:, P0:F0], "l_fa", 4000)
+    dma("s", X("lm0", cut, H), T.lim[:, cut:H], "l_lim1", 6000)
+    for p in range(2):
+        c0, w, h0 = cut * p, PC[p], PC[0] * p
+        tr = [RemoteDMATransfer(dst_ids=[dst(h)], dma_engine_mask=bits(near[i // 2::2][i % 2::2]), remote_sem=S["ha%d" % p],
+                                srcs=[T.lm0[:, c0 + i * w:c0 + (i + 1) * w]], dsts=[T.hl[:, h0:h0 + w]]) for i, h in enumerate(hs)]
+        out = add("g", 2000, lambda tr=tr, p=p: g.remote_dma_fused(tr, local_sem=S["bulk%d" % p]), [X("lm0", c0, c0 + len(hs) * w)], [], sem="bulk%d" % p, cnt=len(near),
+                  lat=5000)
+        back.append((out,))
+    for s in range(1, N):
+        cnt = 2 * sum(len(topo.engines(h, core)) for h in helpers(T, topo, T.cores[(r + s) % N]))
+        add("x", 0, None, [], [X("lm%d" % s, 0, H)], sem="lm_%d" % s, cnt=cnt, lat=AT1 + 4000 * (s - 1))
+    dma("y", X("ft", 0, P0), T.feat[:, 0:P0], "l_fb", (9500, 6000, 4000)[WB], back[WB])
+    dma("y", X("ft", F0, F1), T.feat[:, F0:F1], "l_fc", 10000)
+    dma("y", X("ci", B, 2 * B), T.comp[:, B:2 * B], "l_ci2", (11000, 5000, 3000)[WC], back[WC])
+    dma("y", X("ci", 2 * B, 768), T.comp[:, 2 * B:768], "l_ci3", 5000, back[2])
     add("g", 430, lambda: g.iota(X("io")[0], [[1, 144]], 0, 0), [], [X("io")])
     add("g", 200, lambda: g.iota(X("pi")[0], [[0, 1]], 0, 1), [], [X("pi")])
 
@@ -293,17 +338,18 @@ def rank_program(g, core, T, topo):
         ts(X(n), ID, w, None, A.mult)
     for n, w in (("w1", 32.0 * 613), ("w2", float(BIG)), ("wp", 1.0), ("wm", -1.0)):
         ts(X(n), J8, X("gf"), w, A.is_equal, A.mult)
-    ms(X("ones"), 1.0)
+    ONE = X("ones", 0, W)
+    ms(ONE, 1.0)
     ts(X("cst"), X("idw", 1, 2), -9.0 * BIG, None, A.mult)
     ts(X("ca"), X("idw", 2, 3), -256.0, X("cst"), A.mult, A.add)
-    ts(X("kq0"), X("ones"), X("ca"), None, A.mult)
+    ts(X("kq0"), ONE, X("ca"), None, A.mult)
     for b in range(NB):
         ms(X("ch%d" % b, W, W + 16), 0.0)
 
     def fr(t, eng):
         n = "fr%d" % t
-        step = W if eng == "v" else B
-        for m0 in range(0, B, step):
+        step = W if eng == "v" else GST if t == 1 else B
+        for m0 in range(B - step, -1, -step) if eng == "v" else range(0, B, step):
             i = X("ft", P0 + B * t + m0, P0 + B * t + m0 + step)
             for k in range(16):
                 o = X(n, 16 * m0 + k, 16 * (m0 + step), 16)
@@ -314,35 +360,40 @@ def rank_program(g, core, T, topo):
 
     fr(0, "v")
 
-    tr = [RemoteDMATransfer(dst_ids=[dst(h)], dma_engine_mask=share(near, i, len(hs)), remote_sem=S.ha,
-                            srcs=[T.lm0[:, i * Q4:(i + 1) * Q4]], dsts=[T.hl[:, :]]) for i, h in enumerate(hs)]
-    add("g", 2500, lambda: g.remote_dma_fused(tr, local_sem=S.bulk), [X("lm0", 0, H)], [], sem="bulk", cnt=len(near), lat=3000)
-    for s, at in ((1, 15000), (2, 19000), (3, 23000)):
-        cnt = sum(len(topo.engines(h, core)) for h in helpers(T, topo, T.cores[(r + s) % N]))
-        add("x", 0, None, [], [X("lm%d" % s, 0, H)], sem="lm_%d" % s, cnt=cnt, lat=at)
     fr(1, "g")
     fr(2, "g")
 
     def late():
-        cp(X("cl", B, 768), X("ci", B, 768))
+        cp(X("cl", B, 2 * B), X("ci", B, 2 * B))
         ts(X("km"), X("io", 0, W), 15, None, A.bitwise_and)
         cp(X("kf"), X("km"))
         act(X("keep"), X("kf"), AF.Sigmoid, bias=-128.0, scale=256.0)
         ts(X("rsa"), X("keep"), 2.0e9, -1.0e9, A.mult, A.add)
         ts(X("rsb"), X("keep"), -2.0e9, 1.0e9, A.mult, A.add)
-        ts(X("on32"), X("ones"), 1.0 / 32, None, A.mult)
-        ts(X("p0m"), X("ones"), X("idw", 0, 1), 32.0, A.mult, A.mult)
+        ts(X("on32"), ONE, 1.0 / 32, None, A.mult)
+        ts(X("p0m"), ONE, X("idw", 0, 1), 32.0, A.mult, A.mult)
+        ts(X("dmy"), X("pf"), 2.0, float(H), A.mult, A.add)
         for b in range(NB):
             ms(X("lz%d" % b), 0.0)
             ms(X("dz%d" % b), 0.0)
             ms(X("wz%d" % b), 0.0)
-            ts(X("dmy%d" % b), X("pf"), 2.0, float(H + 2 * W * b), A.mult, A.add)
-        for t in range(NT):
-            ms(X("up%d" % t, B + 16, UP), 0.0)
+            for t in range(NT - 1):
+                ms(X("up%d" % t, b * UP + W + 8, (b + 1) * UP), 0.0)
+        ts(X("ri"), X("pi"), 15, None, A.bitwise_and)
+        ts(X("r0"), X("ri"), 0.0, None, A.is_equal)
+        ts(X("n0"), X("r0"), -2.0, 1.0, A.mult, A.add)
+        ts(X("d1"), ID, X("n0"), None, A.mult)
+        ts(X("ef"), ID, X("r0"), -256.0, A.mult, A.mult)
+        ts(X("id8"), ID, 8.0, None, A.mult)
+        ts(X("idm8"), ID, -8.0, None, A.mult)
+        ts(X("wf", 8, 16), X("wh"), -1.0 / 32, None, A.mult)
+        tt(X("wf", 0, 8), X("wp"), X("wf", 8, 16), A.add)
+        tt(X("st"), J, X("kf"), A.subtract)
+        ts(X("sel0"), X("st"), X("pf"), None, A.is_equal)
         ts(X("hf"), X("keep"), 0.5, None, A.mult)
         ts(X("st"), X("keep"), -1.0, 1.0, A.mult, A.add)
         scan(X("rwa"), X("hf"), X("st"), 0.0, A.mult, A.add)
-        ts(X("hf"), X("ones"), 0.5, None, A.mult)
+        ts(X("hf"), ONE, 0.5, None, A.mult)
         ts(X("st"), X("keep"), 0.0, None, A.mult)
         scan(X("rwb"), X("hf"), X("st"), 2.0 ** 57, A.mult, A.add)
         ts(X("e0", 0, 1), X("idw", 0, 1), 1.0, None, A.mult)
@@ -352,12 +403,21 @@ def rank_program(g, core, T, topo):
         ts(X("wu"), X("wp"), XR("pk0", 0, 0, 1), None, A.mult)
         cp(X("thr"), XR("pk0", 0, 1, 2))
 
-    rot = [0]
+    rot, mark, held = [0], {}, {}
+
+    def hold(i, q):
+        if q in held:
+            ops[i]["after"].add(held[q])
 
     def parts(lo, hi, most):
         n = -(-(hi - lo) // most)
+        if not n:
+            return []
         step = -(-(hi - lo) // (32 * n)) * 32
         return [(a, min(a + step, hi)) for a in range(lo, hi, step)]
+
+    def FR(t, b, lo, hi):
+        return X("fr%d" % t, 16 * MO[b] + lo, 16 * MO[b] + hi)
 
     def col(n, k):
         return X(n, k, E, 16)
@@ -365,17 +425,45 @@ def rank_program(g, core, T, topo):
     def offs(n, c0, lo, hi):
         return X(n, c0 + lo // 16, c0 + hi // 16)
 
+    def gather(out, win, lst, c0, lo, hi, other, op):
+        def call(a, z):
+            return V.tensor_tensor(X(out, a, z)[0], win[0].indirect(offs(lst, c0, a, z)[0]), other(a, z)[0], op)
+        for a, z in parts(lo, hi, VCH):
+            ops[tt(X(out, a, z), IND(win, offs(lst, c0, a, z)), other(a, z), op)]["piece"] = [call, a, z]
+
     def shares(t, b):
-        mn, win, c0 = "mn%d_%d" % (t, b), X("ft", 0, P0 + B * t), B * t + W * b
+        mn, win, c0 = "mn%d_%d" % (t, b), X("ft", 0, P0 + B * t), B * t + MO[b]
         if b not in SSH:
-            for lo, hi in parts(0, E, VCH):
-                tt(X(mn, lo, hi), IND(win, offs("cl", c0, lo, hi)), X("fr%d" % t, E * b + lo, E * b + hi), A.min)
+            gather(mn, win, "cl", c0, 0, E, lambda lo, hi: FR(t, b, lo, hi), A.min)
             return
         for i, (lo, hi) in enumerate(parts(0, E, 512)):
             x, d = X("mx", 512 * (i % 2), 512 * (i % 2) + 512), X("pd3")
-            act(x, IND(win, offs("cl", c0, lo, hi)))
-            mm([(d, ID, X("fr%d" % t, E * b + lo, E * b + hi)), (d, X("nid"), x)])
+            hold(act(x, IND(win, offs("cl", c0, lo, hi))), "s")
+            mm([(d, ID, FR(t, b, lo, hi)), (d, X("nid"), x)])
             act(X(mn, lo, hi), d, AF.Relu)
+
+    def table():
+        for lo, hi in parts(0, P0, 512):
+            d = X("pd3", 0, hi - lo)
+            mm([(d, X("d1"), X("ft", lo, hi)), (d, X("ef"), X("htab", lo, hi))])
+            act(X("tab", lo, hi), d)
+
+    def both(t, b):
+        gather("mf", X("tab", 0, P0 + B * t), "cl", B * t + MO[b], 0, E, lambda lo, hi: FR(t, b, lo, hi), A.min)
+
+    def unpack(t, b):
+        c0, pk, ch = B * t + MO[b], "pk%d" % b, X("ch%d" % b, 0, W)
+        for k0 in range(0, 16, 4):
+            mm([(XI(pk, 0, 16, k), col("mf", k), X("wf")) for k in range(k0, k0 + 4)], apart=True)
+        mi, mj, u = X("mi%d" % b), X("mj%d" % b), bank(W)
+        cp(mi, X3(pk, 8, 16))
+        ts(mj, mi, 3, 32 * (H - 1), A.arith_shift_right, A.bitwise_and)
+        cp(ch, mj)
+        to_list(b)
+        mm([(u, X("ft", P0 + c0, P0 + c0 + W), X("sel0")), (u, X("id8"), ch)])
+        tt(X("v0"), mi, u, A.min)
+        act(X("v1"), X3(pk, 0, 8))
+        mm([(X3(pk, 0, 8), X("idf"), X("v1")), (X3(pk, 0, 8), X("idf"), X("v0")), (X3(pk, 0, 8), X("idm8"), ch)], last=False)
 
     def to_list(b):
         px = "px%d" % b
@@ -383,31 +471,32 @@ def rank_program(g, core, T, topo):
         cp(X("ul%d" % b), X3(px, 0, 8, 16, 32))
 
     def heads(t, b):
-        win, hx, px, c0 = X("htab", 0, P0 + B * t), "hx%d" % b, "px%d" % b, B * t + W * b
-        hv = HV if b == 0 else 0
-        for lo, hi in parts(0, hv, VCH) if hv else []:
+        win, hx, px, c0 = X("htab", 0, P0 + B * t), "hx%d" % b, "px%d" % b, B * t + MO[b]
+        hv = (HV1 if t else HV) if b == 0 else 0
+        for lo, hi in parts(0, hv, 1024 if t == 0 else VCH):
             cp(X(hx, lo, hi), IND(win, offs("cl", c0, lo, hi)))
         for lo, hi in parts(hv, E, HCH):
             act(X(hx, lo, hi), IND(win, offs("cl", c0, lo, hi)))
         mm([(XI(px, 0, 8, k), col(hx, k), X("wh")) for k in range(16)], apart=True)
-        cp(X("ch%d" % b, 0, W), X3(px, 0, 8, 0, 16))
+        (act if "h" in OFF else cp)(X("ch%d" % b, 0, W), X3(px, 0, 8, 0, 16))
         to_list(b)
 
-    def visit(t, b, a):
-        lm, cm, px, fr_ = X("lm%d" % a, 0, H), "cm%d" % b, "px%d" % b, "fr%d" % t
+    def visit(t, b, a, between):
+        lm, cm, px = X("lm%d" % a, 0, H), "cm%d" % b, "px%d" % b
         x, ch = X3(px, 0, 8, 0, 16), X("ch%d" % b, 0, W)
-        act(X("sq%d" % b), ch, AF.Square, bias=16.0, scale=1.0 / 32)
-        mm([(x, X("idf"), X("sq%d" % b)), (x, X("kq%d" % (a if t else 0)), X("ones"))], last=False)
-        todo = []
-        for lo, hi in parts(E - NS, E, 512):
-            xg, d = X("xg%d" % b, lo - E + NS, hi - E + NS), bank(hi - lo)
+        todo, nv = [], E - ((NS2 if t in BOTH else NS0) if (a, b) == (0, 0) else NS3 if (a, b) == (N - 1, 1) else NS1 if t else NS)
+        for lo, hi in parts(nv, E, SCH):
+            xg, d = X("xg%d" % b, lo - nv, hi - nv), bank(hi - lo)
             act(xg, IND(lm, offs("ul%d" % b, 0, lo, hi)))
-            mm([(d, ID, X(fr_, E * b + lo, E * b + hi)), (d, X("nid"), xg)])
+            mm([(d, ID, FR(t, b, lo, hi)), (d, X("nid"), xg)])
             todo.append((X(cm, lo, hi), d))
+        act(X("sq%d" % b), ch, AF.Square, bias=16.0, scale=1.0 / 32)
+        mm([(x, X("idf"), X("sq%d" % b)), (x, X("kq%d" % (a if t else 0)), ONE)], last=False)
+        if between:
+            between()
         for o, d in todo:
-            act(o, d, AF.Sigmoid, bias=-128.0, scale=256.0)
-        for lo, hi in parts(0, E - NS, VCH):
-            tt(X(cm, lo, hi), IND(lm, offs("ul%d" % b, 0, lo, hi)), X(fr_, E * b + lo, E * b + hi), A.is_lt)
+            mark["s"] = act(o, d, AF.Sigmoid, bias=-128.0, scale=256.0)
+        gather(cm, lm, "ul%d" % b, 0, 0, nv, lambda lo, hi: FR(t, b, lo, hi), A.is_lt)
         mm([(XI(px, 0, 8, k), col(cm, k), X(w)) for k in range(16) for w in ("w1", "w2")], first=False)
         tt(X("mi%d" % b), x, ch, A.max)
         ts(X("mj%d" % b), X("mi%d" % b), 32 * (H - 1), None, A.bitwise_and)
@@ -420,7 +509,7 @@ def rank_program(g, core, T, topo):
 
     def sums(t, b):
         pk = "pk%d" % b
-        mm([(X3(pk, 0, 8), X("wi"), X("ones"))] + [(XI(pk, 0, 8, k), col("mn%d_%d" % (t, b), k), X("wm" if b in SSH else "wp")) for k in range(16)], last=False)
+        mm([(X3(pk, 0, 8), X("wi"), ONE)] + [(XI(pk, 0, 8, k), col("mn%d_%d" % (t, b), k), X("wm" if b in SSH else "wp")) for k in range(16)], last=False)
 
     def bank(n):
         rot[0] = (rot[0] + 1) % 3
@@ -435,7 +524,7 @@ def rank_program(g, core, T, topo):
         for d in range(1, 9):
             e = X3(eb, 8 * d - 8, 8 * d)
             tt(e, ch, X3(px, 8, 16, d, d + 16), A.is_equal)
-        for ds in ((1, 2), (3, 4), (5, 6), (7,), (8,)):
+        for ds in DS:
             run = []
             for d in ds:
                 run.append((key, X("wi"), X3(eb, 8 * d - 8, 8 * d)))
@@ -453,32 +542,45 @@ def rank_program(g, core, T, topo):
             out = X("lz%d" % b, 15, 15 + W, 16) if h else X("wz%d" % b, 0, W, 16)
             tt(out, X("yy%d" % b, lo, hi, 16), X("ch%d" % b, 0, W, 16), A.add)
             if h == 0:
-                c0 = P0 + B * t + W * b
+                c0 = P0 + B * t + MO[b]
                 mm([(X3(px, 0, 8, 0, 16), X("wz%d" % b), X("idq"))])
                 act(X("htab", c0, c0 + W), X3(px, 0, 8, 0, 16))
+                if t < max(BOTH, default=0):
+                    d = bank(W)
+                    mm([(d, X("d1"), X("ft", c0, c0 + W)), (d, X("wz%d" % b), X("idm8"))])
+                    (cp if b and "t" not in OFF else act)(X("tab", c0, c0 + W), d)
+
+    def losers(t, b):
+        px, up, lf, c0 = "px%d" % b, "up%d" % t, "lf%d" % b, P0 + B * t + MO[b]
+        row, lst, dup, old = X("lbs%d" % b), XR(px, 8, 0, 8), XR(px, 9, 0, 8), X("old%d" % b)
         scan(X("lr%d" % b), X("keep"), X("lz%d" % b, 15, 15 + W), 0.0, A.mult, A.add)
         mm([(X3(px, 0, 8, 16, 32), X("lr%d" % b), X("idq"))])
-        cp(X("lbs", W * b, W * b + W), X3(px, 0, 8, 16, 32))
-        lists(XR(pk, 16, 0, 8), "lz%d" % b, "idq")
-        cp(X("lf", 8 * b, 8 * b + 8), XR(pk, 16, 0, 8))
-
-    def compare(b):
-        row, pk = X("lbs", W * b, W * b + W), "pk%d" % b
-        o, run = XR(pk, 17, 0, 8), []
-        for a in range(8 * b + 8):
-            i = X("ind", W * (8 * b + a), W * (8 * b + a + 1))
-            ts(i, row, X("lf", a, a + 1), 2.0 ** (56 - 16 * (a - 8 * b)) if a >= 8 * b else 2.0 ** 80, A.is_equal, A.mult)
-            run.append((o, i, X("wu")))
+        lists(lst, "lz%d" % b, "idq")
+        (act if "r" in OFF else cp)(row, X3(px, 0, 8, 16, 32))
+        (act if "l" in OFF else cp)(X(lf), lst)
+        cp(X("lu%d" % b), lst)
+        dif, new = bank(W), bank(W)
+        act(old, IND(X("lm0", 0, H), X("lu%d" % b)))
+        mm([(dif, ID, X("ft", c0, c0 + W)), (dif, X("nid"), old)])
+        run = []
+        for a in range(8):
+            i = X("ind%d" % b, W * a, W * a + W)
+            ts(i, row, X(lf, a, a + 1), 2.0 ** (56 - 16 * a), A.is_equal, A.mult)
+            run.append((dup, i, X("wu")))
         mm(run)
-        ts(X("dz%d" % b, 15, 15 + W, 16), o, X("thr"), X("dmy%d" % b), A.is_ge, A.mult)
-        lists(XR("pk0", 1, 8 * b, 8 * b + 8), "dz%d" % b, "idw")
+        ts(X("clp%d" % b), dif, -32.0, 32.0, A.max, A.min)
+        mm([(new, ID, old), (new, ID, X("clp%d" % b))])
+        act(X(up, b * UP, b * UP + W), new)
+        ts(X("dz%d" % b, 15, 15 + W, 16), dup, X("thr"), X("dmy"), A.is_ge, A.mult)
+        lists(lst, "dz%d" % b, "idw")
+        tt(X(up, b * UP + W, b * UP + W + 8), lst, X(lf), A.max)
 
     def kq(s, k):
         act(X("kc%d" % s), k)
         act(X("kq%d" % s), X("p0m"), AF.Identity, bias=X("ca"), scale=X("kc%d" % s))
 
     def kappa(t):
-        o, ks, k = XR("pk0", 19, 0, 8), X("ks"), X("up%d" % t, B + 16, B + 17)
+        o, ks, k = XR("pk0", 19, 0, 8), X("ks"), X("up%d" % t, UP + W + 8, UP + W + 9)
         mm([(o, X("on32"), X("wz%d" % b, 0, W, 16)) for b in range(NB)])
         add("v", vc(8, 1), lambda: V.tensor_reduce(ks[0], o[0], AxisListType.X, A.add), [o], [ks])
         cp(X("ki"), ks)
@@ -486,63 +588,61 @@ def rank_program(g, core, T, topo):
         cp(k, X("kj"))
         kq(0, k)
 
-    def scat(s, up):
-        cp(X("ou%d" % s), X(up, B, B + 16))
-        cp(IND(X("lm%d" % s), X("ou%d" % s)), X(up, 0, B))
+    def scat(s, up, b):
+        ou = X("ou%d" % s, 16 * b, 16 * b + 8)
+        cp(ou, X(up, b * UP + W, b * UP + W + 8))
+        cp(IND(X("lm%d" % s), ou), X(up, b * UP, b * UP + W))
 
-    def changes(t):
-        up, old, dif, new = "up%d" % t, X("old"), bank(B), bank(B)
-        cp(X("lu"), X("lf"))
-        act(old, IND(X("lm0", 0, H), X("lu")))
-        mm([(dif, ID, X("ft", P0 + B * t, P0 + B * t + B)), (dif, X("nid"), old)])
-        ts(X("clp"), dif, -32.0, 32.0, A.max, A.min)
-        mm([(new, ID, old), (new, ID, X("clp"))])
-        act(X(up, 0, B), new)
-
-    def send(t):
-        up = "up%d" % t
-        rest = [e for e in near if e not in far]
-        tr = [RemoteDMATransfer(dst_ids=[dst(hs[i])], dma_engine_mask=share(rest, i, 2), remote_sem=S["hu%d" % t], srcs=[T[up][:, :]], dsts=[T["hu%d" % t][:, :]])
-              for i in range(2)]
-        tr.append(RemoteDMATransfer(dst_ids=[dst(opp)], dma_engine_mask=topo.mask(core, opp), remote_sem=S["uq2_%d" % t], srcs=[T[up][:, :]],
-                                    dsts=[T["ru2_%d" % t][:, :]]))
-        sent = add("g", 1200, lambda: g.remote_dma_fused(tr, local_sem=S["lo%d" % t]), [X(up)], [], sem="lo%d" % t, cnt=len(near), lat=2500)
+    def send(t, b):
+        lo, hi = b * UP, (b + 1) * UP
+        up, tb = T["up%d" % t][:, lo:hi], "%d%d" % (t, b)
+        es = message_engines(T, topo, core)
+        to = [(hs[0], "hu", "hu%d"), (opp, "uq2_", "ru2_%d"), (hs[1], "hu", "hu%d")]
+        tr = [RemoteDMATransfer(dst_ids=[dst(c)], dma_engine_mask=bits(e), remote_sem=S[sem + tb], srcs=[up], dsts=[T[n % t][:, lo:hi]]) for e, (c, sem, n) in zip(es, to)]
+        sent = add("g", 1200, lambda: g.remote_dma_fused(tr, local_sem=S["lo" + tb]), [X("up%d" % t, lo, hi)], [], sem="lo" + tb, cnt=len(near), lat=2500)
         for s in range(1, N):
             src = T.cores[(r + s) % N]
-            if s != 2:
-                src = helpers(T, topo, src)[s // 2]
-            add("x", 0, None, [], [X("ru%d_%d" % (s, t))], sem="uq%d_%d" % (s, t), cnt=len(topo.engines(src, core)), lat=3000 if s == 2 else 7000, extra=(sent,))
+            cnt = len(message_engines(T, topo, src)[1] if s == 2 else topo.engines(helpers(T, topo, src)[s // 2], core))
+            add("x", 0, None, [], [X("ru%d_%d" % (s, t), lo, hi)], sem="uq%d_%s" % (s, tb), cnt=cnt, lat=ATU + 1500 * (s // 3), extra=(sent,))
 
     def receive(t, s):
         n = "ru%d_%d" % (s, t)
-        kq(s, X(n, B + 16, B + 17))
-        scat(s, n)
+        scat(s, n, 0)
+        kq(s, X(n, UP + W + 8, UP + W + 9))
+        scat(s, n, 1)
 
     for t in range(NT):
-        for b in range(NB):
-            heads(t, b)
+        heads(t, 0)
+        if t in BOTH:
+            both(t, 1)
+        else:
+            heads(t, 1)
         if t == 0:
             late()
         for a in range(N):
             if a == N - 1:
-                for b in range(NB):
+                for b in range(1 if t in BOTH else NB):
                     shares(t, b)
                     sums(t, b)
+            if (t, a) == TA and BOTH:
+                table()
             if t and a:
                 receive(t - 1, a)
             for b in range(NB):
-                visit(t, b, a)
-        elect(t, 0)
-        compare(0)
-        elect(t, 1)
-        if t < NT - 1:
-            kappa(t)
-        changes(t)
-        compare(1)
-        tt(X("up%d" % t, B, B + 16), XR("pk0", 1, 0, 16), X("lf"), A.max)
-        if t < NT - 1:
-            send(t)
-        scat(0, "up%d" % t)
+                visit(t, b, a, (lambda: unpack(t, 1)) if t in BOTH and (a, b) == (0, 0) else None)
+        held.update(mark)
+        if t == 0:
+            cp(X("cl", 2 * B, 768), X("ci", 2 * B, 768))
+        for b in range(NB):
+            elect(t, b)
+        for b in range(NB):
+            if b and t < NT - 1:
+                kappa(t)
+            losers(t, b)
+            if t < NT - 1:
+                send(t, b)
+        for b in range(NB):
+            scat(0, "up%d" % t, b)
     add("y", 60, lambda: Y.dma_start(T.yh[:, :], T.htab[0:128:16, P0:2048]), [X("htab", P0, 2048)], [], sem="st_h", cnt=16, lat=2000)
     dma("y", T.yl[:, :], X("lm0", 0, H), "st_l", 3500)
     emit(g, T, ops)
@@ -559,7 +659,7 @@ def schedule(ops):
             succ[j].append((i, 0.0))
     prio = [0.0] * n
     for i in range(n - 1, -1, -1):
-        prio[i] = -10.0 * i
+        prio[i] = -10.0 * i + (BONUS if ops[i]["q"] == "t" and ops[i]["busy"] < SHORT else 0.0)
     free, ready, avail, queues = {}, [0.0] * n, {}, {}
     for i in range(n):
         if need[i] == 0:
@@ -584,7 +684,8 @@ def schedule(ops):
         lst.remove(pick)
         o = ops[pick]
         e = max(e, ready[pick])
-        fin = e + o["busy"]
+        p = ops[queues[q][-1]].get("piece") if queues.get(q) else None
+        fin = e + o["busy"] - (50 if p and "piece" in o and p[0] is o["piece"][0] else 0)
         if q != "x":
             free[q] = fin
         o["t1"] = fin
@@ -594,11 +695,57 @@ def schedule(ops):
             need[j] -= 1
             if need[j] == 0:
                 avail.setdefault(ops[j]["q"], []).append(j)
+    pred = [[] for _ in range(n)]
+    for i in range(n):
+        for j, w in succ[i]:
+            pred[j].append((i, w))
+
+    def place(order, before, first):
+        fin, line = [0.0] * n, {}
+        for i in order:
+            d = ops[i]["busy"]
+            e = max([fin[j] + w for j, w in before[i]], default=first[i])
+            if ops[i]["q"] != "x":
+                used = line.setdefault(ops[i]["q"], [])
+                k = len(used)
+                while k and used[k - 1][1] > e:
+                    k -= 1
+                while k < len(used) and used[k][0] < e + d:
+                    e = max(e, used[k][1])
+                    k += 1
+                used.insert(k, (e, e + d))
+            fin[i] = e + d
+        return fin
+    fin, best = [o["t1"] for o in ops], None
+    for _ in range(PASSES):
+        back = place(sorted(range(n), key=lambda i: (-fin[i], -i)), succ, [o["lat"] for o in ops])
+        fin = place(sorted(range(n), key=lambda i: (-back[i], i)), pred, [0.0] * n)
+        end = max(fin[i] + ops[i]["lat"] for i in range(n))
+        if best is None or end < best[0]:
+            best = (end, fin)
+    if best:
+        queues = {}
+        for i in sorted(range(n), key=lambda i: (best[1][i], i)):
+            ops[i]["t1"] = best[1][i]
+            queues.setdefault(ops[i]["q"], []).append(i)
     return queues
 
 
 def emit(g, T, ops):
     queues = schedule(ops)
+    same, kept = {}, []
+    for i in queues["v"]:
+        p, o = ops[kept[-1]].get("piece") if kept else None, ops[i].get("piece")
+        if p and o and p[0] is o[0] and p[2] == o[1]:
+            p[2] = o[2]
+            ops[kept[-1]]["deps"] |= ops[i]["deps"]
+            ops[kept[-1]]["fire"] = lambda p=p: p[0](p[1], p[2])
+            same[i] = kept[-1]
+        else:
+            kept.append(i)
+    queues["v"] = kept
+    for o in ops:
+        o["deps"] = {same.get(j, j) for j in o["deps"]}
     S = T.sem
     eng = {"v": g.vector, "s": g.scalar, "t": g.tensor, "g": g, "y": g.sync}
     qsem = {"v": "qv", "s": "qs", "t": "qt", "g": "qg"}
@@ -622,7 +769,7 @@ def emit(g, T, ops):
             o["tok"] = (o["sem"], total[o["sem"]])
     known = {q: {} for q in queues}
     nxt = {q: 0 for q in queues}
-    done = set()
+    done = set(same)
     while len(done) < len(ops):
         for q, lst in queues.items():
             kn = known[q]

@@ -3,45 +3,50 @@ from concourse.mybir import AluOpType as A, ActivationFunctionType as AF, AxisLi
 
 N, H, P0, B, NT = 4, 2048, 1280, 256, 3
 NB, W, E = 2, 128, 2048
+KW = 64
+HK = H + KW
 NS = 704
 NS0 = 256
 NS1 = 768
-NS2 = 768
+NSA = 768
+NS3 = 768
 MO = (W, 0)
-VCH = 256
-SSH = (0,)
-HV = 1024
+CUTS = {"plain": (0, 96, 96, 224, 96), "last": (0, 64, 64, 128), "after": (64, 64, 192, 0), "free": (0, 256, 256, 256, 256)}
+BEAT = [(t, a, b) for t in range(NT) for a in range(N) for b in range(NB) if a > 1 or b or t and a]
+VCH = 128
+SHS = 256
+SV = {(0, 1): 1536}
+FOLD = [(t, b) for t in range(NT) for b in range(NB) if SV.get((t, b), 0) < E]
+LATEST = {(0, 0): (0, 1), (0, 1): (0, 2), (1, 0): (1, 0), (1, 1): (1, 1), (2, 0): (2, 0), (2, 1): (2, 1)}
+SUMS = ((2, 1), (3, 0))
+STAGES = "eq0 eq1 max1 min1 min0 max0 one1 one0 two1 end1 two0 end0 kappa send head0 find0 sc0 sc1 find1 head1"
+HV = (1024, 512, 512)
+RS = (3,)
 PC = (128, 384)
 WB = 0
 WC = 1
-HV1 = 0
-UP = 144
-AT1 = 19000
+UP = 136
+AT1 = 16000
 ATU = 5500
-TA = (0, 1)
+ATR = 9000
+ATF = 7000
 BIG = 68 * 65536
 CY = 0.9
 PCY = 0.45
-WAKE = 130.0
+WAKE = 150.0
 GA, SC = 1.56, 3.8
 DS = ((1, 2), (3, 4), (5, 6), (7,), (8,))
-BONUS = 0.0
-PASSES = 4
-BOTH = ()
-GST = 128
-SHORT = 130.0
-NS3 = 768
+LOOKS = ((900.0, 100.0), (900.0, 300.0), (500.0, 60.0), (300.0, 0.0))
+PASSES = 3
+GST = 256
 OFF = ""
-HCH = 512
 SCH = 512
-LOOK = 900.0
-FIT = 300.0
-THETA = 0.0
 
 SCRATCH = {}
 POOL = {}
 _FILL = {}
 _BYTES = {"float32": 4, "int32": 4, "bfloat16": 2, "float16": 2, "uint16": 2}
+_PLAN = {}
 
 
 def sb(names, shape, dtype):
@@ -58,34 +63,39 @@ def al(names, width, dtype):
         SCRATCH[p] = ("sbuf", [128, _FILL[p]], dtype)
 
 
+MSG = [s for s in range(1, N) if s not in RS]
 for _s in range(N):
-    sb("lm%d" % _s, [128, H + B], "bfloat16")
-    al("kc%d" % _s, 1, "float32")
-    al("kq%d" % _s, 128, "bfloat16")
+    sb("lm%d" % _s, [128, HK + B], "bfloat16")
     al("ou%d" % _s, 32, "uint16")
 sb("ft", [128, 2048], "bfloat16")
 sb("ci", [128, 768], "int32")
 sb("hdi", [128, 80], "int32")
 sb("htab", [128, 2048], "float32")
-sb("tab", [128, P0 + 2 * B], "float32")
 sb("hl", [128, H // 4], "bfloat16")
 al("hdf", 80, "float16")
 al("cl", 768, "uint16")
 for _t in range(NT):
     sb("fr%d" % _t, [128, NB * E], "bfloat16")
-    sb("up%d" % _t, [128, NB * UP], "float16")
-    sb("mn%d_0" % _t, [128, E], "bfloat16")
+    sb("up%d" % _t, [128, NB * UP + KW], "float16")
+    sb("mn%d_0 mn%d_1" % (_t, _t), [128, E], "bfloat16")
+for _t, _b in FOLD:
+    sb("mx%d_%d" % (_t, _b), [128, E], "bfloat16")
 for _t in range(NT - 1):
-    sb("ru1_%d ru2_%d ru3_%d hu%d" % (_t, _t, _t, _t), [128, NB * UP], "float16")
+    sb("hu%d" % _t, [128, NB * UP + KW], "float16")
+    sb("hl%d" % _t, [128, HK // 4], "bfloat16")
+    for _s in MSG:
+        sb("ru%d_%d" % (_s, _t), [128, NB * UP + KW], "float16")
+    for _s in RS:
+        sb("lr%d_%d" % (_s, _t), [128, HK], "bfloat16")
 for _b in range(NB):
     sb("hx%d" % _b, [128, E], "float16")
     sb("cm%d" % _b, [128, E], "bfloat16")
-    al("xg%d" % _b, 1536, "bfloat16")
+    al("xg%d" % _b, 1024, "bfloat16")
     al("ul%d" % _b, W, "uint16")
     al("sq%d" % _b, W, "float32")
     al("mi%d mj%d" % (_b, _b), W, "int32")
-    al("ch%d lz%d dz%d" % (_b, _b, _b), W + 16, "float16")
-    al("wz%d lr%d de%d lbs%d" % (_b, _b, _b, _b), W, "float16")
+    al("ch%d" % _b, W + 16, "float16")
+    al("lz%d dz%d lk%d wz%d lr%d de%d lbs%d" % ((_b,) * 7), W, "float16")
     al("rr%d" % _b, 2 * W, "float32")
     al("nr%d yy%d" % (_b, _b), 2 * W, "float16")
     al("lf%d" % _b, 8, "float32")
@@ -93,22 +103,18 @@ for _b in range(NB):
     al("old%d clp%d" % (_b, _b), W, "bfloat16")
     sb("eb%d" % _b, [128, 64, 16], "bfloat16")
     sb("ind%d" % _b, [128, 8 * W], "bfloat16")
-sb("mn0_1 mn1_1 mn2_1", [128, E], "bfloat16")
-sb("mf", [128, E], "float32")
-sb("mx", [128, 1024], "bfloat16")
-al("ks pf gf cst ca thr dmy r0 n0", 1, "float32")
-al("ki kj pi gi ri", 1, "int32")
+al("pf gf rf c1 c2 c3 cq cw thr dmy", 1, "float32")
+al("pi gi ri", 1, "int32")
+al("ki kj", KW, "int32")
 al("io", 144, "int32")
-al("km", W, "int32")
+al("km gm", W, "int32")
 al("iof", 144, "float32")
-al("kf idf rsa rsb st ef v0 v1", W, "float32")
-al("wf", 16, "float32")
+al("kf gk idf rsa rsb st", W, "float32")
 al("idw", 144, "float16")
-al("nid idq on32 keep id8 idm8 d1", W, "float16")
-al("wi p0m rwa rwb hf sel0", W, "bfloat16")
-al("ones", 2 * W, "bfloat16")
-al("w1 wh", 8, "float16")
-al("w2 wp wm wu", 8, "bfloat16")
+al("nid idq on32 keep own", W, "float16")
+al("wi kl rwa rwb hf ones wu bar", W, "bfloat16")
+al("w1 wh a1 a32", 8, "float16")
+al("w2 wp", 8, "bfloat16")
 al("e0", 2, "bfloat16")
 for _b in range(NB):
     SCRATCH["px%d" % _b] = ("psum", [128, 16, 32], "float32")
@@ -118,7 +124,9 @@ for _n in range(4):
 
 DMASEMS = ["l_comp", "l_ci2", "l_ci3", "l_hd", "l_fa", "l_fb", "l_fc", "l_lim0", "l_lim1", "st_h", "st_l"]
 SEMAPHORES = (["qv", "qs", "qt", "qg"] + DMASEMS + ["lm_1", "lm_2", "lm_3", "bulk0", "bulk1", "ha0", "ha1", "hls"]
-              + ["%s%d%d" % (n, t, b) for t in range(NT - 1) for b in range(NB) for n in ("hu", "lo", "uq1_", "uq2_", "uq3_")])
+              + ["%s%d%d" % (n, t, b) for t in range(NT - 1) for b in range(NB) for n in ["hu", "lo"] + ["uq%d_" % s for s in MSG]]
+              + ["%s%d" % (n, t) for t in range(NT - 1) for n in ["rl", "hr"] + ["rq%d_" % s for s in RS]]
+              + ["%s%d%d" % (n, t, b) for t, b in FOLD for n in ("fa", "fl", "fb")])
 
 
 def helpers(T, topo, core):
@@ -126,41 +134,67 @@ def helpers(T, topo, core):
     return [c for c in cand if topo.die(c) == topo.die(core)] + [c for c in cand if topo.die(c) != topo.die(core)]
 
 
+def mirror(T, topo, core):
+    return [c for c in topo.cores_of(core) if c not in T.cores and c not in helpers(T, topo, core) and topo.die(c) == topo.die(core)][0]
+
+
 def bits(es):
     return sum(1 << e for e in es)
 
 
-def message_engines(T, topo, core):
-    far = topo.engines(core, T.cores[(T.cores.index(core) + 2) % N])
-    return [e for e in topo.engines(core, helpers(T, topo, core)[0]) if e not in far], far[0::2], far[1::2]
+def routes(T, topo, core, b):
+    r, hs = T.cores.index(core), helpers(T, topo, core)
+    far = topo.engines(core, T.cores[(r + 2) % N])
+    pools = [[e for e in topo.engines(core, hs[0]) if e not in far]] + [far[i::len(MSG) - 1] for i in range(len(MSG) - 1)]
+    out = {}
+    for s, es in zip(MSG, pools):
+        to = T.cores[(r - s) % N]
+        out[s] = (to if topo.may_write(core, to) else hs[(b + s // 2) % 2], es)
+    return out
+
+
+def span(b):
+    return b * UP, (b + 1) * UP + (KW if b == NB - 1 else 0)
 
 
 def helper_program(g, core, T, topo):
     S = T.sem
     for r, rank in enumerate(T.cores):
         hs = helpers(T, topo, rank)
-        if core not in hs:
-            continue
-        i = hs.index(core)
         ls = [0]
 
-        def hand(s, out, src, sem):
-            dst = T.cores[(r - s) % N]
+        def hand(dst, out, src, sem):
             rid, pid = topo.addr(dst, core)
             g.remote_dma(out, src, S[sem], S.hls, pid, rid, topo.mask(core, dst))
             ls[0] += len(topo.engines(core, dst))
+        if core == mirror(T, topo, rank):
+            for t, b in FOLD:
+                g.wait_ge(S["fa%d%d" % (t, b)], len(topo.engines(rank, core)))
+                mn = T["mn%d_%d" % (t, b)][:, SV.get((t, b), 0):E]
+                hand(rank, mn, mn, "fb%d%d" % (t, b))
+            g.wait_ge(S.hls, ls[0])
+        if core not in hs:
+            continue
+        i = hs.index(core)
+        part = len(topo.engines(rank, core)) // len(hs)
         for s in range(1, N):
             for p in range(2):
                 if s == 1:
-                    g.wait_ge(S["ha%d" % p], len(topo.engines(rank, core)) // len(hs))
+                    g.wait_ge(S["ha%d" % p], part)
                 c0, h0 = p * len(hs) * PC[0] + i * PC[p], p * PC[0]
-                hand(s, T["lm%d" % s][:, c0:c0 + PC[p]], T.hl[:, h0:h0 + PC[p]], "lm_%d" % s)
-        if i < 2:
-            s = (1, 3)[i]
-            for t in range(NT - 1):
-                for b in range(NB):
-                    g.wait_ge(S["hu%d%d" % (t, b)], len(message_engines(T, topo, rank)[s - 1]))
-                    hand(s, T["ru%d_%d" % (s, t)][:, b * UP:(b + 1) * UP], T["hu%d" % t][:, b * UP:(b + 1) * UP], "uq%d_%d%d" % (s, t, b))
+                hand(T.cores[(r - s) % N], T["lm%d" % s][:, c0:c0 + PC[p]], T.hl[:, h0:h0 + PC[p]], "lm_%d" % s)
+        for t in range(NT - 1):
+            for b in range(NB):
+                lo, hi = span(b)
+                for s, (to, es) in routes(T, topo, rank, b).items():
+                    if to == core:
+                        g.wait_ge(S["hu%d%d" % (t, b)], len(es))
+                        hand(T.cores[(r - s) % N], T["ru%d_%d" % (s, t)][:, lo:hi], T["hu%d" % t][:, lo:hi], "uq%d_%d%d" % (s, t, b))
+            if RS:
+                g.wait_ge(S["hr%d" % t], part)
+            for s in RS:
+                w = HK // len(hs)
+                hand(T.cores[(r - s) % N], T["lr%d_%d" % (s, t)][:, i * w:(i + 1) * w], T["hl%d" % t][:, :], "rq%d_%d" % (s, t))
         g.wait_ge(S.hls, ls[0])
 
 
@@ -171,7 +205,7 @@ def rank_program(g, core, T, topo):
     r = T.rank_of(core)
     S = T.sem
     V, C, M, Y = g.vector, g.scalar, g.tensor, g.sync
-    ops, hist = [], {}
+    ops, hist, lift = [], {}, [None]
     psum = {n for n in SCRATCH if SCRATCH[n][0] == "psum"}
 
     def X(n, lo=0, hi=None, st=1):
@@ -198,6 +232,10 @@ def rank_program(g, core, T, topo):
     def XR(n, a, lo, hi):
         w = T[n].shape[2]
         return (T[n][:, a, lo:hi], n, a * w + lo, a * w + hi)
+
+    def top(n, lo=0, hi=KW):
+        p, o, w = POOL.get(n, (n, 0, 0))
+        return (T[p][0:1, o + lo:o + hi], n, lo, hi)
 
     def IND(win, off):
         return (win[0].indirect(off[0]), win, off)
@@ -229,15 +267,14 @@ def rank_program(g, core, T, topo):
                     deps.add(j)
         for (ap, n, lo, hi), w in acc:
             hist.setdefault(n, ([], []))[w].append((i, w, lo, hi, q))
-        ops.append({"q": q, "busy": busy, "fire": fire, "deps": deps - {i}, "after": after - deps - {i}, "sem": sem, "cnt": cnt, "lat": lat, "team": team})
+        ops.append({"q": q, "busy": busy, "fire": fire, "deps": deps - {i}, "after": after - deps - {i}, "sem": sem, "cnt": cnt, "lat": lat, "team": team,
+                    "rank": i if lift[0] is None else lift[0] + i * 1e-6})
         return i
 
     def vc(n, f):
         return max(64.0, n * f) * CY
 
     def tt(out, a, b, op):
-        if len(a) == 3:
-            return add("v", 50 + vc(size(b), GA), lambda: V.tensor_tensor(out[0], a[0], b[0], op), split(a) + [b], [out])
         return add("v", vc(size(out), 1 if (a[1] in psum or b[1] in psum) else 2), lambda: V.tensor_tensor(out[0], a[0], b[0], op), [a, b], [out])
 
     def ts(out, a, s1, s2, o1, o2=None):
@@ -251,8 +288,6 @@ def rank_program(g, core, T, topo):
         return add("v", vc(size(out), 0.5 if short(out, a) else 1), fn, rd, [out])
 
     def cp(out, a):
-        if len(a) == 3:
-            return add("v", 50 + vc(size(out), GA), lambda: V.tensor_copy(out[0], a[0]), split(a), [out])
         if len(out) == 3:
             return add("v", 50 + vc(size(a), SC), lambda: V.tensor_copy(out[0], a[0]), [a, out[2]], [out[1]])
         return add("v", vc(size(out), 0.5 if short(out, a) else 1), lambda: V.tensor_copy(out[0], a[0]), [a], [out])
@@ -265,10 +300,7 @@ def rank_program(g, core, T, topo):
 
     def act(out, a, func=AF.Copy, bias=0.0, scale=1.0):
         cost = 65 + vc(size(out), GA) if len(a) == 3 else 60 + vc(size(out), 1)
-        cols = [s for s in (bias, scale) if isinstance(s, tuple)]
-        bv = bias[0] if isinstance(bias, tuple) else bias
-        sv = scale[0] if isinstance(scale, tuple) else scale
-        return add("s", cost, lambda: C.activation(out[0], a[0], func, bias=bv, scale=sv), split(a) + cols, [out])
+        return add("s", cost, lambda: C.activation(out[0], a[0], func, bias=bias, scale=scale), split(a), [out])
 
     def mm(lst, first=True, last=True, apart=False):
         rd, wr = {}, {}
@@ -279,7 +311,7 @@ def rank_program(g, core, T, topo):
             for i, (o, l, x) in enumerate(lst):
                 ins = M.matmul(o[0], l[0], x[0], apart or first and i == 0, apart or last and i == len(lst) - 1)
             return ins
-        cost = sum(max(64.0, size(x)) * (1 if short(x) else 4) for o, l, x in lst) * PCY
+        cost = sum(max(min(64.0, size(l)), size(x)) * (1 if short(x) else 4) for o, l, x in lst) * PCY
         return add("t", cost, fire, list(rd.values()), list(wr.values()))
 
     def dma(q, out, in_, sem, lat, extra=()):
@@ -290,12 +322,19 @@ def rank_program(g, core, T, topo):
         return add(q, 60, lambda: e.dma_start(dst_, src), rd, wr, sem=sem, cnt=16, lat=lat, extra=extra)
 
     hs = helpers(T, topo, core)
-    opp = T.cores[(r + 2) % N]
     near = topo.engines(core, hs[0])
 
     def dst(c):
         rid, pid = topo.addr(c, core)
         return DstId(rid=rid, pnc=pid)
+
+    def quarters(c0, w, land, h0, far_sem, sem, busy, extra=()):
+        tr = [RemoteDMATransfer(dst_ids=[dst(h)], dma_engine_mask=bits(near[i // 2::2][i % 2::2]), remote_sem=S[far_sem],
+                                srcs=[T.lm0[:, c0 + i * w:c0 + (i + 1) * w]], dsts=[T[land][:, h0:h0 + w]]) for i, h in enumerate(hs)]
+        return add("g", busy, lambda: g.remote_dma_fused(tr, local_sem=S[sem]), [X("lm0", c0, c0 + len(hs) * w)], [], sem=sem, cnt=len(near), lat=5000, extra=extra)
+
+    def arrivals(s):
+        return sum(len(topo.engines(h, core)) for h in helpers(T, topo, T.cores[(r + s) % N]))
 
     F0, F1 = P0 + B, 2048
     cut, back = len(hs) * PC[0], [()]
@@ -305,15 +344,9 @@ def rank_program(g, core, T, topo):
     dma("y", X("ft", P0, F0), T.feat[:, P0:F0], "l_fa", 4000)
     dma("s", X("lm0", cut, H), T.lim[:, cut:H], "l_lim1", 6000)
     for p in range(2):
-        c0, w, h0 = cut * p, PC[p], PC[0] * p
-        tr = [RemoteDMATransfer(dst_ids=[dst(h)], dma_engine_mask=bits(near[i // 2::2][i % 2::2]), remote_sem=S["ha%d" % p],
-                                srcs=[T.lm0[:, c0 + i * w:c0 + (i + 1) * w]], dsts=[T.hl[:, h0:h0 + w]]) for i, h in enumerate(hs)]
-        out = add("g", 2000, lambda tr=tr, p=p: g.remote_dma_fused(tr, local_sem=S["bulk%d" % p]), [X("lm0", c0, c0 + len(hs) * w)], [], sem="bulk%d" % p, cnt=len(near),
-                  lat=5000)
-        back.append((out,))
+        back.append((quarters(cut * p, PC[p], "hl", PC[0] * p, "ha%d" % p, "bulk%d" % p, 2000),))
     for s in range(1, N):
-        cnt = 2 * sum(len(topo.engines(h, core)) for h in helpers(T, topo, T.cores[(r + s) % N]))
-        add("x", 0, None, [], [X("lm%d" % s, 0, H)], sem="lm_%d" % s, cnt=cnt, lat=AT1 + 4000 * (s - 1))
+        add("x", 0, None, [], [X("lm%d" % s, 0, H)], sem="lm_%d" % s, cnt=2 * arrivals(s), lat=AT1 + 4000 * (s - 1))
     dma("y", X("ft", 0, P0), T.feat[:, 0:P0], "l_fb", (9500, 6000, 4000)[WB], back[WB])
     dma("y", X("ft", F0, F1), T.feat[:, F0:F1], "l_fc", 10000)
     dma("y", X("ci", B, 2 * B), T.comp[:, B:2 * B], "l_ci2", (11000, 5000, 3000)[WC], back[WC])
@@ -324,7 +357,7 @@ def rank_program(g, core, T, topo):
     cp(X("pf"), X("pi"))
     cp(X("iof"), X("io"))
     ts(X("idw"), X("iof"), X("pf"), None, A.is_equal)
-    ID, J, J8 = X("idw", 0, W), X("iof", 0, W), X("iof", 0, 8)
+    ID, J8 = X("idw", 0, W), X("iof", 0, 8)
     cp(X("hdf"), X("hdi"))
     for z, (u0, u1) in enumerate(((0, 6), (6, 12), (12, 16))):
         pd = "pd%d" % z
@@ -336,20 +369,24 @@ def rank_program(g, core, T, topo):
     ts(X("wh"), X("iof", 0, W, 16), X("pf"), 32.0, A.is_equal, A.mult)
     for n, w in (("idq", 1.0 / 32), ("nid", -1.0), ("idf", 1.0), ("wi", 4096.0)):
         ts(X(n), ID, w, None, A.mult)
-    for n, w in (("w1", 32.0 * 613), ("w2", float(BIG)), ("wp", 1.0), ("wm", -1.0)):
+    for n, w in (("w1", 32.0 * 613), ("w2", float(BIG)), ("wp", 1.0), ("a1", 1.0), ("a32", 1.0 / 32)):
         ts(X(n), J8, X("gf"), w, A.is_equal, A.mult)
-    ONE = X("ones", 0, W)
+    ONE, ONK = X("ones"), X("ones", 0, KW)
     ms(ONE, 1.0)
-    ts(X("cst"), X("idw", 1, 2), -9.0 * BIG, None, A.mult)
-    ts(X("ca"), X("idw", 2, 3), -256.0, X("cst"), A.mult, A.add)
-    ts(X("kq0"), ONE, X("ca"), None, A.mult)
+    ts(X("c1"), X("idw", 1, 2), -9.0 * BIG / 65536, None, A.mult)
+    ts(X("cq"), X("idw", 2, 3), -1.0, X("c1"), A.mult, A.add)
+    ts(X("lm0", H, HK), ONK, X("cq"), None, A.mult)
+    ts(X("c2"), X("idw", 0, 1), 32.0, None, A.mult)
+    ts(X("c3"), X("idw", 1, 2), 65536.0, X("c2"), A.mult, A.add)
+    ts(X("cw"), X("idw", 2, 3), 256.0, X("c3"), A.mult, A.add)
+    ts(X("kl"), ONE, X("cw"), None, A.mult)
     for b in range(NB):
         ms(X("ch%d" % b, W, W + 16), 0.0)
 
     def fr(t, eng):
         n = "fr%d" % t
-        step = W if eng == "v" else GST if t == 1 else B
-        for m0 in range(B - step, -1, -step) if eng == "v" else range(0, B, step):
+        step = W if eng == "v" else GST
+        for m0 in range(B - step, -1, -step):
             i = X("ft", P0 + B * t + m0, P0 + B * t + m0 + step)
             for k in range(16):
                 o = X(n, 16 * m0 + k, 16 * (m0 + step), 16)
@@ -359,37 +396,23 @@ def rank_program(g, core, T, topo):
                     add("g", 170 + 2 * step * CY, lambda o=o, i=i: g.affine_select(o[0], i[0], [[0, step]], A.is_gt, 0.0, 1, 0), [i], [o], team=n)
 
     fr(0, "v")
-
     fr(1, "g")
-    fr(2, "g")
 
     def late():
         cp(X("cl", B, 2 * B), X("ci", B, 2 * B))
+        cp(X("cl", 2 * B, 768), X("ci", 2 * B, 768))
         ts(X("km"), X("io", 0, W), 15, None, A.bitwise_and)
         cp(X("kf"), X("km"))
-        act(X("keep"), X("kf"), AF.Sigmoid, bias=-128.0, scale=256.0)
+        ts(X("keep"), X("kf"), 1.0, None, A.min)
         ts(X("rsa"), X("keep"), 2.0e9, -1.0e9, A.mult, A.add)
         ts(X("rsb"), X("keep"), -2.0e9, 1.0e9, A.mult, A.add)
         ts(X("on32"), ONE, 1.0 / 32, None, A.mult)
-        ts(X("p0m"), ONE, X("idw", 0, 1), 32.0, A.mult, A.mult)
-        ts(X("dmy"), X("pf"), 2.0, float(H), A.mult, A.add)
+        ts(X("dmy"), X("pf"), 2.0, float(HK), A.mult, A.add)
+        for t in range(NT - 1):
+            ts(X("up%d" % t, NB * UP, NB * UP + KW), ONK, X("cq"), None, A.mult)
         for b in range(NB):
             ms(X("lz%d" % b), 0.0)
-            ms(X("dz%d" % b), 0.0)
             ms(X("wz%d" % b), 0.0)
-            for t in range(NT - 1):
-                ms(X("up%d" % t, b * UP + W + 8, (b + 1) * UP), 0.0)
-        ts(X("ri"), X("pi"), 15, None, A.bitwise_and)
-        ts(X("r0"), X("ri"), 0.0, None, A.is_equal)
-        ts(X("n0"), X("r0"), -2.0, 1.0, A.mult, A.add)
-        ts(X("d1"), ID, X("n0"), None, A.mult)
-        ts(X("ef"), ID, X("r0"), -256.0, A.mult, A.mult)
-        ts(X("id8"), ID, 8.0, None, A.mult)
-        ts(X("idm8"), ID, -8.0, None, A.mult)
-        ts(X("wf", 8, 16), X("wh"), -1.0 / 32, None, A.mult)
-        tt(X("wf", 0, 8), X("wp"), X("wf", 8, 16), A.add)
-        tt(X("st"), J, X("kf"), A.subtract)
-        ts(X("sel0"), X("st"), X("pf"), None, A.is_equal)
         ts(X("hf"), X("keep"), 0.5, None, A.mult)
         ts(X("st"), X("keep"), -1.0, 1.0, A.mult, A.add)
         scan(X("rwa"), X("hf"), X("st"), 0.0, A.mult, A.add)
@@ -398,16 +421,16 @@ def rank_program(g, core, T, topo):
         scan(X("rwb"), X("hf"), X("st"), 2.0 ** 57, A.mult, A.add)
         ts(X("e0", 0, 1), X("idw", 0, 1), 1.0, None, A.mult)
         ts(X("e0", 1, 2), X("idw", 0, 1), 2.5, None, A.mult)
-        mm([(XR("pk0", 0, 0, 1), X("rwa"), X("e0", 0, 1))])
-        mm([(XR("pk0", 0, 1, 2), X("rwb"), X("e0", 1, 2))])
-        ts(X("wu"), X("wp"), XR("pk0", 0, 0, 1), None, A.mult)
-        cp(X("thr"), XR("pk0", 0, 1, 2))
-
-    rot, mark, held = [0], {}, {}
-
-    def hold(i, q):
-        if q in held:
-            ops[i]["after"].add(held[q])
+        mm([(XR("px1", 12, 0, 1), X("rwa"), X("e0", 0, 1))])
+        mm([(XR("px1", 12, 1, 2), X("rwb"), X("e0", 1, 2))])
+        ts(X("gm"), X("io", 0, W), 4, None, A.logical_shift_right)
+        cp(X("gk"), X("gm"))
+        ts(X("wu"), X("gk"), X("gf"), XR("px1", 12, 0, 1), A.is_equal, A.mult)
+        cp(X("thr"), XR("px1", 12, 1, 2))
+        ts(X("ri"), X("pi"), 15, None, A.bitwise_and)
+        cp(X("rf"), X("ri"))
+        ts(X("own"), X("kf"), X("rf"), None, A.is_equal)
+        ts(X("bar"), X("own"), -1.0, 2.0 ** 70, A.add, A.mult)
 
     def parts(lo, hi, most):
         n = -(-(hi - lo) // most)
@@ -425,99 +448,115 @@ def rank_program(g, core, T, topo):
     def offs(n, c0, lo, hi):
         return X(n, c0 + lo // 16, c0 + hi // 16)
 
-    def gather(out, win, lst, c0, lo, hi, other, op):
+    def gather(q, out, win, lst, c0, lo, hi, other=None, op=None, cuts=None, step=None):
         def call(a, z):
-            return V.tensor_tensor(X(out, a, z)[0], win[0].indirect(offs(lst, c0, a, z)[0]), other(a, z)[0], op)
-        for a, z in parts(lo, hi, VCH):
-            ops[tt(X(out, a, z), IND(win, offs(lst, c0, a, z)), other(a, z), op)]["piece"] = [call, a, z]
+            o, x = X(out, a, z)[0], win[0].indirect(offs(lst, c0, a, z)[0])
+            if q == "s":
+                return C.activation(o, x, AF.Copy)
+            return V.tensor_tensor(o, x, other(a, z)[0], op) if other else V.tensor_copy(o, x)
+        fix = 65 if q == "s" else 50
+        ends, made = [lo], []
+        for n in cuts or ():
+            ends.append(ends[-1] + (n or hi - lo - sum(cuts)))
+        for a, z in (zip(ends, ends[1:]) if cuts else parts(lo, hi, step or VCH)):
+            i = add(q, fix + vc(z - a, GA), None, [win, offs(lst, c0, a, z)] + ([other(a, z)] if other else []), [X(out, a, z)])
+            ops[i]["piece"] = [call, a, z, fix]
+            made.append(i)
+        return made
+
+    folds, sent = [], {}
 
     def shares(t, b):
-        mn, win, c0 = "mn%d_%d" % (t, b), X("ft", 0, P0 + B * t), B * t + MO[b]
-        if b not in SSH:
-            gather(mn, win, "cl", c0, 0, E, lambda lo, hi: FR(t, b, lo, hi), A.min)
+        mn, win, c0, nv = "mn%d_%d" % (t, b), X("ft", 0, P0 + B * t), B * t + MO[b], SV.get((t, b), 0)
+        gather("v", mn, win, "cl", c0, 0, nv, lambda lo, hi: FR(t, b, lo, hi), A.min)
+        if nv == E:
             return
-        for i, (lo, hi) in enumerate(parts(0, E, 512)):
-            x, d = X("mx", 512 * (i % 2), 512 * (i % 2) + 512), X("pd3")
-            hold(act(x, IND(win, offs("cl", c0, lo, hi))), "s")
-            mm([(d, ID, FR(t, b, lo, hi)), (d, X("nid"), x)])
-            act(X(mn, lo, hi), d, AF.Relu)
-
-    def table():
-        for lo, hi in parts(0, P0, 512):
-            d = X("pd3", 0, hi - lo)
-            mm([(d, X("d1"), X("ft", lo, hi)), (d, X("ef"), X("htab", lo, hi))])
-            act(X("tab", lo, hi), d)
-
-    def both(t, b):
-        gather("mf", X("tab", 0, P0 + B * t), "cl", B * t + MO[b], 0, E, lambda lo, hi: FR(t, b, lo, hi), A.min)
-
-    def unpack(t, b):
-        c0, pk, ch = B * t + MO[b], "pk%d" % b, X("ch%d" % b, 0, W)
-        for k0 in range(0, 16, 4):
-            mm([(XI(pk, 0, 16, k), col("mf", k), X("wf")) for k in range(k0, k0 + 4)], apart=True)
-        mi, mj, u = X("mi%d" % b), X("mj%d" % b), bank(W)
-        cp(mi, X3(pk, 8, 16))
-        ts(mj, mi, 3, 32 * (H - 1), A.arith_shift_right, A.bitwise_and)
-        cp(ch, mj)
-        to_list(b)
-        mm([(u, X("ft", P0 + c0, P0 + c0 + W), X("sel0")), (u, X("id8"), ch)])
-        tt(X("v0"), mi, u, A.min)
-        act(X("v1"), X3(pk, 0, 8))
-        mm([(X3(pk, 0, 8), X("idf"), X("v1")), (X3(pk, 0, 8), X("idf"), X("v0")), (X3(pk, 0, 8), X("idm8"), ch)], last=False)
+        mx, tb, to = "mx%d_%d" % (t, b), "%d%d" % (t, b), mirror(T, topo, core)
+        gather("s", mx, win, "cl", c0, nv, E, step=SHS)
+        tr = [RemoteDMATransfer(dst_ids=[dst(to)], dma_engine_mask=bits(near), remote_sem=S["fa" + tb], srcs=[X(mx, nv, E)[0], FR(t, b, nv, E)[0]], dsts=[X(mn, nv, E)[0]], alu_op=3)]
+        i = add("g", 1200, lambda: g.remote_dma_fused(tr, local_sem=S["fl" + tb]), [X(mx, nv, E), FR(t, b, nv, E)], [], sem="fl" + tb, cnt=len(near), lat=ATF // 2,
+                extra=sent[t - 1] if t else back[2])
+        ops[i]["after"] |= set(folds[-1:])
+        folds.append(i)
+        add("x", 0, None, [], [X(mn, nv, E)], sem="fb" + tb, cnt=len(topo.engines(to, core)), lat=ATF // 2, extra=(i,))
 
     def to_list(b):
         px = "px%d" % b
-        mm([(X3(px, 0, 8, 16, 32), X("ch%d" % b, 0, W), X("idq"))])
-        cp(X("ul%d" % b), X3(px, 0, 8, 16, 32))
+        return [mm([(X3(px, 0, 8, 16, 32), X("ch%d" % b, 0, W), X("idq"))])], [cp(X("ul%d" % b), X3(px, 0, 8, 16, 32))]
+
+    def find(t, b):
+        win, hx, c0 = X("htab", 0, P0 + B * t), "hx%d" % b, B * t + MO[b]
+        hv = HV[t] if b == 0 else 0
+        gather("v", hx, win, "cl", c0, 0, hv, step=SHS)
+        gather("s", hx, win, "cl", c0, hv, E, step=SHS)
 
     def heads(t, b):
-        win, hx, px, c0 = X("htab", 0, P0 + B * t), "hx%d" % b, "px%d" % b, B * t + MO[b]
-        hv = (HV1 if t else HV) if b == 0 else 0
-        for lo, hi in parts(0, hv, 1024 if t == 0 else VCH):
-            cp(X(hx, lo, hi), IND(win, offs("cl", c0, lo, hi)))
-        for lo, hi in parts(hv, E, HCH):
-            act(X(hx, lo, hi), IND(win, offs("cl", c0, lo, hi)))
+        hx, px = "hx%d" % b, "px%d" % b
         mm([(XI(px, 0, 8, k), col(hx, k), X("wh")) for k in range(16)], apart=True)
         (act if "h" in OFF else cp)(X("ch%d" % b, 0, W), X3(px, 0, 8, 0, 16))
         to_list(b)
 
-    def visit(t, b, a, between):
-        lm, cm, px = X("lm%d" % a, 0, H), "cm%d" % b, "px%d" % b
-        x, ch = X3(px, 0, 8, 0, 16), X("ch%d" % b, 0, W)
-        todo, nv = [], E - ((NS2 if t in BOTH else NS0) if (a, b) == (0, 0) else NS3 if (a, b) == (N - 1, 1) else NS1 if t else NS)
-        for lo, hi in parts(nv, E, SCH):
-            xg, d = X("xg%d" % b, lo - nv, hi - nv), bank(hi - lo)
-            act(xg, IND(lm, offs("ul%d" % b, 0, lo, hi)))
-            mm([(d, ID, FR(t, b, lo, hi)), (d, X("nid"), xg)])
-            todo.append((X(cm, lo, hi), d))
-        act(X("sq%d" % b), ch, AF.Square, bias=16.0, scale=1.0 / 32)
-        mm([(x, X("idf"), X("sq%d" % b)), (x, X("kq%d" % (a if t else 0)), ONE)], last=False)
-        if between:
-            between()
-        for o, d in todo:
-            mark["s"] = act(o, d, AF.Sigmoid, bias=-128.0, scale=256.0)
-        gather(cm, lm, "ul%d" % b, 0, 0, nv, lambda lo, hi: FR(t, b, lo, hi), A.is_lt)
-        mm([(XI(px, 0, 8, k), col(cm, k), X(w)) for k in range(16) for w in ("w1", "w2")], first=False)
-        tt(X("mi%d" % b), x, ch, A.max)
-        ts(X("mj%d" % b), X("mi%d" % b), 32 * (H - 1), None, A.bitwise_and)
-        cp(ch, X("mj%d" % b))
-        if a < N - 1:
-            to_list(b)
+    def notes(t, a):
+        return "lr%d_%d" % (a, t - 1) if t and a in RS else "lm%d" % a
 
-    def lists(out, pad, idn):
-        mm([(out, X(pad, 15 - u, 15 - u + W), X(idn, u, W, 16)) for u in range(16)])
+    def tile(t, a):
+        if t == 0 or a == 0:
+            return X("lm0", H, HK)
+        return X(notes(t, a), H, HK) if a in RS else X("ru%d_%d" % (a, t - 1), NB * UP, NB * UP + KW)
+
+    def kind(t, a, b):
+        if (a, b) == (N - 1, NB - 1):
+            return "last"
+        if b == 0 and (a == 0 or (t, a) == (0, 1)):
+            return "free"
+        return "after" if t and b == 0 and a in MSG else "plain"
+
+    def bank(b, i, n=W):
+        return X("pd%d" % (2 * b + i), 0, n)
+
+    def visit(t, b, a):
+        lm, cm, px = X(notes(t, a), 0, H), "cm%d" % b, "px%d" % b
+        x, ch = X3(px, 0, 8, 0, 16), X("ch%d" % b, 0, W)
+        todo, nv = [], E - (NS0 if (a, b) == (0, 0) else NS3 if (a, b) == (N - 1, 1) else NSA if kind(t, a, b) == "after" else NS1 if t else NS)
+        v = {"f": [], "g": [], "x": []}
+        for i, (lo, hi) in enumerate(parts(nv, E, SCH)):
+            xg, d = X("xg%d" % b, lo - nv, hi - nv), bank(b, i, hi - lo)
+            v["f"].append(mm([(d, ID, FR(t, b, lo, hi))], last=False))
+            v["g"].append(act(xg, IND(lm, offs("ul%d" % b, 0, lo, hi))))
+            v["x"].append(mm([(d, X("nid"), xg)], first=False))
+            todo.append((X(cm, lo, hi), d))
+        v["sq"] = [act(X("sq%d" % b), ch, AF.Square, bias=16.0, scale=1.0 / 32)]
+        v["open"] = [mm([(x, X("idf"), X("sq%d" % b))] + [(X3(px, 4 * h, 4 * h + 4, 0, 16), X("kl"), tile(t, a)) for h in range(2)], last=False)]
+        v["s"] = [act(o, d, AF.Sigmoid, bias=-128.0, scale=256.0) for o, d in todo]
+        v["v"] = gather("v", cm, lm, "ul%d" % b, 0, 0, nv, lambda lo, hi: FR(t, b, lo, hi), A.is_lt, CUTS[kind(t, a, b)])
+        v["sum"] = [mm([(XI(px, 0, 8, k), col(cm, k), X(w)) for k in range(16) for w in ("w1", "w2")], first=False)]
+        v["new"] = [tt(X("mi%d" % b), x, ch, A.max), ts(X("mj%d" % b), X("mi%d" % b), 32 * (H - 1), None, A.bitwise_and), cp(ch, X("mj%d" % b))]
+        v["turn"], v["list"] = to_list(b) if a < N - 1 else ([], [])
+        return v
+
+    def chain(calls):
+        for i, j in zip(calls, calls[1:]):
+            ops[j]["after"].add(i)
+
+    def beat(last, v, nxt, fill):
+        p, brief = v["v"], last["new"] + last["list"]
+        first = v.get("scat", p[:1])
+        rest = p if "scat" in v else p[1:]
+        chain(first + [i for pair in zip(brief, rest) for i in pair] + rest[len(brief):] + nxt.get("scat", nxt.get("v", []))[:1])
+        chain(v["g"] + v["s"] + nxt.get("sq", []) + nxt.get("g", [])[:1])
+        f = nxt.get("f", [])
+        if "scat" in v:
+            chain(last["sum"] + v["open"] + last["turn"] + v["x"][:1] + f[:1] + v["x"][1:] + f[1:] + fill + v["sum"])
+        else:
+            chain(last["sum"] + v["x"] + v["open"] + f[:1] + last["turn"] + f[1:] + fill + v["sum"])
 
     def sums(t, b):
         pk = "pk%d" % b
-        mm([(X3(pk, 0, 8), X("wi"), ONE)] + [(XI(pk, 0, 8, k), col("mn%d_%d" % (t, b), k), X("wm" if b in SSH else "wp")) for k in range(16)], last=False)
-
-    def bank(n):
-        rot[0] = (rot[0] + 1) % 3
-        return X("pd%d" % rot[0], 0, n)
+        return mm([(X3(pk, 0, 8), X("wi"), ONE)] + [(XI(pk, 0, 8, k), col("mn%d_%d" % (t, b), k), X("wp")) for k in range(16)], last=False)
 
     def elect(t, b):
         px, pk, eb, ch = "px%d" % b, "pk%d" % b, "eb%d" % b, X("ch%d" % b, 0, W)
-        key, de = X3(pk, 0, 8), bank(W)
+        key, de = X3(pk, 0, 8), bank(b, 0)
         mm([(X3(px, 8, 16, 0, 16), ID, ch), (X3(px, 8, 16, 16, 32), ID, ch)], apart=True)
         mm([(de, ID, X("ch%d" % b, 1, W + 1)), (de, X("nid"), ch)])
         act(X("de%d" % b), de)
@@ -533,172 +572,166 @@ def rank_program(g, core, T, topo):
                     run.append((X3(pk, 0, 8, 0, d), X("wi"), X3(eb, 8 * d - 8, 8 * d, 16 - d, 16)))
             mm(run, first=False, last=8 in ds)
         act(X("sq%d" % b), key)
-        back = X("sq%d" % b, 0, W, -1)
-        for h, (rs, o1, o2) in enumerate((("rsa", A.min, A.max), ("rsb", A.max, A.min))):
-            lo, hi = W * h, W * h + W
-            scan(X("rr%d" % b, lo, hi, -1), X(rs), back, 0.0, o1, o2)
-            tt(X("nr%d" % b, lo, hi), X("rr%d" % b, lo, hi), key, A.not_equal)
-            scan(X("yy%d" % b, lo, hi, -1), X("de%d" % b, 0, W, -1), X("nr%d" % b, lo, hi, -1), 0.0, A.add, A.mult)
-            out = X("lz%d" % b, 15, 15 + W, 16) if h else X("wz%d" % b, 0, W, 16)
-            tt(out, X("yy%d" % b, lo, hi, 16), X("ch%d" % b, 0, W, 16), A.add)
-            if h == 0:
-                c0 = P0 + B * t + MO[b]
-                mm([(X3(px, 0, 8, 0, 16), X("wz%d" % b), X("idq"))])
-                act(X("htab", c0, c0 + W), X3(px, 0, 8, 0, 16))
-                if t < max(BOTH, default=0):
-                    d = bank(W)
-                    mm([(d, X("d1"), X("ft", c0, c0 + W)), (d, X("wz%d" % b), X("idm8"))])
-                    (cp if b and "t" not in OFF else act)(X("tab", c0, c0 + W), d)
 
-    def losers(t, b):
-        px, up, lf, c0 = "px%d" % b, "up%d" % t, "lf%d" % b, P0 + B * t + MO[b]
-        row, lst, dup, old = X("lbs%d" % b), XR(px, 8, 0, 8), XR(px, 9, 0, 8), X("old%d" % b)
-        scan(X("lr%d" % b), X("keep"), X("lz%d" % b, 15, 15 + W), 0.0, A.mult, A.add)
-        mm([(X3(px, 0, 8, 16, 32), X("lr%d" % b), X("idq"))])
-        lists(lst, "lz%d" % b, "idq")
-        (act if "r" in OFF else cp)(row, X3(px, 0, 8, 16, 32))
-        (act if "l" in OFF else cp)(X(lf), lst)
-        cp(X("lu%d" % b), lst)
-        dif, new = bank(W), bank(W)
-        act(old, IND(X("lm0", 0, H), X("lu%d" % b)))
-        mm([(dif, ID, X("ft", c0, c0 + W)), (dif, X("nid"), old)])
-        run = []
-        for a in range(8):
-            i = X("ind%d" % b, W * a, W * a + W)
-            ts(i, row, X(lf, a, a + 1), 2.0 ** (56 - 16 * a), A.is_equal, A.mult)
-            run.append((dup, i, X("wu")))
-        mm(run)
-        ts(X("clp%d" % b), dif, -32.0, 32.0, A.max, A.min)
-        mm([(new, ID, old), (new, ID, X("clp%d" % b))])
-        act(X(up, b * UP, b * UP + W), new)
-        ts(X("dz%d" % b, 15, 15 + W, 16), dup, X("thr"), X("dmy"), A.is_ge, A.mult)
-        lists(lst, "dz%d" % b, "idw")
-        tt(X(up, b * UP + W, b * UP + W + 8), lst, X(lf), A.max)
+    def pick(t, b, h):
+        rs, o1, o2 = (("rsa", A.min, A.max), ("rsb", A.max, A.min))[h]
+        lo, hi = W * h, W * h + W
+        scan(X("rr%d" % b, lo, hi, -1), X(rs), X("sq%d" % b, 0, W, -1), 0.0, o1, o2)
+        tt(X("nr%d" % b, lo, hi), X("rr%d" % b, lo, hi), X3("pk%d" % b, 0, 8), A.not_equal)
+        scan(X("yy%d" % b, lo, hi, -1), X("de%d" % b, 0, W, -1), X("nr%d" % b, lo, hi, -1), 0.0, A.add, A.mult)
+        tt(X(("wz%d", "lz%d")[h] % b, 0, W, 16), X("yy%d" % b, lo, hi, 16), X("ch%d" % b, 0, W, 16), A.add)
+        if h == 0:
+            c0, won = P0 + B * t + MO[b], bank(b, 1)
+            mm([(won, X("wz%d" % b), X("idq"))])
+            act(X("htab", c0, c0 + W), won)
 
-    def kq(s, k):
-        act(X("kc%d" % s), k)
-        act(X("kq%d" % s), X("p0m"), AF.Identity, bias=X("ca"), scale=X("kc%d" % s))
+    def losers(t, b, stage):
+        px, pk, up, lf, c0 = "px%d" % b, "pk%d" % b, "up%d" % t, "lf%d" % b, P0 + B * t + MO[b]
+        row, lst, dup, old = X("lbs%d" % b), XR(px, 8, 0, 8), X3(px, 12, 16), X("old%d" % b)
+        dif, new = bank(b, 0), bank(b, 1)
+        if stage == "one":
+            scan(X("lr%d" % b), X("keep"), X("lz%d" % b), 0.0, A.mult, A.add)
+            mm([(X3(pk, 16, 24), X("lr%d" % b), X("idq"))])
+            scan(X("lk%d" % b), X("lr%d" % b), X("own"), 0.0, A.add, A.mult)
+            mm([(lst, X("lk%d" % b), X("a32"))])
+            (act if "r%d" % b in OFF else cp)(row, X3(pk, 16, 24))
+            (act if "l%d" % b in OFF else cp)(X(lf), lst)
+            cp(X("lu%d" % b), lst)
+            act(old, IND(X("lm0", 0, H), X("lu%d" % b)))
+            mm([(dif, ID, X("ft", c0, c0 + W)), (dif, X("nid"), old)])
+        elif stage == "two":
+            mm([(dup, ID, X("bar"))], last=False)
+            for a0 in range(0, 8, 2):
+                run = []
+                for a in range(a0, a0 + 2):
+                    i = X("ind%d" % b, W * a, W * a + W)
+                    ts(i, row, X(lf, a, a + 1), 2.0 ** (56 - 16 * a), A.is_equal, A.mult)
+                    run.append((dup, i, X("wu")))
+                mm(run, first=False, last=a0 == 6)
+            ts(X("dz%d" % b), dup, X("thr"), X("dmy"), A.is_ge, A.mult)
+            mm([(lst, X("dz%d" % b), X("a1"))])
+        else:
+            ts(X("clp%d" % b), dif, -32.0, 32.0, A.max, A.min)
+            mm([(new, ID, old), (new, ID, X("clp%d" % b))])
+            act(X(up, b * UP, b * UP + W), new)
+            tt(X(up, b * UP + W, b * UP + W + 8), lst, X(lf), A.max)
 
     def kappa(t):
-        o, ks, k = XR("pk0", 19, 0, 8), X("ks"), X("up%d" % t, UP + W + 8, UP + W + 9)
-        mm([(o, X("on32"), X("wz%d" % b, 0, W, 16)) for b in range(NB)])
-        add("v", vc(8, 1), lambda: V.tensor_reduce(ks[0], o[0], AxisListType.X, A.add), [o], [ks])
-        cp(X("ki"), ks)
-        ts(X("kj"), X("ki"), 255, None, A.bitwise_and)
-        cp(k, X("kj"))
-        kq(0, k)
+        o = (T.pk0[0:1, 24:28, :], "pk0", 24 * 16, 28 * 16)
+        mm([(o, X("wz%d" % b, 16 * u, 16 * u + 1), X("on32", 0, KW)) for b in range(NB) for u in range(8)])
+        cp(top("ki"), o)
+        ts(top("kj"), top("ki"), 255, None, A.bitwise_and)
+        cp(top("up%d" % t, NB * UP, NB * UP + KW), top("kj"))
+        cp(top("lm0", H, HK), top("kj"))
 
     def scat(s, up, b):
         ou = X("ou%d" % s, 16 * b, 16 * b + 8)
         cp(ou, X(up, b * UP + W, b * UP + W + 8))
-        cp(IND(X("lm%d" % s), ou), X(up, b * UP, b * UP + W))
+        return cp(IND(X("lm%d" % s), ou), X(up, b * UP, b * UP + W))
 
     def send(t, b):
-        lo, hi = b * UP, (b + 1) * UP
+        lo, hi = span(b)
         up, tb = T["up%d" % t][:, lo:hi], "%d%d" % (t, b)
-        es = message_engines(T, topo, core)
-        to = [(hs[0], "hu", "hu%d"), (opp, "uq2_", "ru2_%d"), (hs[1], "hu", "hu%d")]
-        tr = [RemoteDMATransfer(dst_ids=[dst(c)], dma_engine_mask=bits(e), remote_sem=S[sem + tb], srcs=[up], dsts=[T[n % t][:, lo:hi]]) for e, (c, sem, n) in zip(es, to)]
-        sent = add("g", 1200, lambda: g.remote_dma_fused(tr, local_sem=S["lo" + tb]), [X("up%d" % t, lo, hi)], [], sem="lo" + tb, cnt=len(near), lat=2500)
-        for s in range(1, N):
-            src = T.cores[(r + s) % N]
-            cnt = len(message_engines(T, topo, src)[1] if s == 2 else topo.engines(helpers(T, topo, src)[s // 2], core))
-            add("x", 0, None, [], [X("ru%d_%d" % (s, t), lo, hi)], sem="uq%d_%s" % (s, tb), cnt=cnt, lat=ATU + 1500 * (s // 3), extra=(sent,))
+        tr, cnt = [], 0
+        for s, (to, es) in routes(T, topo, core, b).items():
+            sem, n = ("hu" + tb, "hu%d" % t) if to in hs else ("uq%d_%s" % (s, tb), "ru%d_%d" % (s, t))
+            tr.append(RemoteDMATransfer(dst_ids=[dst(to)], dma_engine_mask=bits(es), remote_sem=S[sem], srcs=[up], dsts=[T[n][:, lo:hi]]))
+            cnt += len(es)
+        i = add("g", 1200, lambda: g.remote_dma_fused(tr, local_sem=S["lo" + tb]), [X("up%d" % t, lo, hi)], [], sem="lo" + tb, cnt=cnt, lat=2500)
+        sent[t] = (i,)
+        for s in MSG:
+            to, es = routes(T, topo, T.cores[(r + s) % N], b)[s]
+            add("x", 0, None, [], [X("ru%d_%d" % (s, t), lo, hi)], sem="uq%d_%s" % (s, tb), cnt=len(es if to == core else topo.engines(to, core)), lat=ATU - 2500 + 1500 * (s // 3),
+                extra=(i,))
 
-    def receive(t, s):
-        n = "ru%d_%d" % (s, t)
-        scat(s, n, 0)
-        kq(s, X(n, UP + W + 8, UP + W + 9))
-        scat(s, n, 1)
+    def anew(t):
+        i = quarters(0, HK // len(hs), "hl%d" % t, 0, "hr%d" % t, "rl%d" % t, 1200, sent[t])
+        for n, s in enumerate(RS):
+            add("x", 0, None, [], [X("lr%d_%d" % (s, t))], sem="rq%d_%d" % (s, t), cnt=arrivals(s), lat=ATR - 5000 + 4000 * n, extra=(i,))
 
+    seen, added = {}, {}
+
+    def stage(name, base, call, *args):
+        lift[0] = base + STAGES.split().index(name) / 100
+        call(*args)
+        lift[0] = None
+
+    for b in range(NB):
+        find(0, b)
+        heads(0, b)
+    late()
     for t in range(NT):
-        heads(t, 0)
-        if t in BOTH:
-            both(t, 1)
-        else:
-            heads(t, 1)
-        if t == 0:
-            late()
         for a in range(N):
-            if a == N - 1:
-                for b in range(1 if t in BOTH else NB):
-                    shares(t, b)
-                    sums(t, b)
-            if (t, a) == TA and BOTH:
-                table()
-            if t and a:
-                receive(t - 1, a)
+            for t1, b in LATEST:
+                if LATEST[t1, b] == (t, a):
+                    shares(t1, b)
+            if (t, a) == (0, N - 1):
+                fr(2, "g")
+            new = [scat(a, "ru%d_%d" % (a, t - 1), b) for b in range(NB)] if t and a in MSG else []
             for b in range(NB):
-                visit(t, b, a, (lambda: unpack(t, 1)) if t in BOTH and (a, b) == (0, 0) else None)
-        held.update(mark)
-        if t == 0:
-            cp(X("cl", 2 * B, 768), X("ci", 2 * B, 768))
+                seen[t, a, b] = visit(t, b, a)
+            if new:
+                seen[t, a, 0]["scat"] = new
         for b in range(NB):
-            elect(t, b)
+            added[(t,) + SUMS[b]] = [sums(t, b)]
+        base, more = len(ops), t < NT - 1
         for b in range(NB):
-            if b and t < NT - 1:
-                kappa(t)
-            losers(t, b)
-            if t < NT - 1:
-                send(t, b)
+            stage("eq%d" % b, base, elect, t, b)
+            stage("min%d" % b, base, pick, t, b, 1)
+            stage("max%d" % b, base, pick, t, b, 0)
+            stage("one%d" % b, base, losers, t, b, "one")
+        if more:
+            stage("kappa", base, kappa, t)
         for b in range(NB):
-            scat(0, "up%d" % t, b)
+            stage("two%d" % b, base, losers, t, b, "two")
+            stage("end%d" % b, base, losers, t, b, "end")
+            if more:
+                stage("send", base, send, t, b)
+        for b in range(NB):
+            stage("sc%d" % b, base, scat, 0, "up%d" % t, b)
+        if more:
+            for b in range(NB):
+                stage("find%d" % b, base, find, t + 1, b)
+                stage("head%d" % b, base, heads, t + 1, b)
+            if RS:
+                anew(t)
+    for t, a, b in BEAT:
+        beat(seen[t, a - 1 + b, 1 - b], seen[t, a, b], seen.get((t, a + b, 1 - b), {}), added.get((t, a, b), []))
     add("y", 60, lambda: Y.dma_start(T.yh[:, :], T.htab[0:128:16, P0:2048]), [X("htab", P0, 2048)], [], sem="st_h", cnt=16, lat=2000)
     dma("y", T.yl[:, :], X("lm0", 0, H), "st_l", 3500)
     emit(g, T, ops)
 
 
+def joins(p, o):
+    a, b = p.get("piece"), o.get("piece")
+    return bool(a and b and a[0] is b[0] and a[2] == b[1])
+
+
+def replay(ops, queues, wake):
+    fin = [0.0] * len(ops)
+    last = {}
+    for i, q in queues:
+        o = ops[i]
+        e, d = 0.0, o["busy"]
+        for j in o["deps"]:
+            e = max(e, fin[j] + ops[j]["lat"] + wake)
+        if q != "x" and q in last:
+            p = last[q]
+            if joins(ops[p], o):
+                d -= o["piece"][3]
+            e = max(e, fin[p])
+        last[q] = i
+        fin[i] = e + d
+    return fin
+
+
 def schedule(ops):
     n = len(ops)
-    succ = [[] for _ in range(n)]
-    need = [len(o["deps"]) + len(o["after"]) for o in ops]
+    succ, pred = [[] for _ in range(n)], [[] for _ in range(n)]
     for i, o in enumerate(ops):
-        for j in o["deps"]:
-            succ[j].append((i, ops[j]["lat"] + WAKE))
-        for j in o["after"]:
-            succ[j].append((i, 0.0))
-    prio = [0.0] * n
-    for i in range(n - 1, -1, -1):
-        prio[i] = -10.0 * i + (BONUS if ops[i]["q"] == "t" and ops[i]["busy"] < SHORT else 0.0)
-    free, ready, avail, queues = {}, [0.0] * n, {}, {}
-    for i in range(n):
-        if need[i] == 0:
-            avail.setdefault(ops[i]["q"], []).append(i)
-    for _ in range(n):
-        best = None
-        for q, lst in avail.items():
-            if lst:
-                e = max(free.get(q, 0.0), min(ready[i] for i in lst))
-                if best is None or e < best[0]:
-                    best = (e, q)
-        e, q = best
-        lst = avail[q]
-        now = [i for i in lst if ready[i] <= e + 1e-6]
-        pick = max(now, key=lambda i: (prio[i], -i))
-        soon = [i for i in lst if e + 1e-6 < ready[i] <= e + LOOK and prio[i] > prio[pick] + THETA]
-        if soon and q != "x":
-            p = max(soon, key=lambda i: (prio[i], -i))
-            if e + ops[pick]["busy"] > ready[p] + FIT:
-                ok = [i for i in now if e + ops[i]["busy"] <= ready[p] + FIT]
-                pick = max(ok, key=lambda i: (prio[i], -i)) if ok else p
-        lst.remove(pick)
-        o = ops[pick]
-        e = max(e, ready[pick])
-        p = ops[queues[q][-1]].get("piece") if queues.get(q) else None
-        fin = e + o["busy"] - (50 if p and "piece" in o and p[0] is o["piece"][0] else 0)
-        if q != "x":
-            free[q] = fin
-        o["t1"] = fin
-        queues.setdefault(q, []).append(pick)
-        for j, w in succ[pick]:
-            ready[j] = max(ready[j], fin + w)
-            need[j] -= 1
-            if need[j] == 0:
-                avail.setdefault(ops[j]["q"], []).append(j)
-    pred = [[] for _ in range(n)]
-    for i in range(n):
-        for j, w in succ[i]:
-            pred[j].append((i, w))
+        for j, w in [(j, ops[j]["lat"] + WAKE) for j in o["deps"]] + [(j, 0.0) for j in o["after"]]:
+            succ[j].append((i, w))
+            pred[i].append((j, w))
 
     def place(order, before, first):
         fin, line = [0.0] * n, {}
@@ -716,34 +749,66 @@ def schedule(ops):
                 used.insert(k, (e, e + d))
             fin[i] = e + d
         return fin
-    fin, best = [o["t1"] for o in ops], None
-    for _ in range(PASSES):
-        back = place(sorted(range(n), key=lambda i: (-fin[i], -i)), succ, [o["lat"] for o in ops])
-        fin = place(sorted(range(n), key=lambda i: (-back[i], i)), pred, [0.0] * n)
-        end = max(fin[i] + ops[i]["lat"] for i in range(n))
-        if best is None or end < best[0]:
-            best = (end, fin)
-    if best:
-        queues = {}
-        for i in sorted(range(n), key=lambda i: (best[1][i], i)):
-            ops[i]["t1"] = best[1][i]
-            queues.setdefault(ops[i]["q"], []).append(i)
-    return queues
+
+    def rank(i):
+        return ops[i]["rank"]
+
+    def greedy(look, fit):
+        need = [len(p) for p in pred]
+        free, ready, avail, last, fin = {}, [0.0] * n, {}, {}, [0.0] * n
+        for i in range(n):
+            if need[i] == 0:
+                avail.setdefault(ops[i]["q"], []).append(i)
+        for _ in range(n):
+            e, q = min((max(free.get(q, 0.0), min(ready[i] for i in lst)), q) for q, lst in avail.items() if lst)
+            lst = avail[q]
+            now = [i for i in lst if ready[i] <= e + 1e-6]
+            pick = min(now, key=rank)
+            soon = [i for i in lst if e + 1e-6 < ready[i] <= e + look and rank(i) < rank(pick)]
+            if soon and q != "x":
+                p = min(soon, key=rank)
+                if e + ops[pick]["busy"] > ready[p] + fit:
+                    pick = min([i for i in now if e + ops[i]["busy"] <= ready[p] + fit], default=p, key=rank)
+            lst.remove(pick)
+            o = ops[pick]
+            fin[pick] = max(e, ready[pick]) + o["busy"] - (o["piece"][3] if q in last and joins(ops[last[q]], o) else 0)
+            if q != "x":
+                free[q] = fin[pick]
+            last[q] = pick
+            for j, w in succ[pick]:
+                ready[j] = max(ready[j], fin[pick] + w)
+                need[j] -= 1
+                if need[j] == 0:
+                    avail.setdefault(ops[j]["q"], []).append(j)
+        return fin
+    best = None
+    for look, fit in LOOKS:
+        fin = greedy(look, fit)
+        for z in range(PASSES + 1):
+            if z:
+                late = place(sorted(range(n), key=lambda i: (-fin[i], -i)), succ, [o["lat"] for o in ops])
+                fin = place(sorted(range(n), key=lambda i: (-late[i], i)), pred, [0.0] * n)
+            order = [(i, ops[i]["q"]) for i in sorted(range(n), key=lambda i: (fin[i], i))]
+            run = replay(ops, order, WAKE)
+            end = max(run[i] + ops[i]["lat"] for i in range(n))
+            if best is None or end < best[0]:
+                best = (end, order, run)
+    return best[1], best[2]
 
 
 def emit(g, T, ops):
-    queues = schedule(ops)
-    same, kept = {}, []
-    for i in queues["v"]:
-        p, o = ops[kept[-1]].get("piece") if kept else None, ops[i].get("piece")
-        if p and o and p[0] is o[0] and p[2] == o[1]:
-            p[2] = o[2]
+    if "order" not in _PLAN:
+        _PLAN["order"] = schedule(ops)
+    order, when = _PLAN["order"]
+    queues, same = {}, {}
+    for i, q in order:
+        kept = queues.setdefault(q, [])
+        if kept and joins(ops[kept[-1]], ops[i]):
+            ops[kept[-1]]["piece"][2] = ops[i]["piece"][2]
             ops[kept[-1]]["deps"] |= ops[i]["deps"]
-            ops[kept[-1]]["fire"] = lambda p=p: p[0](p[1], p[2])
             same[i] = kept[-1]
         else:
             kept.append(i)
-    queues["v"] = kept
     for o in ops:
         o["deps"] = {same.get(j, j) for j in o["deps"]}
     S = T.sem
@@ -764,9 +829,6 @@ def emit(g, T, ops):
                 continue
             total[s] = total.get(s, 0) + c
             o["tok"] = (s, total[s])
-    for o in ops:
-        if o["sem"]:
-            o["tok"] = (o["sem"], total[o["sem"]])
     known = {q: {} for q in queues}
     nxt = {q: 0 for q in queues}
     done = set(same)
@@ -776,19 +838,19 @@ def emit(g, T, ops):
             while nxt[q] < len(lst):
                 i = lst[nxt[q]]
                 o = ops[i]
-                if not o["deps"] <= done:
-                    break
                 if q == "x":
                     o["clk"] = {o["tok"][0]: o["tok"][1]}
                 else:
-                    for j in sorted(o["deps"], key=lambda j: -ops[j]["t1"]):
+                    if not o["deps"] <= done:
+                        break
+                    for j in sorted(o["deps"], key=lambda j: -when[j]):
                         s, v = ops[j]["tok"]
                         if kn.get(s, 0) < v:
                             eng[q].wait_ge(S[s], v)
                             for s2, v2 in ops[j]["clk"].items():
                                 kn[s2] = max(kn.get(s2, 0), v2)
                             kn[s] = max(kn.get(s, 0), v)
-                    ins = o["fire"]()
+                    ins = o["piece"][0](o["piece"][1], o["piece"][2]) if "piece" in o else o["fire"]()
                     o["clk"] = dict(kn)
                     if o["sem"] in DMASEMS:
                         ins.then_inc(S[o["sem"]], 16)

@@ -5,42 +5,43 @@ N, H, P0, B, NT = 4, 2048, 1280, 256, 3
 NB, W, E = 2, 128, 2048
 KW = 64
 HK = H + KW
-NS = 704
-NS0 = 256
-NS1 = 768
-NSA = 768
-NS3 = 768
+NQ, G = 4, 1024
+NS = 416
+NSF = (0, 0, 256, 384)
+NSL = 256
+GZ = 14
+FROM = 4
+MID = 128
 MO = (W, 0)
-CUTS = {"plain": (0, 96, 96, 224, 96), "last": (0, 64, 64, 128), "after": (64, 64, 192, 0), "free": (0, 256, 256, 256, 256)}
-BEAT = [(t, a, b) for t in range(NT) for a in range(N) for b in range(NB) if a > 1 or b or t and a]
 VCH = 128
 SHS = 256
-SV = {(0, 1): 1536}
+SV = {(0, 1): 768}
 FOLD = [(t, b) for t in range(NT) for b in range(NB) if SV.get((t, b), 0) < E]
 LATEST = {(0, 0): (0, 1), (0, 1): (0, 2), (1, 0): (1, 0), (1, 1): (1, 1), (2, 0): (2, 0), (2, 1): (2, 1)}
-SUMS = ((2, 1), (3, 0))
-STAGES = "eq0 eq1 max1 min1 min0 max0 one1 one0 two1 end1 two0 end0 kappa send head0 find0 sc0 sc1 find1 head1"
-HV = (1024, 512, 512)
-RS = (3,)
+SUMS, SP = (8, 12), 4
+LAST = "eq0 eq1 min1 min0 one1 one0 two1 end1 two0 end0 sc0 sc1 max1 max0"
+STAGES = "eq0 eq1 max1 min1 min0 max0 one1 one0 two1 end1 two0 end0 kappa send head0 find0 sc0 sc1 head1 find1 head2 find2 head3 find3"
+HV = ((512, 512, 256, 0), (256, 0, 0, 0), (256, 0, 0, 0))
+RS = (2, 3)
 PC = (128, 384)
-WB = 0
-WC = 1
 UP = 136
 AT1 = 16000
-ATU = 5500
+ATU = 6000
 ATR = 9000
-ATF = 7000
+ATF = 8000
 BIG = 68 * 65536
 CY = 0.9
 PCY = 0.45
-WAKE = 150.0
+ACT = 70
+WAKE = 130.0
+OWN = 220.0
 GA, SC = 1.56, 3.8
 DS = ((1, 2), (3, 4), (5, 6), (7,), (8,))
 LOOKS = ((900.0, 100.0), (900.0, 300.0), (500.0, 60.0), (300.0, 0.0))
 PASSES = 3
-GST = 256
-OFF = ""
-SCH = 512
+STEPS, ALLOW = 20000, 40.0
+FG = 8
+OFF = "k0k1d0d1w0w1n0n1"
 
 SCRATCH = {}
 POOL = {}
@@ -90,10 +91,9 @@ for _t in range(NT - 1):
 for _b in range(NB):
     sb("hx%d" % _b, [128, E], "float16")
     sb("cm%d" % _b, [128, E], "bfloat16")
-    al("xg%d" % _b, 1024, "bfloat16")
     al("ul%d" % _b, W, "uint16")
-    al("sq%d" % _b, W, "float32")
-    al("mi%d mj%d" % (_b, _b), W, "int32")
+    al("sq%d sh%d" % (_b, _b), W, "float32")
+    sb("qc%d" % _b, [128, 33, 8], "float16")
     al("ch%d" % _b, W + 16, "float16")
     al("lz%d dz%d lk%d wz%d lr%d de%d lbs%d" % ((_b,) * 7), W, "float16")
     al("rr%d" % _b, 2 * W, "float32")
@@ -116,16 +116,17 @@ al("wi kl rwa rwb hf ones wu bar", W, "bfloat16")
 al("w1 wh a1 a32", 8, "float16")
 al("w2 wp", 8, "bfloat16")
 al("e0", 2, "bfloat16")
+for _j in range(NQ):
+    al("xg%d" % _j, 512, "bfloat16")
+    al("mi%d mj%d" % (_j, _j), 64, "int32")
+    SCRATCH["px%d" % _j] = ("psum", [128, 16, 32], "float32")
 for _b in range(NB):
-    SCRATCH["px%d" % _b] = ("psum", [128, 16, 32], "float32")
     SCRATCH["pk%d" % _b] = ("psum", [128, 32, 16], "float32")
-for _n in range(4):
-    SCRATCH["pd%d" % _n] = ("psum", [128, 512], "float32")
+    SCRATCH["pd%d" % _b] = ("psum", [128, 512], "float32")
 
 DMASEMS = ["l_comp", "l_ci2", "l_ci3", "l_hd", "l_fa", "l_fb", "l_fc", "l_lim0", "l_lim1", "st_h", "st_l"]
 SEMAPHORES = (["qv", "qs", "qt", "qg"] + DMASEMS + ["lm_1", "lm_2", "lm_3", "bulk0", "bulk1", "ha0", "ha1", "hls"]
-              + ["%s%d%d" % (n, t, b) for t in range(NT - 1) for b in range(NB) for n in ["hu", "lo"] + ["uq%d_" % s for s in MSG]]
-              + ["%s%d" % (n, t) for t in range(NT - 1) for n in ["rl", "hr"] + ["rq%d_" % s for s in RS]]
+              + ["%s%d" % (n, t) for t in range(NT - 1) for n in ["hu", "lo", "rl", "hr"] + ["uq%d_" % s for s in MSG] + ["rq%d_" % s for s in RS]]
               + ["%s%d%d" % (n, t, b) for t, b in FOLD for n in ("fa", "fl", "fb")])
 
 
@@ -142,19 +143,15 @@ def bits(es):
     return sum(1 << e for e in es)
 
 
-def routes(T, topo, core, b):
+def routes(T, topo, core):
     r, hs = T.cores.index(core), helpers(T, topo, core)
     far = topo.engines(core, T.cores[(r + 2) % N])
-    pools = [[e for e in topo.engines(core, hs[0]) if e not in far]] + [far[i::len(MSG) - 1] for i in range(len(MSG) - 1)]
+    pools = [[e for e in topo.engines(core, hs[0]) if e not in far or len(MSG) == 1]] + [far[i::len(MSG) - 1] for i in range(len(MSG) - 1)]
     out = {}
     for s, es in zip(MSG, pools):
         to = T.cores[(r - s) % N]
-        out[s] = (to if topo.may_write(core, to) else hs[(b + s // 2) % 2], es)
+        out[s] = (to if topo.may_write(core, to) else hs[s // 2], es)
     return out
-
-
-def span(b):
-    return b * UP, (b + 1) * UP + (KW if b == NB - 1 else 0)
 
 
 def helper_program(g, core, T, topo):
@@ -184,12 +181,10 @@ def helper_program(g, core, T, topo):
                 c0, h0 = p * len(hs) * PC[0] + i * PC[p], p * PC[0]
                 hand(T.cores[(r - s) % N], T["lm%d" % s][:, c0:c0 + PC[p]], T.hl[:, h0:h0 + PC[p]], "lm_%d" % s)
         for t in range(NT - 1):
-            for b in range(NB):
-                lo, hi = span(b)
-                for s, (to, es) in routes(T, topo, rank, b).items():
-                    if to == core:
-                        g.wait_ge(S["hu%d%d" % (t, b)], len(es))
-                        hand(T.cores[(r - s) % N], T["ru%d_%d" % (s, t)][:, lo:hi], T["hu%d" % t][:, lo:hi], "uq%d_%d%d" % (s, t, b))
+            for s, (to, es) in routes(T, topo, rank).items():
+                if to == core:
+                    g.wait_ge(S["hu%d" % t], len(es))
+                    hand(T.cores[(r - s) % N], T["ru%d_%d" % (s, t)][:, :], T["hu%d" % t][:, :], "uq%d_%d" % (s, t))
             if RS:
                 g.wait_ge(S["hr%d" % t], part)
             for s in RS:
@@ -299,8 +294,11 @@ def rank_program(g, core, T, topo):
         return add("v", vc(size(out), 0.5 if short(out, a, b) else 1), lambda: V.tensor_tensor_scan(out[0], a[0], b[0], init, o1, o2), [a, b], [out])
 
     def act(out, a, func=AF.Copy, bias=0.0, scale=1.0):
-        cost = 65 + vc(size(out), GA) if len(a) == 3 else 60 + vc(size(out), 1)
+        cost = 65 + vc(size(out), GA) if len(a) == 3 else ACT + vc(size(out), 1)
         return add("s", cost, lambda: C.activation(out[0], a[0], func, bias=bias, scale=scale), split(a), [out])
+
+    def gcp(out, a):
+        return add("g", 170 + 2 * size(a) * CY, lambda: g.affine_select(out[0], a[0], [[0, size(a)]], A.is_gt, 0.0, 1, 0), [a], [out])
 
     def mm(lst, first=True, last=True, apart=False):
         rd, wr = {}, {}
@@ -328,28 +326,29 @@ def rank_program(g, core, T, topo):
         rid, pid = topo.addr(c, core)
         return DstId(rid=rid, pnc=pid)
 
-    def quarters(c0, w, land, h0, far_sem, sem, busy, extra=()):
+    def quarters(c0, w, land, h0, far_sem, sem, busy):
         tr = [RemoteDMATransfer(dst_ids=[dst(h)], dma_engine_mask=bits(near[i // 2::2][i % 2::2]), remote_sem=S[far_sem],
                                 srcs=[T.lm0[:, c0 + i * w:c0 + (i + 1) * w]], dsts=[T[land][:, h0:h0 + w]]) for i, h in enumerate(hs)]
-        return add("g", busy, lambda: g.remote_dma_fused(tr, local_sem=S[sem]), [X("lm0", c0, c0 + len(hs) * w)], [], sem=sem, cnt=len(near), lat=5000, extra=extra)
+        return add("g", busy, lambda: g.remote_dma_fused(tr, local_sem=S[sem]), [X("lm0", c0, c0 + len(hs) * w)], [], sem=sem, cnt=len(near), lat=3000)
 
     def arrivals(s):
         return sum(len(topo.engines(h, core)) for h in helpers(T, topo, T.cores[(r + s) % N]))
 
     F0, F1 = P0 + B, 2048
     cut, back = len(hs) * PC[0], [()]
-    dma("s", X("lm0", 0, cut), T.lim[:, 0:cut], "l_lim0", 2300)
-    dma("y", X("hdi"), T.hd[:, :], "l_hd", 2600)
-    dma("s", X("ci", 0, B), T.comp[:, 0:B], "l_comp", 3500)
-    dma("y", X("ft", P0, F0), T.feat[:, P0:F0], "l_fa", 4000)
-    dma("s", X("lm0", cut, H), T.lim[:, cut:H], "l_lim1", 6000)
+    first = [dma("s", X("lm0", 0, cut), T.lim[:, 0:cut], "l_lim0", 2300), dma("y", X("hdi"), T.hd[:, :], "l_hd", 2600),
+             dma("s", X("ci", 0, B), T.comp[:, 0:B], "l_comp", 3500), dma("y", X("ft", P0, F0), T.feat[:, P0:F0], "l_fa", 4000),
+             dma("s", X("lm0", cut, H), T.lim[:, cut:H], "l_lim1", 5200)]
+    for i, j in zip(first, first[2:]):
+        ops[j]["after"].add(i)
     for p in range(2):
-        back.append((quarters(cut * p, PC[p], "hl", PC[0] * p, "ha%d" % p, "bulk%d" % p, 2000),))
+        back.append((quarters(cut * p, PC[p], "hl", PC[0] * p, "ha%d" % p, "bulk%d" % p, (2000, 1200)[p]),))
+    ops[back[2][0]]["after"] |= set(back[1])
     for s in range(1, N):
-        add("x", 0, None, [], [X("lm%d" % s, 0, H)], sem="lm_%d" % s, cnt=2 * arrivals(s), lat=AT1 + 4000 * (s - 1))
-    dma("y", X("ft", 0, P0), T.feat[:, 0:P0], "l_fb", (9500, 6000, 4000)[WB], back[WB])
-    dma("y", X("ft", F0, F1), T.feat[:, F0:F1], "l_fc", 10000)
-    dma("y", X("ci", B, 2 * B), T.comp[:, B:2 * B], "l_ci2", (11000, 5000, 3000)[WC], back[WC])
+        add("x", 0, None, [], [X("lm%d" % s, 0, H)], sem="lm_%d" % s, cnt=2 * arrivals(s), lat=AT1 - 10500 + 4000 * (s - 1), extra=back[2])
+    z = dma("y", X("ft", 0, P0), T.feat[:, 0:P0], "l_fb", 5000, first[2:3])
+    ops[dma("y", X("ft", F0, F1), T.feat[:, F0:F1], "l_fc", 5500, first[2:3])]["after"].add(z)
+    dma("y", X("ci", B, 2 * B), T.comp[:, B:2 * B], "l_ci2", 5000, back[1])
     dma("y", X("ci", 2 * B, 768), T.comp[:, 2 * B:768], "l_ci3", 5000, back[2])
     add("g", 430, lambda: g.iota(X("io")[0], [[1, 144]], 0, 0), [], [X("io")])
     add("g", 200, lambda: g.iota(X("pi")[0], [[0, 1]], 0, 1), [], [X("pi")])
@@ -360,9 +359,9 @@ def rank_program(g, core, T, topo):
     ID, J8 = X("idw", 0, W), X("iof", 0, 8)
     cp(X("hdf"), X("hdi"))
     for z, (u0, u1) in enumerate(((0, 6), (6, 12), (12, 16))):
-        pd = "pd%d" % z
+        pd = "pd%d" % (z % 2)
         mm([(X(pd, 80 * (u - u0), 80 * (u - u0) + 80), X("idw", u, u + W), X("hdf")) for u in range(u0, u1)], apart=True)
-        act(X("htab", 80 * u0, 80 * u1), X(pd, 0, 80 * (u1 - u0)))
+        (cp if z == 1 else act)(X("htab", 80 * u0, 80 * u1), X(pd, 0, 80 * (u1 - u0)))
     cp(X("cl", 0, B), X("ci", 0, B))
     ts(X("gi"), X("pi"), 4, None, A.logical_shift_right)
     cp(X("gf"), X("gi"))
@@ -382,28 +381,29 @@ def rank_program(g, core, T, topo):
     ts(X("kl"), ONE, X("cw"), None, A.mult)
     for b in range(NB):
         ms(X("ch%d" % b, W, W + 16), 0.0)
+        ms(X3("qc%d" % b, 0, 33), 0.0)
 
-    def fr(t, eng):
+    def fr(t, step):
         n = "fr%d" % t
-        step = W if eng == "v" else GST
         for m0 in range(B - step, -1, -step):
             i = X("ft", P0 + B * t + m0, P0 + B * t + m0 + step)
             for k in range(16):
                 o = X(n, 16 * m0 + k, 16 * (m0 + step), 16)
-                if eng == "v":
+                if t == 0 and (m0 or k >= FG):
                     add("v", vc(step, 0.5), lambda o=o, i=i: V.tensor_copy(o[0], i[0]), [i], [o], team=n)
                 else:
-                    add("g", 170 + 2 * step * CY, lambda o=o, i=i: g.affine_select(o[0], i[0], [[0, step]], A.is_gt, 0.0, 1, 0), [i], [o], team=n)
+                    z = add("g", 170 + 2 * step * CY, lambda o=o, i=i: g.affine_select(o[0], i[0], [[0, step]], A.is_gt, 0.0, 1, 0), [i], [o], team=n)
+                    ops[z]["after"] |= set(back[2])
 
-    fr(0, "v")
-    fr(1, "g")
+    fr(0, W)
+    fr(1, B)
 
     def late():
-        cp(X("cl", B, 2 * B), X("ci", B, 2 * B))
-        cp(X("cl", 2 * B, 768), X("ci", 2 * B, 768))
+        gcp(X("cl", B, 2 * B), X("ci", B, 2 * B))
+        gcp(X("cl", 2 * B, 768), X("ci", 2 * B, 768))
         ts(X("km"), X("io", 0, W), 15, None, A.bitwise_and)
         cp(X("kf"), X("km"))
-        ts(X("keep"), X("kf"), 1.0, None, A.min)
+        act(X("keep"), X("kf"), AF.Sigmoid, bias=-128.0, scale=256.0)
         ts(X("rsa"), X("keep"), 2.0e9, -1.0e9, A.mult, A.add)
         ts(X("rsb"), X("keep"), -2.0e9, 1.0e9, A.mult, A.add)
         ts(X("on32"), ONE, 1.0 / 32, None, A.mult)
@@ -464,7 +464,7 @@ def rank_program(g, core, T, topo):
             made.append(i)
         return made
 
-    folds, sent = [], {}
+    folds, sent, found = [], {}, {}
 
     def shares(t, b):
         mn, win, c0, nv = "mn%d_%d" % (t, b), X("ft", 0, P0 + B * t), B * t + MO[b], SV.get((t, b), 0)
@@ -480,21 +480,25 @@ def rank_program(g, core, T, topo):
         folds.append(i)
         add("x", 0, None, [], [X(mn, nv, E)], sem="fb" + tb, cnt=len(topo.engines(to, core)), lat=ATF // 2, extra=(i,))
 
-    def to_list(b):
-        px = "px%d" % b
-        return [mm([(X3(px, 0, 8, 16, 32), X("ch%d" % b, 0, W), X("idq"))])], [cp(X("ul%d" % b), X3(px, 0, 8, 16, 32))]
+    def CH(j, wide=1):
+        n, a = "qc%d" % (j // 2), 16 * (j % 2) + 1
+        return (T[n][:, a:a + 16 * wide:2, :], n, 8 * a, 8 * (a + 16 * wide - 1))
 
-    def find(t, b):
-        win, hx, c0 = X("htab", 0, P0 + B * t), "hx%d" % b, B * t + MO[b]
-        hv = HV[t] if b == 0 else 0
-        gather("v", hx, win, "cl", c0, 0, hv, step=SHS)
-        gather("s", hx, win, "cl", c0, hv, E, step=SHS)
+    def to_list(j):
+        out, n, a = X3("px%d" % j, 0, 8, 8, 16), "qc%d" % (j // 2), 16 * (j % 2)
+        return ([mm([(out, X3(n, a + 1, a + 17), X("idq", 0, W, 2)), (out, X3(n, a, a + 16), X("idq", 1, W, 2))])],
+                [cp(X("ul%d" % (j // 2), 64 * (j % 2), 64 * (j % 2) + 64), out)])
 
-    def heads(t, b):
-        hx, px = "hx%d" % b, "px%d" % b
-        mm([(XI(px, 0, 8, k), col(hx, k), X("wh")) for k in range(16)], apart=True)
-        (act if "h" in OFF else cp)(X("ch%d" % b, 0, W), X3(px, 0, 8, 0, 16))
-        to_list(b)
+    def find(t, j):
+        win, hx, c0, lo = X("htab", 0, P0 + B * t), "hx%d" % (j // 2), B * t + MO[j // 2], G * (j % 2)
+        gather("v", hx, win, "cl", c0, lo, lo + HV[t][j], step=SHS)
+        found[t] = gather("s", hx, win, "cl", c0, lo + HV[t][j], lo + G, step=SHS)[-1:]
+
+    def heads(t, j):
+        px, lo = "px%d" % j, G * (j % 2)
+        mm([(XI(px, 0, 8, k), X("hx%d" % (j // 2), lo + k, lo + G, 8), X("wh")) for k in range(8)], apart=True)
+        cp(CH(j), X3(px, 0, 8, 0, 8))
+        to_list(j)
 
     def notes(t, a):
         return "lr%d_%d" % (a, t - 1) if t and a in RS else "lm%d" % a
@@ -504,62 +508,66 @@ def rank_program(g, core, T, topo):
             return X("lm0", H, HK)
         return X(notes(t, a), H, HK) if a in RS else X("ru%d_%d" % (a, t - 1), NB * UP, NB * UP + KW)
 
-    def kind(t, a, b):
-        if (a, b) == (N - 1, NB - 1):
-            return "last"
-        if b == 0 and (a == 0 or (t, a) == (0, 1)):
-            return "free"
-        return "after" if t and b == 0 and a in MSG else "plain"
-
-    def bank(b, i, n=W):
-        return X("pd%d" % (2 * b + i), 0, n)
-
-    def visit(t, b, a):
-        lm, cm, px = X(notes(t, a), 0, H), "cm%d" % b, "px%d" % b
-        x, ch = X3(px, 0, 8, 0, 16), X("ch%d" % b, 0, W)
-        todo, nv = [], E - (NS0 if (a, b) == (0, 0) else NS3 if (a, b) == (N - 1, 1) else NSA if kind(t, a, b) == "after" else NS1 if t else NS)
-        v = {"f": [], "g": [], "x": []}
-        for i, (lo, hi) in enumerate(parts(nv, E, SCH)):
-            xg, d = X("xg%d" % b, lo - nv, hi - nv), bank(b, i, hi - lo)
-            v["f"].append(mm([(d, ID, FR(t, b, lo, hi))], last=False))
-            v["g"].append(act(xg, IND(lm, offs("ul%d" % b, 0, lo, hi))))
-            v["x"].append(mm([(d, X("nid"), xg)], first=False))
-            todo.append((X(cm, lo, hi), d))
-        v["sq"] = [act(X("sq%d" % b), ch, AF.Square, bias=16.0, scale=1.0 / 32)]
-        v["open"] = [mm([(x, X("idf"), X("sq%d" % b))] + [(X3(px, 4 * h, 4 * h + 4, 0, 16), X("kl"), tile(t, a)) for h in range(2)], last=False)]
-        v["s"] = [act(o, d, AF.Sigmoid, bias=-128.0, scale=256.0) for o, d in todo]
-        v["v"] = gather("v", cm, lm, "ul%d" % b, 0, 0, nv, lambda lo, hi: FR(t, b, lo, hi), A.is_lt, CUTS[kind(t, a, b)])
-        v["sum"] = [mm([(XI(px, 0, 8, k), col(cm, k), X(w)) for k in range(16) for w in ("w1", "w2")], first=False)]
-        v["new"] = [tt(X("mi%d" % b), x, ch, A.max), ts(X("mj%d" % b), X("mi%d" % b), 32 * (H - 1), None, A.bitwise_and), cp(ch, X("mj%d" % b))]
-        v["turn"], v["list"] = to_list(b) if a < N - 1 else ([], [])
+    def visit(t, j, a):
+        b, lo = j // 2, G * (j % 2)
+        lm, cm, px, ul = X(notes(t, a), 0, H), "cm%d" % b, "px%d" % j, "ul%d" % b
+        x, ch, mi, mj = X3(px, 0, 8, 0, 8), CH(j), X("mi%d" % j), X("mj%d" % j)
+        ns = NSF[j] if a == 0 else NSL if (a, j) == (N - 1, NQ - 1) else 0 if (a, j) == (1, 0) else NS
+        hi, v = lo + G - ns, {}
+        if ns:
+            xg, d = X("xg%d" % j, 0, ns), X("pd%d" % (j % 2), 0, ns)
+            v["f"] = [mm([(d, ID, FR(t, b, hi, lo + G))], last=False)]
+            v["g"] = [act(xg, IND(lm, offs(ul, 0, hi, lo + G)))]
+            v["x"] = [mm([(d, X("nid"), xg)], first=False)]
+            v["s"] = [act(X(cm, hi, lo + G), d, AF.Sigmoid, bias=-128.0, scale=256.0)]
+        if j % 2 == 0:
+            v["sq"] = [act(X("sh%d" % b), CH(j, 2), AF.Square, bias=16.0, scale=1.0 / 32)]
+        v["open"] = [mm([(x, X("idf"), X("sh%d" % b, 64 * (j % 2), 64 * (j % 2) + 64)), (x, X("kl"), tile(t, a))], last=False)]
+        v["v"] = gather("v", cm, lm, ul, 0, lo, hi, lambda lo, hi: FR(t, b, lo, hi), A.is_lt, (MID, 0))
+        v["sum"] = [mm([(XI(px, 0, 8, k), X(cm, lo + k, lo + G, 8), X(w)) for k in range(8) for w in ("w1", "w2")], first=False)]
+        v["max"], v["and"] = [tt(mi, x, ch, A.max)], [ts(mj, mi, 32 * (H - 1), None, A.bitwise_and)]
+        if NQ * a + j < GZ:
+            gcp(ch, mj)
+        else:
+            v["cp"] = [cp(ch, mj)]
+        if a < N - 1:
+            v["turn"], v["list"] = to_list(j)
         return v
 
     def chain(calls):
         for i, j in zip(calls, calls[1:]):
             ops[j]["after"].add(i)
 
-    def beat(last, v, nxt, fill):
-        p, brief = v["v"], last["new"] + last["list"]
-        first = v.get("scat", p[:1])
-        rest = p if "scat" in v else p[1:]
-        chain(first + [i for pair in zip(brief, rest) for i in pair] + rest[len(brief):] + nxt.get("scat", nxt.get("v", []))[:1])
-        chain(v["g"] + v["s"] + nxt.get("sq", []) + nxt.get("g", [])[:1])
-        f = nxt.get("f", [])
-        if "scat" in v:
-            chain(last["sum"] + v["open"] + last["turn"] + v["x"][:1] + f[:1] + v["x"][1:] + f[1:] + fill + v["sum"])
-        else:
-            chain(last["sum"] + v["x"] + v["open"] + f[:1] + last["turn"] + f[1:] + fill + v["sum"])
+    def beat(t, seq, fill):
+        def of(n, what):
+            return seq[n].get(what, []) if n < len(seq) else []
+        vq, sq, tq = [], [], []
+        chain(found[t] + [i for n in range(FROM + 1) for i in of(n, "g")])
+        for n in range(FROM, len(seq)):
+            p = of(n, "v")
+            if of(n, "scat"):
+                vq += of(n, "scat")[:-1] + of(n - 2, "and") + of(n - 3, "list") + of(n, "scat")[-1:] + of(n - 1, "max") + p
+            else:
+                vq += p[:1] + of(n - 2, "and") + of(n - 3, "list") + p[1:] + of(n - 1, "max") + of(n - 2, "cp")
+            sq += of(n + 1, "g") + of(n, "s") + of(n + 1, "sq")
+            tq += of(n, "x") + of(n - 1, "open") + of(n - 1, "sum") + of(n - 2, "turn") + of(n + 1, "f") + fill.get(n, [])
+        for q in (vq, sq, tq):
+            chain(q)
 
     def sums(t, b):
         pk = "pk%d" % b
-        return mm([(X3(pk, 0, 8), X("wi"), ONE)] + [(XI(pk, 0, 8, k), col("mn%d_%d" % (t, b), k), X("wp")) for k in range(16)], last=False)
+        run = [(X3(pk, 0, 8), X("wi"), ONE)] + [(XI(pk, 0, 8, k), col("mn%d_%d" % (t, b), k), X("wp")) for k in range(16)]
+        ends = [0] + [17 - 16 // SP * i for i in range(SP - 1, -1, -1)]
+        return {SUMS[b] + i: [mm(run[ends[i]:ends[i + 1]], first=i == 0, last=False)] for i in range(SP)}
 
     def elect(t, b):
-        px, pk, eb, ch = "px%d" % b, "pk%d" % b, "eb%d" % b, X("ch%d" % b, 0, W)
-        key, de = X3(pk, 0, 8), bank(b, 0)
-        mm([(X3(px, 8, 16, 0, 16), ID, ch), (X3(px, 8, 16, 16, 32), ID, ch)], apart=True)
+        px, pk, eb, ch = "px%d" % (2 * b), "pk%d" % b, "eb%d" % b, X("ch%d" % b, 0, W)
+        key, de = X3(pk, 0, 8), X3("px%d" % (2 * b + 1), 8, 12)
+        for h in range(2):
+            mm([((T[px][64 * h:64 * h + 64, 8:16, c:c + 8], px, 256, 512), X("idw", c // 8 % 2, W, 2), CH(2 * b + h)) for c in range(0, 32, 8)], apart=True)
+        cp(ch, X3(px, 8, 16, 0, 16))
         mm([(de, ID, X("ch%d" % b, 1, W + 1)), (de, X("nid"), ch)])
-        act(X("de%d" % b), de)
+        (act if "d%d" % b in OFF else cp)(X("de%d" % b), de)
         for d in range(1, 9):
             e = X3(eb, 8 * d - 8, 8 * d)
             tt(e, ch, X3(px, 8, 16, d, d + 16), A.is_equal)
@@ -571,7 +579,7 @@ def rank_program(g, core, T, topo):
                     run.append((X3(pk, 0, 8, d, 16), X("wi"), X3(eb, 8 * d - 8, 8 * d, 0, 16 - d)))
                     run.append((X3(pk, 0, 8, 0, d), X("wi"), X3(eb, 8 * d - 8, 8 * d, 16 - d, 16)))
             mm(run, first=False, last=8 in ds)
-        act(X("sq%d" % b), key)
+        (act if "k%d" % b in OFF else cp)(X("sq%d" % b), key)
 
     def pick(t, b, h):
         rs, o1, o2 = (("rsa", A.min, A.max), ("rsb", A.max, A.min))[h]
@@ -579,16 +587,18 @@ def rank_program(g, core, T, topo):
         scan(X("rr%d" % b, lo, hi, -1), X(rs), X("sq%d" % b, 0, W, -1), 0.0, o1, o2)
         tt(X("nr%d" % b, lo, hi), X("rr%d" % b, lo, hi), X3("pk%d" % b, 0, 8), A.not_equal)
         scan(X("yy%d" % b, lo, hi, -1), X("de%d" % b, 0, W, -1), X("nr%d" % b, lo, hi, -1), 0.0, A.add, A.mult)
-        tt(X(("wz%d", "lz%d")[h] % b, 0, W, 16), X("yy%d" % b, lo, hi, 16), X("ch%d" % b, 0, W, 16), A.add)
         if h == 0:
-            c0, won = P0 + B * t + MO[b], bank(b, 1)
-            mm([(won, X("wz%d" % b), X("idq"))])
-            act(X("htab", c0, c0 + W), won)
+            c0, won = P0 + B * t + MO[b], X3("px%d" % (2 * b + 1), 12, 16)
+            mm([(won, X("ch%d" % b, 0, W), X("idq"))], last=False)
+            mm([(won, X("yy%d" % b, lo, hi), X("idq"))], first=False)
+            (act if "w%d" % b in OFF else cp)(X("htab", c0, c0 + W), won)
+        if h or t < NT - 1:
+            tt(X(("wz%d", "lz%d")[h] % b, 0, W, 16), X("yy%d" % b, lo, hi, 16), X("ch%d" % b, 0, W, 16), A.add)
 
     def losers(t, b, stage):
-        px, pk, up, lf, c0 = "px%d" % b, "pk%d" % b, "up%d" % t, "lf%d" % b, P0 + B * t + MO[b]
-        row, lst, dup, old = X("lbs%d" % b), XR(px, 8, 0, 8), X3(px, 12, 16), X("old%d" % b)
-        dif, new = bank(b, 0), bank(b, 1)
+        pk, up, lf, c0 = "pk%d" % b, "up%d" % t, "lf%d" % b, P0 + B * t + MO[b]
+        row, lst, dup, old = X("lbs%d" % b), XR("px%d" % (2 * b), 0, 16, 24), X("pd%d" % b, 0, W), X("old%d" % b)
+        dif, new = X3("px%d" % (2 * b + 1), 0, 4), X3("px%d" % (2 * b + 1), 4, 8)
         if stage == "one":
             scan(X("lr%d" % b), X("keep"), X("lz%d" % b), 0.0, A.mult, A.add)
             mm([(X3(pk, 16, 24), X("lr%d" % b), X("idq"))])
@@ -613,7 +623,7 @@ def rank_program(g, core, T, topo):
         else:
             ts(X("clp%d" % b), dif, -32.0, 32.0, A.max, A.min)
             mm([(new, ID, old), (new, ID, X("clp%d" % b))])
-            act(X(up, b * UP, b * UP + W), new)
+            (act if "n%d" % b in OFF else cp)(X(up, b * UP, b * UP + W), new)
             tt(X(up, b * UP + W, b * UP + W + 8), lst, X(lf), A.max)
 
     def kappa(t):
@@ -622,58 +632,53 @@ def rank_program(g, core, T, topo):
         cp(top("ki"), o)
         ts(top("kj"), top("ki"), 255, None, A.bitwise_and)
         cp(top("up%d" % t, NB * UP, NB * UP + KW), top("kj"))
-        cp(top("lm0", H, HK), top("kj"))
+        gcp(top("lm0", H, HK), top("kj"))
 
     def scat(s, up, b):
         ou = X("ou%d" % s, 16 * b, 16 * b + 8)
-        cp(ou, X(up, b * UP + W, b * UP + W + 8))
+        (gcp if s else cp)(ou, X(up, b * UP + W, b * UP + W + 8))
         return cp(IND(X("lm%d" % s), ou), X(up, b * UP, b * UP + W))
 
-    def send(t, b):
-        lo, hi = span(b)
-        up, tb = T["up%d" % t][:, lo:hi], "%d%d" % (t, b)
+    def send(t):
         tr, cnt = [], 0
-        for s, (to, es) in routes(T, topo, core, b).items():
-            sem, n = ("hu" + tb, "hu%d" % t) if to in hs else ("uq%d_%s" % (s, tb), "ru%d_%d" % (s, t))
-            tr.append(RemoteDMATransfer(dst_ids=[dst(to)], dma_engine_mask=bits(es), remote_sem=S[sem], srcs=[up], dsts=[T[n][:, lo:hi]]))
+        for s, (to, es) in routes(T, topo, core).items():
+            sem, n = ("hu%d" % t, "hu%d" % t) if to in hs else ("uq%d_%d" % (s, t), "ru%d_%d" % (s, t))
+            tr.append(RemoteDMATransfer(dst_ids=[dst(to)], dma_engine_mask=bits(es), remote_sem=S[sem], srcs=[X("up%d" % t)[0]], dsts=[X(n)[0]]))
             cnt += len(es)
-        i = add("g", 1200, lambda: g.remote_dma_fused(tr, local_sem=S["lo" + tb]), [X("up%d" % t, lo, hi)], [], sem="lo" + tb, cnt=cnt, lat=2500)
+        i = add("g", 1200, lambda: g.remote_dma_fused(tr, local_sem=S["lo%d" % t]), [X("up%d" % t)], [], sem="lo%d" % t, cnt=cnt, lat=2500)
         sent[t] = (i,)
         for s in MSG:
-            to, es = routes(T, topo, T.cores[(r + s) % N], b)[s]
-            add("x", 0, None, [], [X("ru%d_%d" % (s, t), lo, hi)], sem="uq%d_%s" % (s, tb), cnt=len(es if to == core else topo.engines(to, core)), lat=ATU - 2500 + 1500 * (s // 3),
-                extra=(i,))
+            to, es = routes(T, topo, T.cores[(r + s) % N])[s]
+            add("x", 0, None, [], [X("ru%d_%d" % (s, t))], sem="uq%d_%d" % (s, t), cnt=len(es if to == core else topo.engines(to, core)),
+                lat=(ATU * 0.55 if to == core else ATU) - 2500, extra=(i,))
 
     def anew(t):
-        i = quarters(0, HK // len(hs), "hl%d" % t, 0, "hr%d" % t, "rl%d" % t, 1200, sent[t])
+        i = quarters(0, HK // len(hs), "hl%d" % t, 0, "hr%d" % t, "rl%d" % t, 1200)
+        ops[i]["after"] |= set(sent[t])
         for n, s in enumerate(RS):
-            add("x", 0, None, [], [X("lr%d_%d" % (s, t))], sem="rq%d_%d" % (s, t), cnt=arrivals(s), lat=ATR - 5000 + 4000 * n, extra=(i,))
-
-    seen, added = {}, {}
+            add("x", 0, None, [], [X("lr%d_%d" % (s, t))], sem="rq%d_%d" % (s, t), cnt=arrivals(s), lat=ATR - 3000 + 4000 * n, extra=(i,))
 
     def stage(name, base, call, *args):
-        lift[0] = base + STAGES.split().index(name) / 100
+        lift[0] = base + (STAGES if more else LAST).split().index(name) / 100
         call(*args)
         lift[0] = None
 
-    for b in range(NB):
-        find(0, b)
-        heads(0, b)
+    for j in range(NQ):
+        find(0, j)
+        heads(0, j)
     late()
     for t in range(NT):
+        seq = []
         for a in range(N):
             for t1, b in LATEST:
                 if LATEST[t1, b] == (t, a):
                     shares(t1, b)
             if (t, a) == (0, N - 1):
-                fr(2, "g")
-            new = [scat(a, "ru%d_%d" % (a, t - 1), b) for b in range(NB)] if t and a in MSG else []
-            for b in range(NB):
-                seen[t, a, b] = visit(t, b, a)
-            if new:
-                seen[t, a, 0]["scat"] = new
-        for b in range(NB):
-            added[(t,) + SUMS[b]] = [sums(t, b)]
+                fr(2, B)
+            new = [scat(s, "ru%d_%d" % (s, t - 1), b) for s in MSG[::-1] for b in range(NB)] if t and a == 1 else []
+            seq += [visit(t, j, a) for j in range(NQ)]
+            seq[-NQ]["scat"] = new
+        beat(t, seq, {**sums(t, 0), **sums(t, 1)})
         base, more = len(ops), t < NT - 1
         for b in range(NB):
             stage("eq%d" % b, base, elect, t, b)
@@ -685,18 +690,16 @@ def rank_program(g, core, T, topo):
         for b in range(NB):
             stage("two%d" % b, base, losers, t, b, "two")
             stage("end%d" % b, base, losers, t, b, "end")
-            if more:
-                stage("send", base, send, t, b)
+        if more:
+            stage("send", base, send, t)
         for b in range(NB):
             stage("sc%d" % b, base, scat, 0, "up%d" % t, b)
         if more:
-            for b in range(NB):
-                stage("find%d" % b, base, find, t + 1, b)
-                stage("head%d" % b, base, heads, t + 1, b)
+            for j in range(NQ):
+                stage("find%d" % j, base, find, t + 1, j)
+                stage("head%d" % j, base, heads, t + 1, j)
             if RS:
                 anew(t)
-    for t, a, b in BEAT:
-        beat(seen[t, a - 1 + b, 1 - b], seen[t, a, b], seen.get((t, a + b, 1 - b), {}), added.get((t, a, b), []))
     add("y", 60, lambda: Y.dma_start(T.yh[:, :], T.htab[0:128:16, P0:2048]), [X("htab", P0, 2048)], [], sem="st_h", cnt=16, lat=2000)
     dma("y", T.yl[:, :], X("lm0", 0, H), "st_l", 3500)
     emit(g, T, ops)
@@ -714,7 +717,7 @@ def replay(ops, queues, wake):
         o = ops[i]
         e, d = 0.0, o["busy"]
         for j in o["deps"]:
-            e = max(e, fin[j] + ops[j]["lat"] + wake)
+            e = max(e, fin[j] + ops[j]["lat"] + (OWN if ops[j]["q"] == q else wake))
         if q != "x" and q in last:
             p = last[q]
             if joins(ops[p], o):
@@ -729,7 +732,7 @@ def schedule(ops):
     n = len(ops)
     succ, pred = [[] for _ in range(n)], [[] for _ in range(n)]
     for i, o in enumerate(ops):
-        for j, w in [(j, ops[j]["lat"] + WAKE) for j in o["deps"]] + [(j, 0.0) for j in o["after"]]:
+        for j, w in [(j, ops[j]["lat"] + (OWN if ops[j]["q"] == o["q"] else WAKE)) for j in o["deps"]] + [(j, 0.0) for j in o["after"]]:
             succ[j].append((i, w))
             pred[i].append((j, w))
 
@@ -793,7 +796,72 @@ def schedule(ops):
             end = max(run[i] + ops[i]["lat"] for i in range(n))
             if best is None or end < best[0]:
                 best = (end, order, run)
-    return best[1], best[2]
+    order = [(i, ops[i]["q"]) for i in polish(ops, [i for i, q in best[1]], pred, succ)]
+    return order, replay(ops, order, WAKE)
+
+
+def polish(ops, order, pred, succ):
+    n = len(ops)
+    qs, busy, lat = [o["q"] for o in ops], [o["busy"] for o in ops], [o["lat"] for o in ops]
+    glue = {i - 1: o["piece"][3] for i, o in enumerate(ops) if i and joins(ops[i - 1], o)}
+
+    def run(order, start, fin, why):
+        last = {}
+        for i in reversed(order[:start]):
+            last.setdefault(qs[i], i)
+            if len(last) == 6:
+                break
+        for i in order[start:]:
+            e, w0, d, q = 0.0, None, busy[i], qs[i]
+            for j, w in pred[i]:
+                if fin[j] + w > e:
+                    e, w0 = fin[j] + w, j
+            p = last.get(q)
+            if p is not None and q != "x":
+                if p == i - 1:
+                    d -= glue.get(p, 0)
+                if fin[p] >= e:
+                    e, w0 = fin[p], -p - 1
+            last[q] = i
+            fin[i], why[i] = e + d, w0
+        return max(fin[i] + lat[i] for i in order[-40:])
+    fin, why, seed = [0.0] * n, [None] * n, 1
+    now = run(order, 0, fin, why)
+    best, pairs = (now, order), None
+    for step in range(STEPS):
+        if pairs is None:
+            order = sorted(order, key=lambda i: fin[i])
+            at = {i: k for k, i in enumerate(order)}
+            pairs, i = [], max(order[-40:], key=lambda i: fin[i] + lat[i])
+            while why[i] is not None:
+                if why[i] < 0:
+                    pairs.append((-why[i] - 1, i))
+                i = why[i] if why[i] >= 0 else -why[i] - 1
+        seed = (seed * 1103515245 + 12345) % 2147483648
+        p, i = pairs[(seed >> 8) % len(pairs)]
+        far, k = (1, 1, 1, 2, 2, 3, 4, 6)[seed >> 4 & 7], at[i]
+        if seed >> 7 & 1:
+            while far and k:
+                k -= 1
+                far -= qs[order[k]] == qs[i]
+            if any(at[j] >= k for j, w in pred[i]):
+                continue
+            new, start = order[:k] + [i] + order[k:at[i]] + order[at[i] + 1:], k
+        else:
+            far -= 1
+            while far and k < n - 1:
+                k += 1
+                far -= qs[order[k]] == qs[i]
+            if any(at[j] <= k for j, w in succ[p]):
+                continue
+            new, start = order[:at[p]] + order[at[p] + 1:k + 1] + [p] + order[k + 1:], at[p]
+        f, y = list(fin), list(why)
+        end = run(new, start, f, y)
+        if end <= now + ALLOW * (1 - step / STEPS) * (seed >> 12 & 255) / 255:
+            order, fin, why, now, pairs = new, f, y, end, None
+            if end < best[0]:
+                best = (end, new)
+    return best[1]
 
 
 def emit(g, T, ops):

from concourse.bass import DstId, RemoteDMATransfer
from concourse.mybir import AluOpType as A, ActivationFunctionType as AF, AxisListType

N, H, P0, B, NT = 4, 2048, 1280, 256, 3
NB, W, E = 2, 128, 2048
KW = 64
HK = H + KW
NQ, G = 4, 1024
NS = 416
NSF = (0, 0, 256, 384)
NSL = 256
GZ = 14
FROM = 4
MID = 128
MO = (W, 0)
VCH = 128
SHS = 256
SV = {(0, 1): 768}
FOLD = [(t, b) for t in range(NT) for b in range(NB) if SV.get((t, b), 0) < E]
LATEST = {(0, 0): (0, 1), (0, 1): (0, 2), (1, 0): (1, 0), (1, 1): (1, 1), (2, 0): (2, 0), (2, 1): (2, 1)}
SUMS, SP = (8, 12), 4
LAST = "eq0 eq1 min1 min0 one1 one0 two1 end1 two0 end0 sc0 sc1 max1 max0"
STAGES = "eq0 eq1 max1 min1 min0 max0 one1 one0 two1 end1 two0 end0 kappa send head0 find0 sc0 sc1 head1 find1 head2 find2 head3 find3"
HV = ((512, 512, 256, 0), (256, 0, 0, 0), (256, 0, 0, 0))
RS = (2, 3)
PC = (128, 384)
UP = 136
AT1 = 16000
ATU = 6000
ATR = 9000
ATF = 8000
BIG = 68 * 65536
CY = 0.9
PCY = 0.45
ACT = 70
WAKE = 130.0
OWN = 220.0
GA, SC = 1.56, 3.8
DS = ((1, 2), (3, 4), (5, 6), (7,), (8,))
LOOKS = ((900.0, 100.0), (900.0, 300.0), (500.0, 60.0), (300.0, 0.0))
PASSES = 3
STEPS, ALLOW = 20000, 40.0
FG = 8
OFF = "k0k1d0d1w0w1n0n1"

SCRATCH = {}
POOL = {}
_FILL = {}
_BYTES = {"float32": 4, "int32": 4, "bfloat16": 2, "float16": 2, "uint16": 2}
_PLAN = {}


def sb(names, shape, dtype):
    for n in names.split():
        SCRATCH[n] = ("sbuf", shape, dtype)


def al(names, width, dtype):
    unit = 32 // _BYTES[dtype]
    for n in names.split():
        p = "p_" + dtype
        POOL[n] = (p, _FILL.get(p, 0), width)
        _FILL[p] = _FILL.get(p, 0) + -(-width // unit) * unit
        SCRATCH[p] = ("sbuf", [128, _FILL[p]], dtype)


MSG = [s for s in range(1, N) if s not in RS]
for _s in range(N):
    sb("lm%d" % _s, [128, HK + B], "bfloat16")
    al("ou%d" % _s, 32, "uint16")
sb("ft", [128, 2048], "bfloat16")
sb("ci", [128, 768], "int32")
sb("hdi", [128, 80], "int32")
sb("htab", [128, 2048], "float32")
sb("hl", [128, H // 4], "bfloat16")
al("hdf", 80, "float16")
al("cl", 768, "uint16")
for _t in range(NT):
    sb("fr%d" % _t, [128, NB * E], "bfloat16")
    sb("up%d" % _t, [128, NB * UP + KW], "float16")
    sb("mn%d_0 mn%d_1" % (_t, _t), [128, E], "bfloat16")
for _t, _b in FOLD:
    sb("mx%d_%d" % (_t, _b), [128, E], "bfloat16")
for _t in range(NT - 1):
    sb("hu%d" % _t, [128, NB * UP + KW], "float16")
    sb("hl%d" % _t, [128, HK // 4], "bfloat16")
    for _s in MSG:
        sb("ru%d_%d" % (_s, _t), [128, NB * UP + KW], "float16")
    for _s in RS:
        sb("lr%d_%d" % (_s, _t), [128, HK], "bfloat16")
for _b in range(NB):
    sb("hx%d" % _b, [128, E], "float16")
    sb("cm%d" % _b, [128, E], "bfloat16")
    al("ul%d" % _b, W, "uint16")
    al("sq%d sh%d" % (_b, _b), W, "float32")
    sb("qc%d" % _b, [128, 33, 8], "float16")
    al("ch%d" % _b, W + 16, "float16")
    al("lz%d dz%d lk%d wz%d lr%d de%d lbs%d" % ((_b,) * 7), W, "float16")
    al("rr%d" % _b, 2 * W, "float32")
    al("nr%d yy%d" % (_b, _b), 2 * W, "float16")
    al("lf%d" % _b, 8, "float32")
    al("lu%d" % _b, 8, "uint16")
    al("old%d clp%d" % (_b, _b), W, "bfloat16")
    sb("eb%d" % _b, [128, 64, 16], "bfloat16")
    sb("ind%d" % _b, [128, 8 * W], "bfloat16")
al("pf gf rf c1 c2 c3 cq cw thr dmy", 1, "float32")
al("pi gi ri", 1, "int32")
al("ki kj", KW, "int32")
al("io", 144, "int32")
al("km gm", W, "int32")
al("iof", 144, "float32")
al("kf gk idf rsa rsb st", W, "float32")
al("idw", 144, "float16")
al("nid idq on32 keep own", W, "float16")
al("wi kl rwa rwb hf ones wu bar", W, "bfloat16")
al("w1 wh a1 a32", 8, "float16")
al("w2 wp", 8, "bfloat16")
al("e0", 2, "bfloat16")
for _j in range(NQ):
    al("xg%d" % _j, 512, "bfloat16")
    al("mi%d mj%d" % (_j, _j), 64, "int32")
    SCRATCH["px%d" % _j] = ("psum", [128, 16, 32], "float32")
for _b in range(NB):
    SCRATCH["pk%d" % _b] = ("psum", [128, 32, 16], "float32")
    SCRATCH["pd%d" % _b] = ("psum", [128, 512], "float32")

DMASEMS = ["l_comp", "l_ci2", "l_ci3", "l_hd", "l_fa", "l_fb", "l_fc", "l_lim0", "l_lim1", "st_h", "st_l"]
SEMAPHORES = (["qv", "qs", "qt", "qg"] + DMASEMS + ["lm_1", "lm_2", "lm_3", "bulk0", "bulk1", "ha0", "ha1", "hls"]
              + ["%s%d" % (n, t) for t in range(NT - 1) for n in ["hu", "lo", "rl", "hr"] + ["uq%d_" % s for s in MSG] + ["rq%d_" % s for s in RS]]
              + ["%s%d%d" % (n, t, b) for t, b in FOLD for n in ("fa", "fl", "fb")])


def helpers(T, topo, core):
    cand = [c for c in topo.cores_of(core) if c not in T.cores and all(topo.may_write(c, d) for d in T.cores)]
    return [c for c in cand if topo.die(c) == topo.die(core)] + [c for c in cand if topo.die(c) != topo.die(core)]


def mirror(T, topo, core):
    return [c for c in topo.cores_of(core) if c not in T.cores and c not in helpers(T, topo, core) and topo.die(c) == topo.die(core)][0]


def bits(es):
    return sum(1 << e for e in es)


def routes(T, topo, core):
    r, hs = T.cores.index(core), helpers(T, topo, core)
    far = topo.engines(core, T.cores[(r + 2) % N])
    pools = [[e for e in topo.engines(core, hs[0]) if e not in far or len(MSG) == 1]] + [far[i::len(MSG) - 1] for i in range(len(MSG) - 1)]
    out = {}
    for s, es in zip(MSG, pools):
        to = T.cores[(r - s) % N]
        out[s] = (to if topo.may_write(core, to) else hs[s // 2], es)
    return out


def helper_program(g, core, T, topo):
    S = T.sem
    for r, rank in enumerate(T.cores):
        hs = helpers(T, topo, rank)
        ls = [0]

        def hand(dst, out, src, sem):
            rid, pid = topo.addr(dst, core)
            g.remote_dma(out, src, S[sem], S.hls, pid, rid, topo.mask(core, dst))
            ls[0] += len(topo.engines(core, dst))
        if core == mirror(T, topo, rank):
            for t, b in FOLD:
                g.wait_ge(S["fa%d%d" % (t, b)], len(topo.engines(rank, core)))
                mn = T["mn%d_%d" % (t, b)][:, SV.get((t, b), 0):E]
                hand(rank, mn, mn, "fb%d%d" % (t, b))
            g.wait_ge(S.hls, ls[0])
        if core not in hs:
            continue
        i = hs.index(core)
        part = len(topo.engines(rank, core)) // len(hs)
        for s in range(1, N):
            for p in range(2):
                if s == 1:
                    g.wait_ge(S["ha%d" % p], part)
                c0, h0 = p * len(hs) * PC[0] + i * PC[p], p * PC[0]
                hand(T.cores[(r - s) % N], T["lm%d" % s][:, c0:c0 + PC[p]], T.hl[:, h0:h0 + PC[p]], "lm_%d" % s)
        for t in range(NT - 1):
            for s, (to, es) in routes(T, topo, rank).items():
                if to == core:
                    g.wait_ge(S["hu%d" % t], len(es))
                    hand(T.cores[(r - s) % N], T["ru%d_%d" % (s, t)][:, :], T["hu%d" % t][:, :], "uq%d_%d" % (s, t))
            if RS:
                g.wait_ge(S["hr%d" % t], part)
            for s in RS:
                w = HK // len(hs)
                hand(T.cores[(r - s) % N], T["lr%d_%d" % (s, t)][:, i * w:(i + 1) * w], T["hl%d" % t][:, :], "rq%d_%d" % (s, t))
        g.wait_ge(S.hls, ls[0])


def rank_program(g, core, T, topo):
    if T.rank_of(core) is None:
        helper_program(g, core, T, topo)
        return
    r = T.rank_of(core)
    S = T.sem
    V, C, M, Y = g.vector, g.scalar, g.tensor, g.sync
    ops, hist, lift = [], {}, [None]
    psum = {n for n in SCRATCH if SCRATCH[n][0] == "psum"}

    def X(n, lo=0, hi=None, st=1):
        if n in POOL:
            p, o, w = POOL[n]
            t = T[p]
        else:
            t = T[n]
            o, w = 0, t.shape[1]
        if hi is None:
            hi = w
        if st == -1:
            return (t[:, o + hi - 1:(o + lo - 1 if o + lo else None):-1], n, lo, hi)
        return (t[:, o + lo:o + hi:st] if st != 1 else t[:, o + lo:o + hi], n, lo, hi)

    def X3(n, a, b, lo=0, hi=None):
        w = T[n].shape[2]
        return (T[n][:, a:b, lo:w if hi is None else hi], n, a * w, b * w)

    def XI(n, a, b, i):
        w = T[n].shape[2]
        return (T[n][:, a:b, i], n, a * w, b * w)

    def XR(n, a, lo, hi):
        w = T[n].shape[2]
        return (T[n][:, a, lo:hi], n, a * w + lo, a * w + hi)

    def top(n, lo=0, hi=KW):
        p, o, w = POOL.get(n, (n, 0, 0))
        return (T[p][0:1, o + lo:o + hi], n, lo, hi)

    def IND(win, off):
        return (win[0].indirect(off[0]), win, off)

    def split(a):
        return [a[1], a[2]] if len(a) == 3 else [a]

    def size(a):
        k = 1
        for d in a[0].shape[1:]:
            k *= d
        return k

    def short(*aps):
        return all(_BYTES[SCRATCH[POOL[a[1]][0] if a[1] in POOL else a[1]][2]] == 2 for a in aps)

    def add(q, busy, fire, reads, writes, sem=None, cnt=0, lat=0.0, extra=(), team=None):
        i = len(ops)
        deps, after = set(extra), set()
        acc = [(x, 0) for x in reads] + [(x, 1) for x in writes]
        for (ap, n, lo, hi), w in acc:
            past = hist.get(n, ([], []))
            for (j, jw, jlo, jhi, jq) in (past[0] + past[1] if w or n in psum else past[1]):
                if n in psum and jq == q == "t":
                    after.add(j)
                elif team and ops[j]["team"] == team:
                    continue
                elif n in psum and jq != q or jhi > lo and jlo < hi and (w or jw):
                    deps.add(j)
        for (ap, n, lo, hi), w in acc:
            hist.setdefault(n, ([], []))[w].append((i, w, lo, hi, q))
        ops.append({"q": q, "busy": busy, "fire": fire, "deps": deps - {i}, "after": after - deps - {i}, "sem": sem, "cnt": cnt, "lat": lat, "team": team,
                    "rank": i if lift[0] is None else lift[0] + i * 1e-6})
        return i

    def vc(n, f):
        return max(64.0, n * f) * CY

    def tt(out, a, b, op):
        return add("v", vc(size(out), 1 if (a[1] in psum or b[1] in psum) else 2), lambda: V.tensor_tensor(out[0], a[0], b[0], op), [a, b], [out])

    def ts(out, a, s1, s2, o1, o2=None):
        rd = [a] + [s for s in (s1, s2) if isinstance(s, tuple)]
        v1 = s1[0] if isinstance(s1, tuple) else s1
        v2 = s2[0] if isinstance(s2, tuple) else s2
        if o2 is None:
            fn = lambda: V.tensor_scalar(out[0], a[0], v1, None, o1)
        else:
            fn = lambda: V.tensor_scalar(out[0], a[0], v1, v2, o1, o2)
        return add("v", vc(size(out), 0.5 if short(out, a) else 1), fn, rd, [out])

    def cp(out, a):
        if len(out) == 3:
            return add("v", 50 + vc(size(a), SC), lambda: V.tensor_copy(out[0], a[0]), [a, out[2]], [out[1]])
        return add("v", vc(size(out), 0.5 if short(out, a) else 1), lambda: V.tensor_copy(out[0], a[0]), [a], [out])

    def ms(out, c):
        return add("v", vc(size(out), 0.5 if short(out) else 1), lambda: V.memset(out[0], c), [], [out])

    def scan(out, a, b, init, o1, o2):
        return add("v", vc(size(out), 0.5 if short(out, a, b) else 1), lambda: V.tensor_tensor_scan(out[0], a[0], b[0], init, o1, o2), [a, b], [out])

    def act(out, a, func=AF.Copy, bias=0.0, scale=1.0):
        cost = 65 + vc(size(out), GA) if len(a) == 3 else ACT + vc(size(out), 1)
        return add("s", cost, lambda: C.activation(out[0], a[0], func, bias=bias, scale=scale), split(a), [out])

    def gcp(out, a):
        return add("g", 170 + 2 * size(a) * CY, lambda: g.affine_select(out[0], a[0], [[0, size(a)]], A.is_gt, 0.0, 1, 0), [a], [out])

    def mm(lst, first=True, last=True, apart=False):
        rd, wr = {}, {}
        for o, l, x in lst:
            rd[l[1:]], rd[x[1:]], wr[o[1:]] = l, x, o

        def fire():
            for i, (o, l, x) in enumerate(lst):
                ins = M.matmul(o[0], l[0], x[0], apart or first and i == 0, apart or last and i == len(lst) - 1)
            return ins
        cost = sum(max(min(64.0, size(l)), size(x)) * (1 if short(x) else 4) for o, l, x in lst) * PCY
        return add("t", cost, fire, list(rd.values()), list(wr.values()))

    def dma(q, out, in_, sem, lat, extra=()):
        e = {"y": Y, "s": C}[q]
        rd = [in_] if isinstance(in_, tuple) else []
        wr = [out] if isinstance(out, tuple) else []
        src, dst_ = (in_[0] if rd else in_), (out[0] if wr else out)
        return add(q, 60, lambda: e.dma_start(dst_, src), rd, wr, sem=sem, cnt=16, lat=lat, extra=extra)

    hs = helpers(T, topo, core)
    near = topo.engines(core, hs[0])

    def dst(c):
        rid, pid = topo.addr(c, core)
        return DstId(rid=rid, pnc=pid)

    def quarters(c0, w, land, h0, far_sem, sem, busy):
        tr = [RemoteDMATransfer(dst_ids=[dst(h)], dma_engine_mask=bits(near[i // 2::2][i % 2::2]), remote_sem=S[far_sem],
                                srcs=[T.lm0[:, c0 + i * w:c0 + (i + 1) * w]], dsts=[T[land][:, h0:h0 + w]]) for i, h in enumerate(hs)]
        return add("g", busy, lambda: g.remote_dma_fused(tr, local_sem=S[sem]), [X("lm0", c0, c0 + len(hs) * w)], [], sem=sem, cnt=len(near), lat=3000)

    def arrivals(s):
        return sum(len(topo.engines(h, core)) for h in helpers(T, topo, T.cores[(r + s) % N]))

    F0, F1 = P0 + B, 2048
    cut, back = len(hs) * PC[0], [()]
    first = [dma("s", X("lm0", 0, cut), T.lim[:, 0:cut], "l_lim0", 2300), dma("y", X("hdi"), T.hd[:, :], "l_hd", 2600),
             dma("s", X("ci", 0, B), T.comp[:, 0:B], "l_comp", 3500), dma("y", X("ft", P0, F0), T.feat[:, P0:F0], "l_fa", 4000),
             dma("s", X("lm0", cut, H), T.lim[:, cut:H], "l_lim1", 5200)]
    for i, j in zip(first, first[2:]):
        ops[j]["after"].add(i)
    for p in range(2):
        back.append((quarters(cut * p, PC[p], "hl", PC[0] * p, "ha%d" % p, "bulk%d" % p, (2000, 1200)[p]),))
    ops[back[2][0]]["after"] |= set(back[1])
    for s in range(1, N):
        add("x", 0, None, [], [X("lm%d" % s, 0, H)], sem="lm_%d" % s, cnt=2 * arrivals(s), lat=AT1 - 10500 + 4000 * (s - 1), extra=back[2])
    z = dma("y", X("ft", 0, P0), T.feat[:, 0:P0], "l_fb", 5000, first[2:3])
    ops[dma("y", X("ft", F0, F1), T.feat[:, F0:F1], "l_fc", 5500, first[2:3])]["after"].add(z)
    dma("y", X("ci", B, 2 * B), T.comp[:, B:2 * B], "l_ci2", 5000, back[1])
    dma("y", X("ci", 2 * B, 768), T.comp[:, 2 * B:768], "l_ci3", 5000, back[2])
    add("g", 430, lambda: g.iota(X("io")[0], [[1, 144]], 0, 0), [], [X("io")])
    add("g", 200, lambda: g.iota(X("pi")[0], [[0, 1]], 0, 1), [], [X("pi")])

    cp(X("pf"), X("pi"))
    cp(X("iof"), X("io"))
    ts(X("idw"), X("iof"), X("pf"), None, A.is_equal)
    ID, J8 = X("idw", 0, W), X("iof", 0, 8)
    cp(X("hdf"), X("hdi"))
    for z, (u0, u1) in enumerate(((0, 6), (6, 12), (12, 16))):
        pd = "pd%d" % (z % 2)
        mm([(X(pd, 80 * (u - u0), 80 * (u - u0) + 80), X("idw", u, u + W), X("hdf")) for u in range(u0, u1)], apart=True)
        (cp if z == 1 else act)(X("htab", 80 * u0, 80 * u1), X(pd, 0, 80 * (u1 - u0)))
    cp(X("cl", 0, B), X("ci", 0, B))
    ts(X("gi"), X("pi"), 4, None, A.logical_shift_right)
    cp(X("gf"), X("gi"))
    ts(X("wh"), X("iof", 0, W, 16), X("pf"), 32.0, A.is_equal, A.mult)
    for n, w in (("idq", 1.0 / 32), ("nid", -1.0), ("idf", 1.0), ("wi", 4096.0)):
        ts(X(n), ID, w, None, A.mult)
    for n, w in (("w1", 32.0 * 613), ("w2", float(BIG)), ("wp", 1.0), ("a1", 1.0), ("a32", 1.0 / 32)):
        ts(X(n), J8, X("gf"), w, A.is_equal, A.mult)
    ONE, ONK = X("ones"), X("ones", 0, KW)
    ms(ONE, 1.0)
    ts(X("c1"), X("idw", 1, 2), -9.0 * BIG / 65536, None, A.mult)
    ts(X("cq"), X("idw", 2, 3), -1.0, X("c1"), A.mult, A.add)
    ts(X("lm0", H, HK), ONK, X("cq"), None, A.mult)
    ts(X("c2"), X("idw", 0, 1), 32.0, None, A.mult)
    ts(X("c3"), X("idw", 1, 2), 65536.0, X("c2"), A.mult, A.add)
    ts(X("cw"), X("idw", 2, 3), 256.0, X("c3"), A.mult, A.add)
    ts(X("kl"), ONE, X("cw"), None, A.mult)
    for b in range(NB):
        ms(X("ch%d" % b, W, W + 16), 0.0)
        ms(X3("qc%d" % b, 0, 33), 0.0)

    def fr(t, step):
        n = "fr%d" % t
        for m0 in range(B - step, -1, -step):
            i = X("ft", P0 + B * t + m0, P0 + B * t + m0 + step)
            for k in range(16):
                o = X(n, 16 * m0 + k, 16 * (m0 + step), 16)
                if t == 0 and (m0 or k >= FG):
                    add("v", vc(step, 0.5), lambda o=o, i=i: V.tensor_copy(o[0], i[0]), [i], [o], team=n)
                else:
                    z = add("g", 170 + 2 * step * CY, lambda o=o, i=i: g.affine_select(o[0], i[0], [[0, step]], A.is_gt, 0.0, 1, 0), [i], [o], team=n)
                    ops[z]["after"] |= set(back[2])

    fr(0, W)
    fr(1, B)

    def late():
        gcp(X("cl", B, 2 * B), X("ci", B, 2 * B))
        gcp(X("cl", 2 * B, 768), X("ci", 2 * B, 768))
        ts(X("km"), X("io", 0, W), 15, None, A.bitwise_and)
        cp(X("kf"), X("km"))
        act(X("keep"), X("kf"), AF.Sigmoid, bias=-128.0, scale=256.0)
        ts(X("rsa"), X("keep"), 2.0e9, -1.0e9, A.mult, A.add)
        ts(X("rsb"), X("keep"), -2.0e9, 1.0e9, A.mult, A.add)
        ts(X("on32"), ONE, 1.0 / 32, None, A.mult)
        ts(X("dmy"), X("pf"), 2.0, float(HK), A.mult, A.add)
        for t in range(NT - 1):
            ts(X("up%d" % t, NB * UP, NB * UP + KW), ONK, X("cq"), None, A.mult)
        for b in range(NB):
            ms(X("lz%d" % b), 0.0)
            ms(X("wz%d" % b), 0.0)
        ts(X("hf"), X("keep"), 0.5, None, A.mult)
        ts(X("st"), X("keep"), -1.0, 1.0, A.mult, A.add)
        scan(X("rwa"), X("hf"), X("st"), 0.0, A.mult, A.add)
        ts(X("hf"), ONE, 0.5, None, A.mult)
        ts(X("st"), X("keep"), 0.0, None, A.mult)
        scan(X("rwb"), X("hf"), X("st"), 2.0 ** 57, A.mult, A.add)
        ts(X("e0", 0, 1), X("idw", 0, 1), 1.0, None, A.mult)
        ts(X("e0", 1, 2), X("idw", 0, 1), 2.5, None, A.mult)
        mm([(XR("px1", 12, 0, 1), X("rwa"), X("e0", 0, 1))])
        mm([(XR("px1", 12, 1, 2), X("rwb"), X("e0", 1, 2))])
        ts(X("gm"), X("io", 0, W), 4, None, A.logical_shift_right)
        cp(X("gk"), X("gm"))
        ts(X("wu"), X("gk"), X("gf"), XR("px1", 12, 0, 1), A.is_equal, A.mult)
        cp(X("thr"), XR("px1", 12, 1, 2))
        ts(X("ri"), X("pi"), 15, None, A.bitwise_and)
        cp(X("rf"), X("ri"))
        ts(X("own"), X("kf"), X("rf"), None, A.is_equal)
        ts(X("bar"), X("own"), -1.0, 2.0 ** 70, A.add, A.mult)

    def parts(lo, hi, most):
        n = -(-(hi - lo) // most)
        if not n:
            return []
        step = -(-(hi - lo) // (32 * n)) * 32
        return [(a, min(a + step, hi)) for a in range(lo, hi, step)]

    def FR(t, b, lo, hi):
        return X("fr%d" % t, 16 * MO[b] + lo, 16 * MO[b] + hi)

    def col(n, k):
        return X(n, k, E, 16)

    def offs(n, c0, lo, hi):
        return X(n, c0 + lo // 16, c0 + hi // 16)

    def gather(q, out, win, lst, c0, lo, hi, other=None, op=None, cuts=None, step=None):
        def call(a, z):
            o, x = X(out, a, z)[0], win[0].indirect(offs(lst, c0, a, z)[0])
            if q == "s":
                return C.activation(o, x, AF.Copy)
            return V.tensor_tensor(o, x, other(a, z)[0], op) if other else V.tensor_copy(o, x)
        fix = 65 if q == "s" else 50
        ends, made = [lo], []
        for n in cuts or ():
            ends.append(ends[-1] + (n or hi - lo - sum(cuts)))
        for a, z in (zip(ends, ends[1:]) if cuts else parts(lo, hi, step or VCH)):
            i = add(q, fix + vc(z - a, GA), None, [win, offs(lst, c0, a, z)] + ([other(a, z)] if other else []), [X(out, a, z)])
            ops[i]["piece"] = [call, a, z, fix]
            made.append(i)
        return made

    folds, sent, found = [], {}, {}

    def shares(t, b):
        mn, win, c0, nv = "mn%d_%d" % (t, b), X("ft", 0, P0 + B * t), B * t + MO[b], SV.get((t, b), 0)
        gather("v", mn, win, "cl", c0, 0, nv, lambda lo, hi: FR(t, b, lo, hi), A.min)
        if nv == E:
            return
        mx, tb, to = "mx%d_%d" % (t, b), "%d%d" % (t, b), mirror(T, topo, core)
        gather("s", mx, win, "cl", c0, nv, E, step=SHS)
        tr = [RemoteDMATransfer(dst_ids=[dst(to)], dma_engine_mask=bits(near), remote_sem=S["fa" + tb], srcs=[X(mx, nv, E)[0], FR(t, b, nv, E)[0]], dsts=[X(mn, nv, E)[0]], alu_op=3)]
        i = add("g", 1200, lambda: g.remote_dma_fused(tr, local_sem=S["fl" + tb]), [X(mx, nv, E), FR(t, b, nv, E)], [], sem="fl" + tb, cnt=len(near), lat=ATF // 2,
                extra=sent[t - 1] if t else back[2])
        ops[i]["after"] |= set(folds[-1:])
        folds.append(i)
        add("x", 0, None, [], [X(mn, nv, E)], sem="fb" + tb, cnt=len(topo.engines(to, core)), lat=ATF // 2, extra=(i,))

    def CH(j, wide=1):
        n, a = "qc%d" % (j // 2), 16 * (j % 2) + 1
        return (T[n][:, a:a + 16 * wide:2, :], n, 8 * a, 8 * (a + 16 * wide - 1))

    def to_list(j):
        out, n, a = X3("px%d" % j, 0, 8, 8, 16), "qc%d" % (j // 2), 16 * (j % 2)
        return ([mm([(out, X3(n, a + 1, a + 17), X("idq", 0, W, 2)), (out, X3(n, a, a + 16), X("idq", 1, W, 2))])],
                [cp(X("ul%d" % (j // 2), 64 * (j % 2), 64 * (j % 2) + 64), out)])

    def find(t, j):
        win, hx, c0, lo = X("htab", 0, P0 + B * t), "hx%d" % (j // 2), B * t + MO[j // 2], G * (j % 2)
        gather("v", hx, win, "cl", c0, lo, lo + HV[t][j], step=SHS)
        found[t] = gather("s", hx, win, "cl", c0, lo + HV[t][j], lo + G, step=SHS)[-1:]

    def heads(t, j):
        px, lo = "px%d" % j, G * (j % 2)
        mm([(XI(px, 0, 8, k), X("hx%d" % (j // 2), lo + k, lo + G, 8), X("wh")) for k in range(8)], apart=True)
        cp(CH(j), X3(px, 0, 8, 0, 8))
        to_list(j)

    def notes(t, a):
        return "lr%d_%d" % (a, t - 1) if t and a in RS else "lm%d" % a

    def tile(t, a):
        if t == 0 or a == 0:
            return X("lm0", H, HK)
        return X(notes(t, a), H, HK) if a in RS else X("ru%d_%d" % (a, t - 1), NB * UP, NB * UP + KW)

    def visit(t, j, a):
        b, lo = j // 2, G * (j % 2)
        lm, cm, px, ul = X(notes(t, a), 0, H), "cm%d" % b, "px%d" % j, "ul%d" % b
        x, ch, mi, mj = X3(px, 0, 8, 0, 8), CH(j), X("mi%d" % j), X("mj%d" % j)
        ns = NSF[j] if a == 0 else NSL if (a, j) == (N - 1, NQ - 1) else 0 if (a, j) == (1, 0) else NS
        hi, v = lo + G - ns, {}
        if ns:
            xg, d = X("xg%d" % j, 0, ns), X("pd%d" % (j % 2), 0, ns)
            v["f"] = [mm([(d, ID, FR(t, b, hi, lo + G))], last=False)]
            v["g"] = [act(xg, IND(lm, offs(ul, 0, hi, lo + G)))]
            v["x"] = [mm([(d, X("nid"), xg)], first=False)]
            v["s"] = [act(X(cm, hi, lo + G), d, AF.Sigmoid, bias=-128.0, scale=256.0)]
        if j % 2 == 0:
            v["sq"] = [act(X("sh%d" % b), CH(j, 2), AF.Square, bias=16.0, scale=1.0 / 32)]
        v["open"] = [mm([(x, X("idf"), X("sh%d" % b, 64 * (j % 2), 64 * (j % 2) + 64)), (x, X("kl"), tile(t, a))], last=False)]
        v["v"] = gather("v", cm, lm, ul, 0, lo, hi, lambda lo, hi: FR(t, b, lo, hi), A.is_lt, (MID, 0))
        v["sum"] = [mm([(XI(px, 0, 8, k), X(cm, lo + k, lo + G, 8), X(w)) for k in range(8) for w in ("w1", "w2")], first=False)]
        v["max"], v["and"] = [tt(mi, x, ch, A.max)], [ts(mj, mi, 32 * (H - 1), None, A.bitwise_and)]
        if NQ * a + j < GZ:
            gcp(ch, mj)
        else:
            v["cp"] = [cp(ch, mj)]
        if a < N - 1:
            v["turn"], v["list"] = to_list(j)
        return v

    def chain(calls):
        for i, j in zip(calls, calls[1:]):
            ops[j]["after"].add(i)

    def beat(t, seq, fill):
        def of(n, what):
            return seq[n].get(what, []) if n < len(seq) else []
        vq, sq, tq = [], [], []
        chain(found[t] + [i for n in range(FROM + 1) for i in of(n, "g")])
        for n in range(FROM, len(seq)):
            p = of(n, "v")
            if of(n, "scat"):
                vq += of(n, "scat")[:-1] + of(n - 2, "and") + of(n - 3, "list") + of(n, "scat")[-1:] + of(n - 1, "max") + p
            else:
                vq += p[:1] + of(n - 2, "and") + of(n - 3, "list") + p[1:] + of(n - 1, "max") + of(n - 2, "cp")
            sq += of(n + 1, "g") + of(n, "s") + of(n + 1, "sq")
            tq += of(n, "x") + of(n - 1, "open") + of(n - 1, "sum") + of(n - 2, "turn") + of(n + 1, "f") + fill.get(n, [])
        for q in (vq, sq, tq):
            chain(q)

    def sums(t, b):
        pk = "pk%d" % b
        run = [(X3(pk, 0, 8), X("wi"), ONE)] + [(XI(pk, 0, 8, k), col("mn%d_%d" % (t, b), k), X("wp")) for k in range(16)]
        ends = [0] + [17 - 16 // SP * i for i in range(SP - 1, -1, -1)]
        return {SUMS[b] + i: [mm(run[ends[i]:ends[i + 1]], first=i == 0, last=False)] for i in range(SP)}

    def elect(t, b):
        px, pk, eb, ch = "px%d" % (2 * b), "pk%d" % b, "eb%d" % b, X("ch%d" % b, 0, W)
        key, de = X3(pk, 0, 8), X3("px%d" % (2 * b + 1), 8, 12)
        for h in range(2):
            mm([((T[px][64 * h:64 * h + 64, 8:16, c:c + 8], px, 256, 512), X("idw", c // 8 % 2, W, 2), CH(2 * b + h)) for c in range(0, 32, 8)], apart=True)
        cp(ch, X3(px, 8, 16, 0, 16))
        mm([(de, ID, X("ch%d" % b, 1, W + 1)), (de, X("nid"), ch)])
        (act if "d%d" % b in OFF else cp)(X("de%d" % b), de)
        for d in range(1, 9):
            e = X3(eb, 8 * d - 8, 8 * d)
            tt(e, ch, X3(px, 8, 16, d, d + 16), A.is_equal)
        for ds in DS:
            run = []
            for d in ds:
                run.append((key, X("wi"), X3(eb, 8 * d - 8, 8 * d)))
                if d < 8:
                    run.append((X3(pk, 0, 8, d, 16), X("wi"), X3(eb, 8 * d - 8, 8 * d, 0, 16 - d)))
                    run.append((X3(pk, 0, 8, 0, d), X("wi"), X3(eb, 8 * d - 8, 8 * d, 16 - d, 16)))
            mm(run, first=False, last=8 in ds)
        (act if "k%d" % b in OFF else cp)(X("sq%d" % b), key)

    def pick(t, b, h):
        rs, o1, o2 = (("rsa", A.min, A.max), ("rsb", A.max, A.min))[h]
        lo, hi = W * h, W * h + W
        scan(X("rr%d" % b, lo, hi, -1), X(rs), X("sq%d" % b, 0, W, -1), 0.0, o1, o2)
        tt(X("nr%d" % b, lo, hi), X("rr%d" % b, lo, hi), X3("pk%d" % b, 0, 8), A.not_equal)
        scan(X("yy%d" % b, lo, hi, -1), X("de%d" % b, 0, W, -1), X("nr%d" % b, lo, hi, -1), 0.0, A.add, A.mult)
        if h == 0:
            c0, won = P0 + B * t + MO[b], X3("px%d" % (2 * b + 1), 12, 16)
            mm([(won, X("ch%d" % b, 0, W), X("idq"))], last=False)
            mm([(won, X("yy%d" % b, lo, hi), X("idq"))], first=False)
            (act if "w%d" % b in OFF else cp)(X("htab", c0, c0 + W), won)
        if h or t < NT - 1:
            tt(X(("wz%d", "lz%d")[h] % b, 0, W, 16), X("yy%d" % b, lo, hi, 16), X("ch%d" % b, 0, W, 16), A.add)

    def losers(t, b, stage):
        pk, up, lf, c0 = "pk%d" % b, "up%d" % t, "lf%d" % b, P0 + B * t + MO[b]
        row, lst, dup, old = X("lbs%d" % b), XR("px%d" % (2 * b), 0, 16, 24), X("pd%d" % b, 0, W), X("old%d" % b)
        dif, new = X3("px%d" % (2 * b + 1), 0, 4), X3("px%d" % (2 * b + 1), 4, 8)
        if stage == "one":
            scan(X("lr%d" % b), X("keep"), X("lz%d" % b), 0.0, A.mult, A.add)
            mm([(X3(pk, 16, 24), X("lr%d" % b), X("idq"))])
            scan(X("lk%d" % b), X("lr%d" % b), X("own"), 0.0, A.add, A.mult)
            mm([(lst, X("lk%d" % b), X("a32"))])
            (act if "r%d" % b in OFF else cp)(row, X3(pk, 16, 24))
            (act if "l%d" % b in OFF else cp)(X(lf), lst)
            cp(X("lu%d" % b), lst)
            act(old, IND(X("lm0", 0, H), X("lu%d" % b)))
            mm([(dif, ID, X("ft", c0, c0 + W)), (dif, X("nid"), old)])
        elif stage == "two":
            mm([(dup, ID, X("bar"))], last=False)
            for a0 in range(0, 8, 2):
                run = []
                for a in range(a0, a0 + 2):
                    i = X("ind%d" % b, W * a, W * a + W)
                    ts(i, row, X(lf, a, a + 1), 2.0 ** (56 - 16 * a), A.is_equal, A.mult)
                    run.append((dup, i, X("wu")))
                mm(run, first=False, last=a0 == 6)
            ts(X("dz%d" % b), dup, X("thr"), X("dmy"), A.is_ge, A.mult)
            mm([(lst, X("dz%d" % b), X("a1"))])
        else:
            ts(X("clp%d" % b), dif, -32.0, 32.0, A.max, A.min)
            mm([(new, ID, old), (new, ID, X("clp%d" % b))])
            (act if "n%d" % b in OFF else cp)(X(up, b * UP, b * UP + W), new)
            tt(X(up, b * UP + W, b * UP + W + 8), lst, X(lf), A.max)

    def kappa(t):
        o = (T.pk0[0:1, 24:28, :], "pk0", 24 * 16, 28 * 16)
        mm([(o, X("wz%d" % b, 16 * u, 16 * u + 1), X("on32", 0, KW)) for b in range(NB) for u in range(8)])
        cp(top("ki"), o)
        ts(top("kj"), top("ki"), 255, None, A.bitwise_and)
        cp(top("up%d" % t, NB * UP, NB * UP + KW), top("kj"))
        gcp(top("lm0", H, HK), top("kj"))

    def scat(s, up, b):
        ou = X("ou%d" % s, 16 * b, 16 * b + 8)
        (gcp if s else cp)(ou, X(up, b * UP + W, b * UP + W + 8))
        return cp(IND(X("lm%d" % s), ou), X(up, b * UP, b * UP + W))

    def send(t):
        tr, cnt = [], 0
        for s, (to, es) in routes(T, topo, core).items():
            sem, n = ("hu%d" % t, "hu%d" % t) if to in hs else ("uq%d_%d" % (s, t), "ru%d_%d" % (s, t))
            tr.append(RemoteDMATransfer(dst_ids=[dst(to)], dma_engine_mask=bits(es), remote_sem=S[sem], srcs=[X("up%d" % t)[0]], dsts=[X(n)[0]]))
            cnt += len(es)
        i = add("g", 1200, lambda: g.remote_dma_fused(tr, local_sem=S["lo%d" % t]), [X("up%d" % t)], [], sem="lo%d" % t, cnt=cnt, lat=2500)
        sent[t] = (i,)
        for s in MSG:
            to, es = routes(T, topo, T.cores[(r + s) % N])[s]
            add("x", 0, None, [], [X("ru%d_%d" % (s, t))], sem="uq%d_%d" % (s, t), cnt=len(es if to == core else topo.engines(to, core)),
                lat=(ATU * 0.55 if to == core else ATU) - 2500, extra=(i,))

    def anew(t):
        i = quarters(0, HK // len(hs), "hl%d" % t, 0, "hr%d" % t, "rl%d" % t, 1200)
        ops[i]["after"] |= set(sent[t])
        for n, s in enumerate(RS):
            add("x", 0, None, [], [X("lr%d_%d" % (s, t))], sem="rq%d_%d" % (s, t), cnt=arrivals(s), lat=ATR - 3000 + 4000 * n, extra=(i,))

    def stage(name, base, call, *args):
        lift[0] = base + (STAGES if more else LAST).split().index(name) / 100
        call(*args)
        lift[0] = None

    for j in range(NQ):
        find(0, j)
        heads(0, j)
    late()
    for t in range(NT):
        seq = []
        for a in range(N):
            for t1, b in LATEST:
                if LATEST[t1, b] == (t, a):
                    shares(t1, b)
            if (t, a) == (0, N - 1):
                fr(2, B)
            new = [scat(s, "ru%d_%d" % (s, t - 1), b) for s in MSG[::-1] for b in range(NB)] if t and a == 1 else []
            seq += [visit(t, j, a) for j in range(NQ)]
            seq[-NQ]["scat"] = new
        beat(t, seq, {**sums(t, 0), **sums(t, 1)})
        base, more = len(ops), t < NT - 1
        for b in range(NB):
            stage("eq%d" % b, base, elect, t, b)
            stage("min%d" % b, base, pick, t, b, 1)
            stage("max%d" % b, base, pick, t, b, 0)
            stage("one%d" % b, base, losers, t, b, "one")
        if more:
            stage("kappa", base, kappa, t)
        for b in range(NB):
            stage("two%d" % b, base, losers, t, b, "two")
            stage("end%d" % b, base, losers, t, b, "end")
        if more:
            stage("send", base, send, t)
        for b in range(NB):
            stage("sc%d" % b, base, scat, 0, "up%d" % t, b)
        if more:
            for j in range(NQ):
                stage("find%d" % j, base, find, t + 1, j)
                stage("head%d" % j, base, heads, t + 1, j)
            if RS:
                anew(t)
    add("y", 60, lambda: Y.dma_start(T.yh[:, :], T.htab[0:128:16, P0:2048]), [X("htab", P0, 2048)], [], sem="st_h", cnt=16, lat=2000)
    dma("y", T.yl[:, :], X("lm0", 0, H), "st_l", 3500)
    emit(g, T, ops)


def joins(p, o):
    a, b = p.get("piece"), o.get("piece")
    return bool(a and b and a[0] is b[0] and a[2] == b[1])


def replay(ops, queues, wake):
    fin = [0.0] * len(ops)
    last = {}
    for i, q in queues:
        o = ops[i]
        e, d = 0.0, o["busy"]
        for j in o["deps"]:
            e = max(e, fin[j] + ops[j]["lat"] + (OWN if ops[j]["q"] == q else wake))
        if q != "x" and q in last:
            p = last[q]
            if joins(ops[p], o):
                d -= o["piece"][3]
            e = max(e, fin[p])
        last[q] = i
        fin[i] = e + d
    return fin


def schedule(ops):
    n = len(ops)
    succ, pred = [[] for _ in range(n)], [[] for _ in range(n)]
    for i, o in enumerate(ops):
        for j, w in [(j, ops[j]["lat"] + (OWN if ops[j]["q"] == o["q"] else WAKE)) for j in o["deps"]] + [(j, 0.0) for j in o["after"]]:
            succ[j].append((i, w))
            pred[i].append((j, w))

    def place(order, before, first):
        fin, line = [0.0] * n, {}
        for i in order:
            d = ops[i]["busy"]
            e = max([fin[j] + w for j, w in before[i]], default=first[i])
            if ops[i]["q"] != "x":
                used = line.setdefault(ops[i]["q"], [])
                k = len(used)
                while k and used[k - 1][1] > e:
                    k -= 1
                while k < len(used) and used[k][0] < e + d:
                    e = max(e, used[k][1])
                    k += 1
                used.insert(k, (e, e + d))
            fin[i] = e + d
        return fin

    def rank(i):
        return ops[i]["rank"]

    def greedy(look, fit):
        need = [len(p) for p in pred]
        free, ready, avail, last, fin = {}, [0.0] * n, {}, {}, [0.0] * n
        for i in range(n):
            if need[i] == 0:
                avail.setdefault(ops[i]["q"], []).append(i)
        for _ in range(n):
            e, q = min((max(free.get(q, 0.0), min(ready[i] for i in lst)), q) for q, lst in avail.items() if lst)
            lst = avail[q]
            now = [i for i in lst if ready[i] <= e + 1e-6]
            pick = min(now, key=rank)
            soon = [i for i in lst if e + 1e-6 < ready[i] <= e + look and rank(i) < rank(pick)]
            if soon and q != "x":
                p = min(soon, key=rank)
                if e + ops[pick]["busy"] > ready[p] + fit:
                    pick = min([i for i in now if e + ops[i]["busy"] <= ready[p] + fit], default=p, key=rank)
            lst.remove(pick)
            o = ops[pick]
            fin[pick] = max(e, ready[pick]) + o["busy"] - (o["piece"][3] if q in last and joins(ops[last[q]], o) else 0)
            if q != "x":
                free[q] = fin[pick]
            last[q] = pick
            for j, w in succ[pick]:
                ready[j] = max(ready[j], fin[pick] + w)
                need[j] -= 1
                if need[j] == 0:
                    avail.setdefault(ops[j]["q"], []).append(j)
        return fin
    best = None
    for look, fit in LOOKS:
        fin = greedy(look, fit)
        for z in range(PASSES + 1):
            if z:
                late = place(sorted(range(n), key=lambda i: (-fin[i], -i)), succ, [o["lat"] for o in ops])
                fin = place(sorted(range(n), key=lambda i: (-late[i], i)), pred, [0.0] * n)
            order = [(i, ops[i]["q"]) for i in sorted(range(n), key=lambda i: (fin[i], i))]
            run = replay(ops, order, WAKE)
            end = max(run[i] + ops[i]["lat"] for i in range(n))
            if best is None or end < best[0]:
                best = (end, order, run)
    order = [(i, ops[i]["q"]) for i in polish(ops, [i for i, q in best[1]], pred, succ)]
    return order, replay(ops, order, WAKE)


def polish(ops, order, pred, succ):
    n = len(ops)
    qs, busy, lat = [o["q"] for o in ops], [o["busy"] for o in ops], [o["lat"] for o in ops]
    glue = {i - 1: o["piece"][3] for i, o in enumerate(ops) if i and joins(ops[i - 1], o)}

    def run(order, start, fin, why):
        last = {}
        for i in reversed(order[:start]):
            last.setdefault(qs[i], i)
            if len(last) == 6:
                break
        for i in order[start:]:
            e, w0, d, q = 0.0, None, busy[i], qs[i]
            for j, w in pred[i]:
                if fin[j] + w > e:
                    e, w0 = fin[j] + w, j
            p = last.get(q)
            if p is not None and q != "x":
                if p == i - 1:
                    d -= glue.get(p, 0)
                if fin[p] >= e:
                    e, w0 = fin[p], -p - 1
            last[q] = i
            fin[i], why[i] = e + d, w0
        return max(fin[i] + lat[i] for i in order[-40:])
    fin, why, seed = [0.0] * n, [None] * n, 1
    now = run(order, 0, fin, why)
    best, pairs = (now, order), None
    for step in range(STEPS):
        if pairs is None:
            order = sorted(order, key=lambda i: fin[i])
            at = {i: k for k, i in enumerate(order)}
            pairs, i = [], max(order[-40:], key=lambda i: fin[i] + lat[i])
            while why[i] is not None:
                if why[i] < 0:
                    pairs.append((-why[i] - 1, i))
                i = why[i] if why[i] >= 0 else -why[i] - 1
        seed = (seed * 1103515245 + 12345) % 2147483648
        p, i = pairs[(seed >> 8) % len(pairs)]
        far, k = (1, 1, 1, 2, 2, 3, 4, 6)[seed >> 4 & 7], at[i]
        if seed >> 7 & 1:
            while far and k:
                k -= 1
                far -= qs[order[k]] == qs[i]
            if any(at[j] >= k for j, w in pred[i]):
                continue
            new, start = order[:k] + [i] + order[k:at[i]] + order[at[i] + 1:], k
        else:
            far -= 1
            while far and k < n - 1:
                k += 1
                far -= qs[order[k]] == qs[i]
            if any(at[j] <= k for j, w in succ[p]):
                continue
            new, start = order[:at[p]] + order[at[p] + 1:k + 1] + [p] + order[k + 1:], at[p]
        f, y = list(fin), list(why)
        end = run(new, start, f, y)
        if end <= now + ALLOW * (1 - step / STEPS) * (seed >> 12 & 255) / 255:
            order, fin, why, now, pairs = new, f, y, end, None
            if end < best[0]:
                best = (end, new)
    return best[1]


def emit(g, T, ops):
    if "order" not in _PLAN:
        _PLAN["order"] = schedule(ops)
    order, when = _PLAN["order"]
    queues, same = {}, {}
    for i, q in order:
        kept = queues.setdefault(q, [])
        if kept and joins(ops[kept[-1]], ops[i]):
            ops[kept[-1]]["piece"][2] = ops[i]["piece"][2]
            ops[kept[-1]]["deps"] |= ops[i]["deps"]
            same[i] = kept[-1]
        else:
            kept.append(i)
    for o in ops:
        o["deps"] = {same.get(j, j) for j in o["deps"]}
    S = T.sem
    eng = {"v": g.vector, "s": g.scalar, "t": g.tensor, "g": g, "y": g.sync}
    qsem = {"v": "qv", "s": "qs", "t": "qt", "g": "qg"}
    wanted = set()
    for o in ops:
        wanted |= o["deps"]
    total = {}
    for q, lst in queues.items():
        for i in lst:
            o = ops[i]
            if o["sem"]:
                s, c = o["sem"], o["cnt"]
            elif i in wanted:
                s, c = qsem[q], 1
            else:
                continue
            total[s] = total.get(s, 0) + c
            o["tok"] = (s, total[s])
    known = {q: {} for q in queues}
    nxt = {q: 0 for q in queues}
    done = set(same)
    while len(done) < len(ops):
        for q, lst in queues.items():
            kn = known[q]
            while nxt[q] < len(lst):
                i = lst[nxt[q]]
                o = ops[i]
                if q == "x":
                    o["clk"] = {o["tok"][0]: o["tok"][1]}
                else:
                    if not o["deps"] <= done:
                        break
                    for j in sorted(o["deps"], key=lambda j: -when[j]):
                        s, v = ops[j]["tok"]
                        if kn.get(s, 0) < v:
                            eng[q].wait_ge(S[s], v)
                            for s2, v2 in ops[j]["clk"].items():
                                kn[s2] = max(kn.get(s2, 0), v2)
                            kn[s] = max(kn.get(s, 0), v)
                    ins = o["piece"][0](o["piece"][1], o["piece"][2]) if "piece" in o else o["fire"]()
                    o["clk"] = dict(kn)
                    if o["sem"] in DMASEMS:
                        ins.then_inc(S[o["sem"]], 16)
                    elif not o["sem"] and i in wanted:
                        ins.then_inc(S[o["tok"][0]], 1)
                    if "tok" in o:
                        o["clk"][o["tok"][0]] = max(kn.get(o["tok"][0], 0), o["tok"][1])
                done.add(i)
                nxt[q] += 1
    for s, v in total.items():
        if known["g"].get(s, 0) < v:
            g.wait_ge(S[s], v)
